import numpy as np
import ml_dtypes


def mxq(x, axis, fmt="e4m3"):
    dtype, down = {"e4m3": (ml_dtypes.float8_e4m3fn, 7), "e5m2": (ml_dtypes.float8_e5m2, 14)}[fmt]
    v = np.moveaxis(np.asarray(x, np.float32).astype(ml_dtypes.bfloat16).astype(np.float64), axis, -1)
    blocks = v.reshape(v.shape[:-1] + (-1, 32))
    amax = np.abs(blocks).max(-1, keepdims=True)
    byte = np.maximum(np.where(amax > 0, np.frexp(amax)[1] - 1 + 127, 0) - down, 1)
    scale = np.exp2(byte - 127.0)
    codes = (blocks / scale).astype(np.float32).astype(dtype).astype(np.float64)
    return np.moveaxis((codes * scale).reshape(v.shape), -1, axis)


WIDE = False


def mx_kscale(k):
    if not WIDE:
        return np.ones(k)
    levels = np.array([10, -10, 5, -5, 0])
    if k % 512:
        return np.exp2(np.random.permutation(np.resize(levels, k // 32))).repeat(32)
    a = np.empty((k // 512, 16))
    for p in range(k // 512):
        a[p, :8] = np.random.permutation(np.resize(levels, 8))
        for g in range(8):
            far = levels[np.abs(levels - a[p, g]) >= 10]
            a[p, g + 8] = far[np.random.randint(len(far))]
    return np.exp2(a.ravel()).repeat(32)


def f64(x):
    return np.asarray(x).astype(np.float64)


def striped(idx):
    return np.tile(idx.reshape(-1, 16).T, (8, 1)).astype(np.uint16)


def unstriped(offs):
    return offs[:16].T.reshape(-1).astype(np.int64)


E2M1 = np.array([0.0, 0.5, 1.0, 1.5, 2.0, 3.0, 4.0, 6.0, -0.0, -0.5, -1.0, -1.5, -2.0, -3.0, -4.0, -6.0])


def pack_weight(w, fmt):
    k, n = w.shape
    w = f64(np.asarray(w, np.float32).astype(ml_dtypes.bfloat16)).reshape(k // 32, 32, n)
    amax = np.abs(w).max(1)
    if fmt == "e4m3":
        byte = np.frexp(amax)[1] - 1 + 127 - 7
    else:
        mant, ex = np.frexp(amax / 6.0)
        byte = np.where(mant > 0.5, ex, ex - 1) + 127
    byte = np.clip(np.where(amax > 0, byte, 1), 1, 254)
    scaled = (w * np.exp2(127.0 - byte)[:, None, :]).reshape(k, n).astype(np.float32)
    by_word = np.ascontiguousarray(scaled.reshape(k // 512, 128, 4, n).transpose(0, 1, 3, 2))
    if fmt == "e4m3":
        words = by_word.astype(ml_dtypes.float8_e4m3fn).view(np.uint8)
    else:
        c = by_word.astype(ml_dtypes.float4_e2m1fn).view(np.uint8) & 0xF
        words = (c[..., 0::2] | (c[..., 1::2] << 4)).reshape(k // 512, 128, 2 * n)
    return np.ascontiguousarray(words), np.ascontiguousarray(byte.astype(np.uint8).reshape(k // 512, 16, n))


def unpack_weight(words, scales, fmt):
    g, _, n = scales.shape
    words = np.ascontiguousarray(words).reshape(g, 128, n, -1)
    if fmt == "e4m3":
        vals = words.view(ml_dtypes.float8_e4m3fn).astype(np.float64)
    else:
        nib = np.empty((g, 128, n, 4), np.uint8)
        nib[..., 0::2] = words & 0xF
        nib[..., 1::2] = words >> 4
        vals = E2M1[nib]
    vals = vals * np.repeat(np.exp2(scales.astype(np.float64) - 127.0), 8, axis=1)[..., None]
    return vals.transpose(0, 1, 3, 2).reshape(g * 512, n)


def silu(v):
    return v / (1.0 + np.exp(-np.maximum(v, -700.0)))


K, T, E, G, H, N = 1024, 256, 6, 3, 512, 512


def setup_inputs():
    n = np.random.standard_normal
    s = mx_kscale(K)
    u = mx_kscale(H)
    chosen = np.random.permutation(E)[:G]
    w1 = pack_weight(n((K, E * H)) / np.sqrt(K) / s[:, None] * np.tile(u, E), "e4m3")
    w2 = pack_weight(n((H, E * N)) / np.sqrt(H) / u[:, None], "e4m3")
    return {
        "xT": (n((K, T)) * s[:, None]).astype(np.float32),
        "w1_words": w1[0],
        "w1_scales": w1[1],
        "w2_words": w2[0],
        "w2_scales": w2[1],
        "gate": np.stack([np.tile(r, (128, 1)) for r in np.random.uniform(0.2, 1.0, (G, T))]).astype(np.float32),
        "offs": striped((chosen[:, None] * H + np.arange(H)).reshape(-1)),
        "offs2": striped((chosen[:, None] * N + np.arange(N)).reshape(-1)),
    }


def reference(xT, w1_words, w1_scales, w2_words, w2_scales, gate, offs, offs2):
    idx, idx2 = unstriped(offs), unstriped(offs2)
    x = mxq(f64(xT), 0, "e4m3")
    w1 = unpack_weight(w1_words, w1_scales, "e4m3")[:, idx]
    w2 = unpack_weight(w2_words, w2_scales, "e4m3")[:, idx2]
    y = np.zeros((N, T))
    for r in range(G):
        h = f64(gate[r, :1]) * silu(w1[:, r * H:(r + 1) * H].T @ x)
        y = y + w2[:, r * N:(r + 1) * N].T @ mxq(h, 0, "e4m3")
    return y

@@ -1,0 +1,195 @@
+from contextlib import ExitStack
+
+import concourse.mybir as mybir
+from concourse.masks import make_identity
+
+K, T, E, G, H, N = 1024, 256, 6, 3, 512, 512
+FLOPS = 2 * G * T * (K * H + H * N)
+BYTES = 4 * K * T + (K * E * H + H * E * N) * 33 // 32 + 4 * G * T + 2 * 128 * (G * H + G * N) // 16 + 4 * N * T
+
+F32 = mybir.dt.float32
+BF16 = mybir.dt.bfloat16
+I32 = mybir.dt.int32
+U32 = mybir.dt.uint32
+U16 = mybir.dt.uint16
+U8 = mybir.dt.uint8
+FP8X4 = mybir.dt.float8_e4m3fn_x4
+SILU = mybir.ActivationFunctionType.Silu
+MULT = mybir.AluOpType.mult
+
+P = 128
+PASSES = K // 512
+TOKEN_TILES = T // P
+OUT_TILES = N // P
+COLS = E * H
+W2_PLANE = 8
+
+
+def tile_moe_wsel_b_silu_f_kernel(
+    tc, xT, w1_words, w1_scales, w2_words, w2_scales, gate, offs, offs2, out
+):
+    nc = tc.nc
+    with ExitStack() as ctx:
+        sb = ctx.enter_context(tc.tile_pool(name="sb", bufs=1))
+        ps = ctx.enter_context(tc.psum_pool(name="ps", bufs=1))
+
+        def tile(shape, dtype, name):
+            return sb.tile(shape, dtype, name=name, align_bytes=64)
+
+        list1 = tile([P, G * H // 16], U16, "list1")
+        list2 = tile([P, G * N // 16], U16, "list2")
+        x_raw = [tile([P, 4, T], F32, f"x_raw{a}") for a in range(PASSES)]
+        w1_all = [tile([P, COLS], I32, f"w1_all{a}") for a in range(PASSES)]
+        w2_all = tile([P, COLS], I32, "w2_all")
+        s1_all = tile([P, COLS], U8, "s1_all")
+        s2_all = tile([P, COLS], U8, "s2_all")
+        gate_rows = tile([P, P], F32, "gate_rows")
+        ident = tile([P, P], F32, "ident")
+        warm_in = tile([P, 8], F32, "warm_in")
+        warm_out = tile([P, 8], F32, "warm_out")
+
+        def words_of(dram, a):
+            return dram[a].rearrange("p n d -> p (n d)").bitcast(I32)
+
+        nc.vector.memset(s1_all[:].bitcast(I32), 0)
+        nc.vector.memset(s2_all[:].bitcast(I32), 0)
+        nc.vector.memset(gate_rows[:], 0.0)
+        nc.vector.memset(warm_in[:], 0.0)
+
+        nc.sync.dma_start(list1[:], offs)
+        nc.sync.dma_start(list2[:], offs2)
+        nc.sync.dma_start(x_raw[0][:], xT[0:512, :].rearrange("(p j) t -> p j t", j=4))
+        nc.sync.dma_start(w1_all[0][:], words_of(w1_words, 0))
+        nc.sync.dma_start(x_raw[1][:], xT[512:1024, :].rearrange("(p j) t -> p j t", j=4))
+        nc.sync.dma_start(w1_all[1][:], words_of(w1_words, 1))
+        nc.sync.dma_start(w2_all[:], words_of(w2_words, 0))
+        for q in range(4):
+            nc.gpsimd.dma_start(
+                s1_all[32 * q : 32 * q + 4 * PASSES, :].bitcast(I32),
+                w1_scales[:, 4 * q : 4 * q + 4, :].bitcast(I32),
+            )
+        for q in range(4):
+            nc.scalar.dma_start(
+                s2_all[32 * q + W2_PLANE : 32 * q + W2_PLANE + 4, :].bitcast(I32),
+                w2_scales[0, 4 * q : 4 * q + 4, :].bitcast(I32),
+            )
+        nc.scalar.activation(warm_out[:], warm_in[:], SILU)
+        nc.gpsimd.dma_start(gate_rows[0 : G * TOKEN_TILES, :], gate[:, 0, :].rearrange("r (c t) -> r c t", t=P))
+        make_identity(nc, ident[:])
+
+        x_bf = [tile([P, T, 4], BF16, f"x_bf{a}") for a in range(PASSES)]
+        x_codes = [tile([P, T], U32, f"x_codes{a}") for a in range(PASSES)]
+        x_scales = [tile([P, T], U8, f"x_scales{a}") for a in range(PASSES)]
+
+        def round_x(a):
+            nc.scalar.copy(x_bf[a][:], x_raw[a][:].rearrange("p j t -> p t j"))
+
+        def quantize_x(a):
+            nc.vector.quantize_mx(
+                out=x_codes[a][:].bitcast(FP8X4), scales=x_scales[a][:], in_=x_bf[a][:].rearrange("p t j -> p (t j)")
+            )
+
+        s1 = tile([P, G * H], U8, "s1")
+        s2 = tile([P, G * N], U8, "s2")
+        w1 = [[tile([P, H], U32, f"w1_{a}_{r}") for r in range(G)] for a in range(PASSES)]
+
+        def gather_words(dst, window, lst, r):
+            nc.vector.tensor_copy(dst[:], window[:].bitcast(U32).indirect(lst[:, 32 * r : 32 * (r + 1)]))
+
+        acc = {}
+
+        def first_product(a, r, c):
+            if a == 0:
+                acc[r, c] = ps.tile([P, H], F32, name=f"bank{2 * r + c}")
+            nc.tensor.matmul_mx(
+                out=acc[r, c][:],
+                lhsT=x_codes[a][:, P * c : P * (c + 1)].bitcast(FP8X4),
+                lhsT_scale=x_scales[a][:, P * c : P * (c + 1)],
+                rhs=w1[a][r][:].bitcast(FP8X4),
+                rhs_scale=s1[4 * a : P, H * r : H * (r + 1)],
+                start=(a == 0),
+                stop=(a == PASSES - 1),
+            )
+
+        round_x(0)
+        nc.vector.tensor_copy(s2[:], s2_all[:].indirect(list2[:]))
+        quantize_x(0)
+        nc.vector.tensor_copy(s1[:], s1_all[:].indirect(list1[:]))
+        gate_ps = ps.tile([P, P], F32, name="bank6")
+        nc.tensor.transpose(gate_ps[:], gate_rows[:], ident[:])
+        gate_cols = tile([P, 8], F32, "gate_cols")
+        nc.scalar.copy(gate_cols[:], gate_ps[:, 0:8])
+        round_x(1)
+        for r in range(G):
+            gather_words(w1[0][r], w1_all[0], list1, r)
+            for c in range(TOKEN_TILES):
+                first_product(0, r, c)
+        quantize_x(1)
+        for r in range(G):
+            gather_words(w1[1][r], w1_all[1], list1, r)
+            for c in range(TOKEN_TILES):
+                first_product(1, r, c)
+
+        act = {(r, c): tile([P, 2, P, 2], F32, f"act{r}{c}") for r in range(G) for c in range(TOKEN_TILES)}
+        h_bf = {(r, c): tile([P, H], BF16, f"h_bf{r}{c}") for r in range(G) for c in range(TOKEN_TILES)}
+        hT = [tile([P, T, 4], BF16, f"hT{r}") for r in range(G)]
+        h_codes = [tile([P, T], U32, f"h_codes{r}") for r in range(G)]
+        h_scales = [tile([P, T], U8, f"h_scales{r}") for r in range(G)]
+        turned = {}
+
+        def activate(r, c):
+            nc.scalar.activation(act[r, c][:], acc[r, c][:].rearrange("t (p u e) -> t u p e", u=2, e=2), SILU)
+
+        def weigh_and_turn(r, c):
+            col = TOKEN_TILES * r + c
+            nc.vector.tensor_scalar(
+                h_bf[r, c][:], act[r, c][:].rearrange("t u p e -> t (u p e)"), gate_cols[:, col : col + 1], None, MULT
+            )
+            if c == 0:
+                turned[r] = ps.tile([P, 2, T], F32, name=f"bank{6 + r % 2}")
+            pairs = h_bf[r, c][:].bitcast(F32)
+            for u in range(2):
+                nc.tensor.transpose(turned[r][:, u, P * c : P * (c + 1)], pairs[:, P * u : P * (u + 1)], ident[:])
+
+        def take_out(r):
+            dst = hT[r][:].bitcast(F32)
+            src = turned[r][:].rearrange("p u t -> p t u")
+            if r == 0:
+                nc.vector.tensor_copy(dst, src)
+            else:
+                nc.scalar.copy(dst, src)
+
+        def quantize_h(r):
+            nc.vector.quantize_mx(
+                out=h_codes[r][:].bitcast(FP8X4), scales=h_scales[r][:], in_=hT[r][:].rearrange("p t j -> p (t j)")
+            )
+
+        for r in range(G):
+            for c in range(TOKEN_TILES):
+                activate(r, c)
+                weigh_and_turn(r, c)
+        for r in range(G):
+            take_out(r)
+        y = [ps.tile([P, T], F32, name=f"bank{m}") for m in range(OUT_TILES)]
+        w2 = [tile([P, N], U32, name) for name in ("act11", "act20", "act21")]
+        for r in range(G):
+            gather_words(w2[r], w2_all, list2, r)
+        for r in range(G):
+            quantize_h(r)
+            for m in range(OUT_TILES):
+                nc.tensor.matmul_mx(
+                    out=y[m][:],
+                    lhsT=w2[r][:, P * m : P * (m + 1)].bitcast(FP8X4),
+                    lhsT_scale=s2[W2_PLANE:P, N * r + P * m : N * r + P * (m + 1)],
+                    rhs=h_codes[r][:].bitcast(FP8X4),
+                    rhs_scale=h_scales[r][:],
+                    start=(r == 0),
+                    stop=(r == G - 1),
+                )
+        for m in range(OUT_TILES):
+            res = tile([P, T], F32, f"res{m}")
+            if m % 2 == 0:
+                nc.scalar.copy(res[:], y[m][:])
+            else:
+                nc.vector.tensor_copy(res[:], y[m][:])
+            nc.sync.dma_start(out[P * m : P * (m + 1), :], res[:])

@@ -1,7 +1,6 @@
 from contextlib import ExitStack
 
 import concourse.mybir as mybir
-from concourse.masks import make_identity
 
 K, T, E, G, H, N = 1024, 256, 6, 3, 512, 512
 FLOPS = 2 * G * T * (K * H + H * N)
@@ -16,6 +15,8 @@ U8 = mybir.dt.uint8
 FP8X4 = mybir.dt.float8_e4m3fn_x4
 SILU = mybir.ActivationFunctionType.Silu
 MULT = mybir.AluOpType.mult
+ADD = mybir.AluOpType.add
+IS_EQUAL = mybir.AluOpType.is_equal
 
 P = 128
 PASSES = K // 512
@@ -38,44 +39,54 @@ def tile_moe_wsel_b_silu_f_kernel(
 
         list1 = tile([P, G * H // 16], U16, "list1")
         list2 = tile([P, G * N // 16], U16, "list2")
-        x_raw = [tile([P, 4, T], F32, f"x_raw{a}") for a in range(PASSES)]
-        w1_all = [tile([P, COLS], I32, f"w1_all{a}") for a in range(PASSES)]
-        w2_all = tile([P, COLS], I32, "w2_all")
         s1_all = tile([P, COLS], U8, "s1_all")
         s2_all = tile([P, COLS], U8, "s2_all")
         gate_rows = tile([P, P], F32, "gate_rows")
         ident = tile([P, P], F32, "ident")
         warm_in = tile([P, 8], F32, "warm_in")
         warm_out = tile([P, 8], F32, "warm_out")
+        ones = tile([P, P], F32, "buf_w1_0")
+        column = tile([P, P], F32, "buf_x1")
+        row = tile([P, P], F32, "buf_w1_1")
 
         def words_of(dram, a):
             return dram[a].rearrange("p n d -> p (n d)").bitcast(I32)
 
-        nc.vector.memset(s1_all[:].bitcast(I32), 0)
-        nc.vector.memset(s2_all[:].bitcast(I32), 0)
+        def rows_of_x(a):
+            return xT[512 * a : 512 * (a + 1), :].rearrange("(p j) t -> p j t", j=4)
+
         nc.vector.memset(gate_rows[:], 0.0)
+        nc.vector.memset(s1_all[:].bitcast(I32), 0)
         nc.vector.memset(warm_in[:], 0.0)
+        nc.vector.memset(ones[:], 1.0)
+        nc.vector.tensor_tensor_scan(column[:], ones[:], ones[:], 0.0, MULT, ADD)
+        nc.vector.memset(s2_all[:].bitcast(I32), 0)
+        nc.vector.transpose(row[:], column[:])
+        for q in range(4):
+            rows = slice(32 * q, 32 * (q + 1))
+            nc.vector.tensor_scalar(ident[rows, :], column[rows, :], row[rows, 32 * q : 32 * q + 1], None, IS_EQUAL)
+
+        x_raw = [tile([P, 4, T], F32, "buf_w2"), tile([P, 4, T], F32, "buf_x1")]
+        w1_all = [tile([P, COLS], I32, f"buf_w1_{a}") for a in range(PASSES)]
 
         nc.sync.dma_start(list1[:], offs)
+        nc.sync.dma_start(x_raw[0][:], rows_of_x(0))
         nc.sync.dma_start(list2[:], offs2)
-        nc.sync.dma_start(x_raw[0][:], xT[0:512, :].rearrange("(p j) t -> p j t", j=4))
-        nc.sync.dma_start(w1_all[0][:], words_of(w1_words, 0))
-        nc.sync.dma_start(x_raw[1][:], xT[512:1024, :].rearrange("(p j) t -> p j t", j=4))
-        nc.sync.dma_start(w1_all[1][:], words_of(w1_words, 1))
-        nc.sync.dma_start(w2_all[:], words_of(w2_words, 0))
+        nc.scalar.dma_start(gate_rows[0 : G * TOKEN_TILES, :], gate[:, 0, :].rearrange("r (c t) -> r c t", t=P))
         for q in range(4):
-            nc.gpsimd.dma_start(
+            nc.sync.dma_start(
                 s1_all[32 * q : 32 * q + 4 * PASSES, :].bitcast(I32),
                 w1_scales[:, 4 * q : 4 * q + 4, :].bitcast(I32),
             )
+        nc.sync.dma_start(w1_all[0][:], words_of(w1_words, 0))
         for q in range(4):
-            nc.scalar.dma_start(
+            nc.sync.dma_start(
                 s2_all[32 * q + W2_PLANE : 32 * q + W2_PLANE + 4, :].bitcast(I32),
                 w2_scales[0, 4 * q : 4 * q + 4, :].bitcast(I32),
             )
+        nc.sync.dma_start(x_raw[1][:], rows_of_x(1))
+        nc.sync.dma_start(w1_all[1][:], words_of(w1_words, 1))
         nc.scalar.activation(warm_out[:], warm_in[:], SILU)
-        nc.gpsimd.dma_start(gate_rows[0 : G * TOKEN_TILES, :], gate[:, 0, :].rearrange("r (c t) -> r c t", t=P))
-        make_identity(nc, ident[:])
 
         x_bf = [tile([P, T, 4], BF16, f"x_bf{a}") for a in range(PASSES)]
         x_codes = [tile([P, T], U32, f"x_codes{a}") for a in range(PASSES)]
@@ -112,9 +123,10 @@ def tile_moe_wsel_b_silu_f_kernel(
             )
 
         round_x(0)
-        nc.vector.tensor_copy(s2[:], s2_all[:].indirect(list2[:]))
-        quantize_x(0)
+        w2_all = tile([P, COLS], I32, "buf_w2")
+        nc.sync.dma_start(w2_all[:], words_of(w2_words, 0))
         nc.vector.tensor_copy(s1[:], s1_all[:].indirect(list1[:]))
+        quantize_x(0)
         gate_ps = ps.tile([P, P], F32, name="bank6")
         nc.tensor.transpose(gate_ps[:], gate_rows[:], ident[:])
         gate_cols = tile([P, 8], F32, "gate_cols")
@@ -124,6 +136,7 @@ def tile_moe_wsel_b_silu_f_kernel(
             gather_words(w1[0][r], w1_all[0], list1, r)
             for c in range(TOKEN_TILES):
                 first_product(0, r, c)
+        nc.vector.tensor_copy(s2[:], s2_all[:].indirect(list2[:]))
         quantize_x(1)
         for r in range(G):
             gather_words(w1[1][r], w1_all[1], list1, r)

@@ -43,11 +43,8 @@ def tile_moe_wsel_b_silu_f_kernel(
         s2_all = tile([P, COLS], U8, "s2_all")
         gate_rows = tile([P, P], F32, "gate_rows")
         ident = tile([P, P], F32, "ident")
-        warm_in = tile([P, 8], F32, "warm_in")
-        warm_out = tile([P, 8], F32, "warm_out")
-        ones = tile([P, P], F32, "buf_w1_0")
-        column = tile([P, P], F32, "buf_x1")
-        row = tile([P, P], F32, "buf_w1_1")
+        warm_in = tile([P, 8], F32, "buf_w1_0")
+        warm_out = tile([P, 8], F32, "buf_x1")
 
         def words_of(dram, a):
             return dram[a].rearrange("p n d -> p (n d)").bitcast(I32)
@@ -55,54 +52,43 @@ def tile_moe_wsel_b_silu_f_kernel(
         def rows_of_x(a):
             return xT[512 * a : 512 * (a + 1), :].rearrange("(p j) t -> p j t", j=4)
 
-        nc.vector.memset(gate_rows[:], 0.0)
         nc.vector.memset(s1_all[:].bitcast(I32), 0)
-        nc.vector.memset(warm_in[:], 0.0)
-        nc.vector.memset(ones[:], 1.0)
-        nc.vector.tensor_tensor_scan(column[:], ones[:], ones[:], 0.0, MULT, ADD)
         nc.vector.memset(s2_all[:].bitcast(I32), 0)
-        nc.vector.transpose(row[:], column[:])
-        for q in range(4):
-            rows = slice(32 * q, 32 * (q + 1))
-            nc.vector.tensor_scalar(ident[rows, :], column[rows, :], row[rows, 32 * q : 32 * q + 1], None, IS_EQUAL)
+        nc.vector.memset(warm_in[:], 0.0)
+        nc.vector.memset(gate_rows[:], 0.0)
+        nc.scalar.activation(warm_out[:], warm_in[:], SILU)
 
-        x_raw = [tile([P, 4, T], F32, "buf_w2"), tile([P, 4, T], F32, "buf_x1")]
-        w1_all = [tile([P, COLS], I32, f"buf_w1_{a}") for a in range(PASSES)]
+        x_raw = [tile([P, 4, T], F32, "buf_w1_1"), tile([P, 4, T], F32, "buf_x1")]
+        w1_all = [tile([P, COLS], I32, "buf_w1_0")]
 
-        nc.sync.dma_start(list1[:], offs)
-        nc.sync.dma_start(x_raw[0][:], rows_of_x(0))
-        nc.sync.dma_start(list2[:], offs2)
-        nc.scalar.dma_start(gate_rows[0 : G * TOKEN_TILES, :], gate[:, 0, :].rearrange("r (c t) -> r c t", t=P))
         for q in range(4):
-            nc.sync.dma_start(
+            nc.gpsimd.dma_start(
                 s1_all[32 * q : 32 * q + 4 * PASSES, :].bitcast(I32),
                 w1_scales[:, 4 * q : 4 * q + 4, :].bitcast(I32),
             )
+        nc.sync.dma_start(list2[:], offs2)
+        nc.sync.dma_start(list1[:], offs)
+        nc.sync.dma_start(x_raw[0][:], rows_of_x(0))
+        for j in range(4):
+            nc.sync.dma_start(s2_all[W2_PLANE + j : P : 32, :].bitcast(I32), w2_scales[0, j:16:4, :].bitcast(I32))
+        nc.sync.dma_start(gate_rows[0 : G * TOKEN_TILES, :], gate[:, 0, :].rearrange("r (c t) -> r c t", t=P))
         nc.sync.dma_start(w1_all[0][:], words_of(w1_words, 0))
-        for q in range(4):
-            nc.sync.dma_start(
-                s2_all[32 * q + W2_PLANE : 32 * q + W2_PLANE + 4, :].bitcast(I32),
-                w2_scales[0, 4 * q : 4 * q + 4, :].bitcast(I32),
-            )
         nc.sync.dma_start(x_raw[1][:], rows_of_x(1))
-        nc.sync.dma_start(w1_all[1][:], words_of(w1_words, 1))
-        nc.scalar.activation(warm_out[:], warm_in[:], SILU)
 
         x_bf = [tile([P, T, 4], BF16, f"x_bf{a}") for a in range(PASSES)]
-        x_codes = [tile([P, T], U32, f"x_codes{a}") for a in range(PASSES)]
+        x_codes = {}
         x_scales = [tile([P, T], U8, f"x_scales{a}") for a in range(PASSES)]
 
         def round_x(a):
             nc.scalar.copy(x_bf[a][:], x_raw[a][:].rearrange("p j t -> p t j"))
 
         def quantize_x(a):
+            x_codes[a] = tile([P, T], U32, "row" if a == 0 else "x_codes1")
             nc.vector.quantize_mx(
                 out=x_codes[a][:].bitcast(FP8X4), scales=x_scales[a][:], in_=x_bf[a][:].rearrange("p t j -> p (t j)")
             )
 
-        s1 = tile([P, G * H], U8, "s1")
         s2 = tile([P, G * N], U8, "s2")
-        w1 = [[tile([P, H], U32, f"w1_{a}_{r}") for r in range(G)] for a in range(PASSES)]
 
         def gather_words(dst, window, lst, r):
             nc.vector.tensor_copy(dst[:], window[:].bitcast(U32).indirect(lst[:, 32 * r : 32 * (r + 1)]))
@@ -123,20 +109,33 @@ def tile_moe_wsel_b_silu_f_kernel(
             )
 
         round_x(0)
-        w2_all = tile([P, COLS], I32, "buf_w2")
-        nc.sync.dma_start(w2_all[:], words_of(w2_words, 0))
-        nc.vector.tensor_copy(s1[:], s1_all[:].indirect(list1[:]))
+        w1_all.append(tile([P, COLS], I32, "buf_w1_1"))
+        nc.sync.dma_start(w1_all[1][:], words_of(w1_words, 1))
+        nc.vector.tensor_copy(s2[:], s2_all[:].indirect(list2[:]))
+        ones = tile([P, P], F32, "s2_all")
+        column = tile([P, P], F32, "column")
+        row = tile([P, P], F32, "row")
+        nc.vector.memset(ones[:], 1.0)
+        nc.vector.tensor_tensor_scan(column[:], ones[:], ones[:], 0.0, MULT, ADD)
+        nc.vector.transpose(row[:], column[:])
+        for q in range(4):
+            rows = slice(32 * q, 32 * (q + 1))
+            nc.vector.tensor_scalar(ident[rows, :], column[rows, :], row[rows, 32 * q : 32 * q + 1], None, IS_EQUAL)
         quantize_x(0)
+        s1 = tile([P, G * H], U8, "x_bf0")
+        nc.vector.tensor_copy(s1[:], s1_all[:].indirect(list1[:]))
+        w1 = [[tile([P, H], U32, f"w1_{a}_{r}") for r in range(G)] for a in range(PASSES)]
+        round_x(1)
+        w2_all = tile([P, COLS], I32, "column")
+        nc.sync.dma_start(w2_all[:], words_of(w2_words, 0))
         gate_ps = ps.tile([P, P], F32, name="bank6")
         nc.tensor.transpose(gate_ps[:], gate_rows[:], ident[:])
         gate_cols = tile([P, 8], F32, "gate_cols")
         nc.scalar.copy(gate_cols[:], gate_ps[:, 0:8])
-        round_x(1)
         for r in range(G):
             gather_words(w1[0][r], w1_all[0], list1, r)
             for c in range(TOKEN_TILES):
                 first_product(0, r, c)
-        nc.vector.tensor_copy(s2[:], s2_all[:].indirect(list2[:]))
         quantize_x(1)
         for r in range(G):
             gather_words(w1[1][r], w1_all[1], list1, r)
@@ -155,9 +154,8 @@ def tile_moe_wsel_b_silu_f_kernel(
 
         def weigh_and_turn(r, c):
             col = TOKEN_TILES * r + c
-            nc.vector.tensor_scalar(
-                h_bf[r, c][:], act[r, c][:].rearrange("t u p e -> t (u p e)"), gate_cols[:, col : col + 1], None, MULT
-            )
+            values = act[r, c][:].rearrange("t u p e -> t (u p e)")
+            nc.vector.tensor_scalar(h_bf[r, c][:], values, gate_cols[:, col : col + 1], None, MULT)
             if c == 0:
                 turned[r] = ps.tile([P, 2, T], F32, name=f"bank{6 + r % 2}")
             pairs = h_bf[r, c][:].bitcast(F32)
@@ -165,30 +163,20 @@ def tile_moe_wsel_b_silu_f_kernel(
                 nc.tensor.transpose(turned[r][:, u, P * c : P * (c + 1)], pairs[:, P * u : P * (u + 1)], ident[:])
 
         def take_out(r):
-            dst = hT[r][:].bitcast(F32)
-            src = turned[r][:].rearrange("p u t -> p t u")
-            if r == 0:
-                nc.vector.tensor_copy(dst, src)
-            else:
-                nc.scalar.copy(dst, src)
+            nc.scalar.copy(hT[r][:].bitcast(F32), turned[r][:].rearrange("p u t -> p t u"))
 
         def quantize_h(r):
             nc.vector.quantize_mx(
                 out=h_codes[r][:].bitcast(FP8X4), scales=h_scales[r][:], in_=hT[r][:].rearrange("p t j -> p (t j)")
             )
 
-        for r in range(G):
-            for c in range(TOKEN_TILES):
-                activate(r, c)
-                weigh_and_turn(r, c)
-        for r in range(G):
-            take_out(r)
-        y = [ps.tile([P, T], F32, name=f"bank{m}") for m in range(OUT_TILES)]
-        w2 = [tile([P, N], U32, name) for name in ("act11", "act20", "act21")]
-        for r in range(G):
+        w2 = {}
+
+        def gather_w2(r, buffer):
+            w2[r] = tile([P, N], U32, buffer)
             gather_words(w2[r], w2_all, list2, r)
-        for r in range(G):
-            quantize_h(r)
+
+        def second_product(r):
             for m in range(OUT_TILES):
                 nc.tensor.matmul_mx(
                     out=y[m][:],
@@ -199,6 +187,23 @@ def tile_moe_wsel_b_silu_f_kernel(
                     start=(r == 0),
                     stop=(r == G - 1),
                 )
+
+        for r in range(G):
+            if r == G - 1:
+                gather_w2(0, "act11")
+            for c in range(TOKEN_TILES):
+                activate(r, c)
+                weigh_and_turn(r, c)
+        gather_w2(1, "act21")
+        for r in range(G):
+            take_out(r)
+        y = [ps.tile([P, T], F32, name=f"bank{m}") for m in range(OUT_TILES)]
+        quantize_h(0)
+        second_product(0)
+        gather_w2(2, "hT0")
+        for r in range(1, G):
+            quantize_h(r)
+            second_product(r)
         for m in range(OUT_TILES):
             res = tile([P, T], F32, f"res{m}")
             if m % 2 == 0:

@@ -14,6 +14,7 @@ U16 = mybir.dt.uint16
 U8 = mybir.dt.uint8
 FP8X4 = mybir.dt.float8_e4m3fn_x4
 SILU = mybir.ActivationFunctionType.Silu
+COPY = mybir.ActivationFunctionType.Copy
 MULT = mybir.AluOpType.mult
 ADD = mybir.AluOpType.add
 IS_EQUAL = mybir.AluOpType.is_equal
@@ -24,6 +25,7 @@ TOKEN_TILES = T // P
 OUT_TILES = N // P
 COLS = E * H
 W2_PLANE = 8
+GATED_ON_VECTOR = ((0, 0), (0, 1), (2, 0), (2, 1))
 
 
 def tile_moe_wsel_b_silu_f_kernel(
@@ -39,12 +41,13 @@ def tile_moe_wsel_b_silu_f_kernel(
 
         list1 = tile([P, G * H // 16], U16, "list1")
         list2 = tile([P, G * N // 16], U16, "list2")
-        s1_all = tile([P, COLS], U8, "s1_all")
-        s2_all = tile([P, COLS], U8, "s2_all")
+        s1_all = tile([P, COLS], U8, "s1_then_w2")
+        s2_all = tile([P, COLS], U8, "s2_then_w1_1")
         gate_rows = tile([P, P], F32, "gate_rows")
         ident = tile([P, P], F32, "ident")
-        warm_in = tile([P, 8], F32, "buf_w1_0")
-        warm_out = tile([P, 8], F32, "buf_x1")
+        ones = tile([P, P], F32, "ones_then_x0")
+        column = tile([P, P], F32, "column_then_w1_0")
+        row = tile([P, P], F32, "row_then_x1")
 
         def words_of(dram, a):
             return dram[a].rearrange("p n d -> p (n d)").bitcast(I32)
@@ -52,95 +55,72 @@ def tile_moe_wsel_b_silu_f_kernel(
         def rows_of_x(a):
             return xT[512 * a : 512 * (a + 1), :].rearrange("(p j) t -> p j t", j=4)
 
-        nc.vector.memset(s1_all[:].bitcast(I32), 0)
         nc.vector.memset(s2_all[:].bitcast(I32), 0)
-        nc.vector.memset(warm_in[:], 0.0)
-        nc.vector.memset(gate_rows[:], 0.0)
-        nc.scalar.activation(warm_out[:], warm_in[:], SILU)
-
-        x_raw = [tile([P, 4, T], F32, "buf_w1_1"), tile([P, 4, T], F32, "buf_x1")]
-        w1_all = [tile([P, COLS], I32, "buf_w1_0")]
-
-        for q in range(4):
-            nc.gpsimd.dma_start(
-                s1_all[32 * q : 32 * q + 4 * PASSES, :].bitcast(I32),
-                w1_scales[:, 4 * q : 4 * q + 4, :].bitcast(I32),
-            )
-        nc.sync.dma_start(list2[:], offs2)
-        nc.sync.dma_start(list1[:], offs)
-        nc.sync.dma_start(x_raw[0][:], rows_of_x(0))
-        for j in range(4):
-            nc.sync.dma_start(s2_all[W2_PLANE + j : P : 32, :].bitcast(I32), w2_scales[0, j:16:4, :].bitcast(I32))
-        nc.sync.dma_start(gate_rows[0 : G * TOKEN_TILES, :], gate[:, 0, :].rearrange("r (c t) -> r c t", t=P))
-        nc.sync.dma_start(w1_all[0][:], words_of(w1_words, 0))
-        nc.sync.dma_start(x_raw[1][:], rows_of_x(1))
-
-        x_bf = [tile([P, T, 4], BF16, f"x_bf{a}") for a in range(PASSES)]
-        x_codes = {}
-        x_scales = [tile([P, T], U8, f"x_scales{a}") for a in range(PASSES)]
-
-        def round_x(a):
-            nc.scalar.copy(x_bf[a][:], x_raw[a][:].rearrange("p j t -> p t j"))
-
-        def quantize_x(a):
-            x_codes[a] = tile([P, T], U32, "row" if a == 0 else "x_codes1")
-            nc.vector.quantize_mx(
-                out=x_codes[a][:].bitcast(FP8X4), scales=x_scales[a][:], in_=x_bf[a][:].rearrange("p t j -> p (t j)")
-            )
-
-        s2 = tile([P, G * N], U8, "s2")
-
-        def gather_words(dst, window, lst, r):
-            nc.vector.tensor_copy(dst[:], window[:].bitcast(U32).indirect(lst[:, 32 * r : 32 * (r + 1)]))
-
-        acc = {}
-
-        def first_product(a, r, c):
-            if a == 0:
-                acc[r, c] = ps.tile([P, H], F32, name=f"bank{2 * r + c}")
-            nc.tensor.matmul_mx(
-                out=acc[r, c][:],
-                lhsT=x_codes[a][:, P * c : P * (c + 1)].bitcast(FP8X4),
-                lhsT_scale=x_scales[a][:, P * c : P * (c + 1)],
-                rhs=w1[a][r][:].bitcast(FP8X4),
-                rhs_scale=s1[4 * a : P, H * r : H * (r + 1)],
-                start=(a == 0),
-                stop=(a == PASSES - 1),
-            )
-
-        round_x(0)
-        w1_all.append(tile([P, COLS], I32, "buf_w1_1"))
-        nc.sync.dma_start(w1_all[1][:], words_of(w1_words, 1))
-        nc.vector.tensor_copy(s2[:], s2_all[:].indirect(list2[:]))
-        ones = tile([P, P], F32, "s2_all")
-        column = tile([P, P], F32, "column")
-        row = tile([P, P], F32, "row")
+        nc.vector.memset(s1_all[:].bitcast(I32), 0)
         nc.vector.memset(ones[:], 1.0)
+        nc.vector.memset(gate_rows[:], 0.0)
         nc.vector.tensor_tensor_scan(column[:], ones[:], ones[:], 0.0, MULT, ADD)
         nc.vector.transpose(row[:], column[:])
         for q in range(4):
             rows = slice(32 * q, 32 * (q + 1))
             nc.vector.tensor_scalar(ident[rows, :], column[rows, :], row[rows, 32 * q : 32 * q + 1], None, IS_EQUAL)
-        quantize_x(0)
-        s1 = tile([P, G * H], U8, "x_bf0")
+
+        nc.sync.dma_start(list2[:], offs2)
+        nc.sync.dma_start(list1[:], offs)
+        for j in range(4):
+            nc.sync.dma_start(s2_all[W2_PLANE + j : P : 32, :].bitcast(I32), w2_scales[0, j:16:4, :].bitcast(I32))
+        for q in range(4):
+            nc.sync.dma_start(
+                s1_all[32 * q : 32 * q + 4 * PASSES, :].bitcast(I32),
+                w1_scales[:, 4 * q : 4 * q + 4, :].bitcast(I32),
+            )
+        nc.scalar.dma_start(gate_rows[0 : G * TOKEN_TILES, :], gate[:, 0, :].rearrange("r (c t) -> r c t", t=P))
+        x_raw = [tile([P, 4, T], F32, "ones_then_x0"), tile([P, 4, T], F32, "row_then_x1")]
+        w1_all = [tile([P, COLS], I32, "column_then_w1_0")]
+        nc.sync.dma_start(x_raw[0][:], rows_of_x(0))
+        nc.sync.dma_start(w1_all[0][:], words_of(w1_words, 0))
+        nc.sync.dma_start(x_raw[1][:], rows_of_x(1))
+
+        s1 = tile([P, G * H], U8, "s1")
+        s2 = tile([P, G * N], U8, "s2")
+        nc.vector.tensor_copy(s2[:], s2_all[:].indirect(list2[:]))
+        w1_all.append(tile([P, COLS], I32, "s2_then_w1_1"))
+        nc.sync.dma_start(w1_all[1][:], words_of(w1_words, 1))
         nc.vector.tensor_copy(s1[:], s1_all[:].indirect(list1[:]))
-        w1 = [[tile([P, H], U32, f"w1_{a}_{r}") for r in range(G)] for a in range(PASSES)]
-        round_x(1)
-        w2_all = tile([P, COLS], I32, "column")
+        w2_all = tile([P, COLS], I32, "s1_then_w2")
         nc.sync.dma_start(w2_all[:], words_of(w2_words, 0))
+
         gate_ps = ps.tile([P, P], F32, name="bank6")
         nc.tensor.transpose(gate_ps[:], gate_rows[:], ident[:])
         gate_cols = tile([P, 8], F32, "gate_cols")
         nc.scalar.copy(gate_cols[:], gate_ps[:, 0:8])
-        for r in range(G):
-            gather_words(w1[0][r], w1_all[0], list1, r)
-            for c in range(TOKEN_TILES):
-                first_product(0, r, c)
-        quantize_x(1)
-        for r in range(G):
-            gather_words(w1[1][r], w1_all[1], list1, r)
-            for c in range(TOKEN_TILES):
-                first_product(1, r, c)
+
+        x_bf = [tile([P, T, 4], BF16, f"x_bf{a}") for a in range(PASSES)]
+        x_codes = [tile([P, T], U32, f"x_codes{a}") for a in range(PASSES)]
+        x_scales = [tile([P, T], U8, f"x_scales{a}") for a in range(PASSES)]
+        w1 = [[tile([P, H], U32, f"w1_{a}_{r}") for r in range(G)] for a in range(PASSES)]
+        acc = {(r, c): ps.tile([P, H], F32, name=f"bank{2 * r + c}") for r in range(G) for c in range(TOKEN_TILES)}
+
+        def gather_words(dst, window, lst, r):
+            nc.vector.tensor_copy(dst[:], window[:].bitcast(U32).indirect(lst[:, 32 * r : 32 * (r + 1)]))
+
+        for a in range(PASSES):
+            nc.scalar.copy(x_bf[a][:], x_raw[a][:].rearrange("p j t -> p t j"))
+            nc.vector.quantize_mx(
+                out=x_codes[a][:].bitcast(FP8X4), scales=x_scales[a][:], in_=x_bf[a][:].rearrange("p t j -> p (t j)")
+            )
+            for r in range(G):
+                gather_words(w1[a][r], w1_all[a], list1, r)
+                for c in range(TOKEN_TILES):
+                    nc.tensor.matmul_mx(
+                        out=acc[r, c][:],
+                        lhsT=x_codes[a][:, P * c : P * (c + 1)].bitcast(FP8X4),
+                        lhsT_scale=x_scales[a][:, P * c : P * (c + 1)],
+                        rhs=w1[a][r][:].bitcast(FP8X4),
+                        rhs_scale=s1[4 * a : P, H * r : H * (r + 1)],
+                        start=(a == 0),
+                        stop=(a == PASSES - 1),
+                    )
 
         act = {(r, c): tile([P, 2, P, 2], F32, f"act{r}{c}") for r in range(G) for c in range(TOKEN_TILES)}
         h_bf = {(r, c): tile([P, H], BF16, f"h_bf{r}{c}") for r in range(G) for c in range(TOKEN_TILES)}
@@ -148,6 +128,8 @@ def tile_moe_wsel_b_silu_f_kernel(
         h_codes = [tile([P, T], U32, f"h_codes{r}") for r in range(G)]
         h_scales = [tile([P, T], U8, f"h_scales{r}") for r in range(G)]
         turned = {}
+        w2 = {}
+        y = {}
 
         def activate(r, c):
             nc.scalar.activation(act[r, c][:], acc[r, c][:].rearrange("t (p u e) -> t u p e", u=2, e=2), SILU)
@@ -155,7 +137,10 @@ def tile_moe_wsel_b_silu_f_kernel(
         def weigh_and_turn(r, c):
             col = TOKEN_TILES * r + c
             values = act[r, c][:].rearrange("t u p e -> t (u p e)")
-            nc.vector.tensor_scalar(h_bf[r, c][:], values, gate_cols[:, col : col + 1], None, MULT)
+            if (r, c) in GATED_ON_VECTOR:
+                nc.vector.tensor_scalar(h_bf[r, c][:], values, gate_cols[:, col : col + 1], None, MULT)
+            else:
+                nc.scalar.activation(h_bf[r, c][:], values, COPY, scale=gate_cols[:, col : col + 1])
             if c == 0:
                 turned[r] = ps.tile([P, 2, T], F32, name=f"bank{6 + r % 2}")
             pairs = h_bf[r, c][:].bitcast(F32)
@@ -170,14 +155,14 @@ def tile_moe_wsel_b_silu_f_kernel(
                 out=h_codes[r][:].bitcast(FP8X4), scales=h_scales[r][:], in_=hT[r][:].rearrange("p t j -> p (t j)")
             )
 
-        w2 = {}
-
         def gather_w2(r, buffer):
             w2[r] = tile([P, N], U32, buffer)
             gather_words(w2[r], w2_all, list2, r)
 
         def second_product(r):
             for m in range(OUT_TILES):
+                if r == 0:
+                    y[m] = ps.tile([P, T], F32, name=f"bank{m}")
                 nc.tensor.matmul_mx(
                     out=y[m][:],
                     lhsT=w2[r][:, P * m : P * (m + 1)].bitcast(FP8X4),
@@ -188,22 +173,23 @@ def tile_moe_wsel_b_silu_f_kernel(
                     stop=(r == G - 1),
                 )
 
-        for r in range(G):
-            if r == G - 1:
-                gather_w2(0, "act11")
+        for r in range(2):
             for c in range(TOKEN_TILES):
                 activate(r, c)
                 weigh_and_turn(r, c)
-        gather_w2(1, "act21")
-        for r in range(G):
+        gather_w2(0, "w2_0")
+        gather_w2(1, "w2_1")
+        for r in range(2):
             take_out(r)
-        y = [ps.tile([P, T], F32, name=f"bank{m}") for m in range(OUT_TILES)]
-        quantize_h(0)
-        second_product(0)
-        gather_w2(2, "hT0")
-        for r in range(1, G):
             quantize_h(r)
             second_product(r)
+        for c in range(TOKEN_TILES):
+            activate(2, c)
+            weigh_and_turn(2, c)
+        gather_w2(2, "act21")
+        take_out(2)
+        quantize_h(2)
+        second_product(2)
         for m in range(OUT_TILES):
             res = tile([P, T], F32, f"res{m}")
             if m % 2 == 0:

@@ -25,7 +25,7 @@ TOKEN_TILES = T // P
 OUT_TILES = N // P
 COLS = E * H
 W2_PLANE = 8
-GATED_ON_VECTOR = ((0, 0), (0, 1), (2, 0), (2, 1))
+GATED_ON_VECTOR = ((0, 0), (0, 1))
 
 
 def tile_moe_wsel_b_silu_f_kernel(
@@ -41,13 +41,13 @@ def tile_moe_wsel_b_silu_f_kernel(
 
         list1 = tile([P, G * H // 16], U16, "list1")
         list2 = tile([P, G * N // 16], U16, "list2")
-        s1_all = tile([P, COLS], U8, "s1_then_w2")
-        s2_all = tile([P, COLS], U8, "s2_then_w1_1")
+        s1_all = tile([P, COLS], U8, "s1_all")
+        s2_all = tile([P, COLS], U8, "s2_all")
         gate_rows = tile([P, P], F32, "gate_rows")
         ident = tile([P, P], F32, "ident")
-        ones = tile([P, P], F32, "ones_then_x0")
-        column = tile([P, P], F32, "column_then_w1_0")
-        row = tile([P, P], F32, "row_then_x1")
+        ones = tile([P, P], F32, "ones")
+        column = tile([P, P], F32, "column_then_w2")
+        row = tile([P, P], F32, "row")
 
         def words_of(dram, a):
             return dram[a].rearrange("p n d -> p (n d)").bitcast(I32)
@@ -55,39 +55,33 @@ def tile_moe_wsel_b_silu_f_kernel(
         def rows_of_x(a):
             return xT[512 * a : 512 * (a + 1), :].rearrange("(p j) t -> p j t", j=4)
 
-        nc.vector.memset(s2_all[:].bitcast(I32), 0)
         nc.vector.memset(s1_all[:].bitcast(I32), 0)
-        nc.vector.memset(ones[:], 1.0)
         nc.vector.memset(gate_rows[:], 0.0)
+        nc.vector.memset(s2_all[:].bitcast(I32), 0)
+        nc.vector.memset(ones[:], 1.0)
         nc.vector.tensor_tensor_scan(column[:], ones[:], ones[:], 0.0, MULT, ADD)
         nc.vector.transpose(row[:], column[:])
         for q in range(4):
             rows = slice(32 * q, 32 * (q + 1))
             nc.vector.tensor_scalar(ident[rows, :], column[rows, :], row[rows, 32 * q : 32 * q + 1], None, IS_EQUAL)
 
-        nc.sync.dma_start(list2[:], offs2)
-        nc.sync.dma_start(list1[:], offs)
-        for j in range(4):
-            nc.sync.dma_start(s2_all[W2_PLANE + j : P : 32, :].bitcast(I32), w2_scales[0, j:16:4, :].bitcast(I32))
+        x_raw = [tile([P, 4, T], F32, "x_raw0_then_s1"), tile([P, 4, T], F32, "x_raw1")]
+        w1_all = [tile([P, COLS], I32, f"w1_all{a}") for a in range(PASSES)]
+        w2_all = tile([P, COLS], I32, "column_then_w2")
         for q in range(4):
-            nc.sync.dma_start(
+            nc.gpsimd.dma_start(
                 s1_all[32 * q : 32 * q + 4 * PASSES, :].bitcast(I32),
                 w1_scales[:, 4 * q : 4 * q + 4, :].bitcast(I32),
             )
-        nc.scalar.dma_start(gate_rows[0 : G * TOKEN_TILES, :], gate[:, 0, :].rearrange("r (c t) -> r c t", t=P))
-        x_raw = [tile([P, 4, T], F32, "ones_then_x0"), tile([P, 4, T], F32, "row_then_x1")]
-        w1_all = [tile([P, COLS], I32, "column_then_w1_0")]
-        nc.sync.dma_start(x_raw[0][:], rows_of_x(0))
+        nc.sync.dma_start(list1[:], offs)
         nc.sync.dma_start(w1_all[0][:], words_of(w1_words, 0))
+        nc.sync.dma_start(x_raw[0][:], rows_of_x(0))
         nc.sync.dma_start(x_raw[1][:], rows_of_x(1))
-
-        s1 = tile([P, G * H], U8, "s1")
-        s2 = tile([P, G * N], U8, "s2")
-        nc.vector.tensor_copy(s2[:], s2_all[:].indirect(list2[:]))
-        w1_all.append(tile([P, COLS], I32, "s2_then_w1_1"))
         nc.sync.dma_start(w1_all[1][:], words_of(w1_words, 1))
-        nc.vector.tensor_copy(s1[:], s1_all[:].indirect(list1[:]))
-        w2_all = tile([P, COLS], I32, "s1_then_w2")
+        nc.sync.dma_start(list2[:], offs2)
+        nc.sync.dma_start(gate_rows[0 : G * TOKEN_TILES, :], gate[:, 0, :].rearrange("r (c t) -> r c t", t=P))
+        for j in range(4):
+            nc.sync.dma_start(s2_all[W2_PLANE + j : P : 32, :].bitcast(I32), w2_scales[0, j:16:4, :].bitcast(I32))
         nc.sync.dma_start(w2_all[:], words_of(w2_words, 0))
 
         gate_ps = ps.tile([P, P], F32, name="bank6")
@@ -104,20 +98,15 @@ def tile_moe_wsel_b_silu_f_kernel(
         def gather_words(dst, window, lst, r):
             nc.vector.tensor_copy(dst[:], window[:].bitcast(U32).indirect(lst[:, 32 * r : 32 * (r + 1)]))
 
-        for a in range(PASSES):
-            nc.scalar.copy(x_bf[a][:], x_raw[a][:].rearrange("p j t -> p t j"))
-            nc.vector.quantize_mx(
-                out=x_codes[a][:].bitcast(FP8X4), scales=x_scales[a][:], in_=x_bf[a][:].rearrange("p t j -> p (t j)")
-            )
-            for r in range(G):
-                gather_words(w1[a][r], w1_all[a], list1, r)
-                for c in range(TOKEN_TILES):
+        def first_product(r):
+            for c in range(TOKEN_TILES):
+                for a in range(PASSES):
                     nc.tensor.matmul_mx(
                         out=acc[r, c][:],
                         lhsT=x_codes[a][:, P * c : P * (c + 1)].bitcast(FP8X4),
                         lhsT_scale=x_scales[a][:, P * c : P * (c + 1)],
                         rhs=w1[a][r][:].bitcast(FP8X4),
-                        rhs_scale=s1[4 * a : P, H * r : H * (r + 1)],
+                        rhs_scale=s1[r][4 * a : P, :],
                         start=(a == 0),
                         stop=(a == PASSES - 1),
                     )
@@ -125,7 +114,7 @@ def tile_moe_wsel_b_silu_f_kernel(
         act = {(r, c): tile([P, 2, P, 2], F32, f"act{r}{c}") for r in range(G) for c in range(TOKEN_TILES)}
         h_bf = {(r, c): tile([P, H], BF16, f"h_bf{r}{c}") for r in range(G) for c in range(TOKEN_TILES)}
         hT = [tile([P, T, 4], BF16, f"hT{r}") for r in range(G)]
-        h_codes = [tile([P, T], U32, f"h_codes{r}") for r in range(G)]
+        h_codes = {}
         h_scales = [tile([P, T], U8, f"h_scales{r}") for r in range(G)]
         turned = {}
         w2 = {}
@@ -150,7 +139,8 @@ def tile_moe_wsel_b_silu_f_kernel(
         def take_out(r):
             nc.scalar.copy(hT[r][:].bitcast(F32), turned[r][:].rearrange("p u t -> p t u"))
 
-        def quantize_h(r):
+        def quantize_h(r, buffer):
+            h_codes[r] = tile([P, T], U32, buffer)
             nc.vector.quantize_mx(
                 out=h_codes[r][:].bitcast(FP8X4), scales=h_scales[r][:], in_=hT[r][:].rearrange("p t j -> p (t j)")
             )
@@ -173,23 +163,47 @@ def tile_moe_wsel_b_silu_f_kernel(
                     stop=(r == G - 1),
                 )
 
-        for r in range(2):
-            for c in range(TOKEN_TILES):
-                activate(r, c)
-                weigh_and_turn(r, c)
-        gather_w2(0, "w2_0")
-        gather_w2(1, "w2_1")
-        for r in range(2):
-            take_out(r)
-            quantize_h(r)
-            second_product(r)
+        for r in range(G):
+            gather_words(w1[0][r], w1_all[0], list1, r)
+        for a in range(PASSES):
+            nc.scalar.copy(x_bf[a][:], x_raw[a][:].rearrange("p j t -> p t j"))
+        s1_early = tile([P, 2 * H], U8, "x_raw0_then_s1")
+        nc.vector.tensor_copy(s1_early[:], s1_all[:].indirect(list1[:, 0:64]))
+        for a in range(PASSES):
+            nc.vector.quantize_mx(
+                out=x_codes[a][:].bitcast(FP8X4), scales=x_scales[a][:], in_=x_bf[a][:].rearrange("p t j -> p (t j)")
+            )
+        s1 = [s1_early[:, 0:H], s1_early[:, H : 2 * H]]
+        for r in range(G):
+            gather_words(w1[1][r], w1_all[1], list1, r)
+            if r < G - 1:
+                first_product(r)
         for c in range(TOKEN_TILES):
-            activate(2, c)
-            weigh_and_turn(2, c)
-        gather_w2(2, "act21")
+            activate(0, c)
+        for c in range(TOKEN_TILES):
+            weigh_and_turn(0, c)
+        s1_late = tile([P, H], U8, "w1_1_0")
+        nc.vector.tensor_copy(s1_late[:], s1_all[:].indirect(list1[:, 64:96]))
+        s1.append(s1_late[:])
+        first_product(G - 1)
+        s2 = tile([P, G * N], U8, "act01")
+        nc.vector.tensor_copy(s2[:], s2_all[:].indirect(list2[:]))
+
+        for c in range(TOKEN_TILES):
+            activate(1, c)
+        for c in range(TOKEN_TILES):
+            weigh_and_turn(1, c)
+        activate(2, 0)
+        take_out(0)
+        activate(2, 1)
+        take_out(1)
+        weigh_and_turn(2, 0)
+        weigh_and_turn(2, 1)
         take_out(2)
-        quantize_h(2)
-        second_product(2)
+        for r in range(G):
+            gather_w2(r, f"w2_{r}")
+            quantize_h(r, "w2_0" if r == G - 1 else f"h_codes{r}")
+            second_product(r)
         for m in range(OUT_TILES):
             res = tile([P, T], F32, f"res{m}")
             if m % 2 == 0:

@@ -14,7 +14,6 @@ U16 = mybir.dt.uint16
 U8 = mybir.dt.uint8
 FP8X4 = mybir.dt.float8_e4m3fn_x4
 SILU = mybir.ActivationFunctionType.Silu
-COPY = mybir.ActivationFunctionType.Copy
 MULT = mybir.AluOpType.mult
 ADD = mybir.AluOpType.add
 IS_EQUAL = mybir.AluOpType.is_equal
@@ -25,7 +24,6 @@ TOKEN_TILES = T // P
 OUT_TILES = N // P
 COLS = E * H
 W2_PLANE = 8
-GATED_ON_VECTOR = ((0, 0), (0, 1))
 
 
 def tile_moe_wsel_b_silu_f_kernel(
@@ -46,7 +44,7 @@ def tile_moe_wsel_b_silu_f_kernel(
         gate_rows = tile([P, P], F32, "gate_rows")
         ident = tile([P, P], F32, "ident")
         ones = tile([P, P], F32, "ones")
-        column = tile([P, P], F32, "column_then_w2")
+        column = tile([P, P], F32, "column")
         row = tile([P, P], F32, "row")
 
         def words_of(dram, a):
@@ -55,34 +53,31 @@ def tile_moe_wsel_b_silu_f_kernel(
         def rows_of_x(a):
             return xT[512 * a : 512 * (a + 1), :].rearrange("(p j) t -> p j t", j=4)
 
-        nc.vector.memset(s1_all[:].bitcast(I32), 0)
-        nc.vector.memset(gate_rows[:], 0.0)
         nc.vector.memset(s2_all[:].bitcast(I32), 0)
+        nc.vector.memset(s1_all[:].bitcast(I32), 0)
         nc.vector.memset(ones[:], 1.0)
+        nc.vector.memset(gate_rows[:], 0.0)
         nc.vector.tensor_tensor_scan(column[:], ones[:], ones[:], 0.0, MULT, ADD)
         nc.vector.transpose(row[:], column[:])
         for q in range(4):
             rows = slice(32 * q, 32 * (q + 1))
             nc.vector.tensor_scalar(ident[rows, :], column[rows, :], row[rows, 32 * q : 32 * q + 1], None, IS_EQUAL)
 
-        x_raw = [tile([P, 4, T], F32, "x_raw0_then_s1"), tile([P, 4, T], F32, "x_raw1")]
-        w1_all = [tile([P, COLS], I32, f"w1_all{a}") for a in range(PASSES)]
-        w2_all = tile([P, COLS], I32, "column_then_w2")
+        x_raw = [tile([P, 4, T], F32, "x_raw0"), tile([P, 4, T], F32, "row")]
+        w1_all = [tile([P, COLS], I32, "ones")]
         for q in range(4):
             nc.gpsimd.dma_start(
                 s1_all[32 * q : 32 * q + 4 * PASSES, :].bitcast(I32),
                 w1_scales[:, 4 * q : 4 * q + 4, :].bitcast(I32),
             )
-        nc.sync.dma_start(list1[:], offs)
-        nc.sync.dma_start(w1_all[0][:], words_of(w1_words, 0))
-        nc.sync.dma_start(x_raw[0][:], rows_of_x(0))
-        nc.sync.dma_start(x_raw[1][:], rows_of_x(1))
-        nc.sync.dma_start(w1_all[1][:], words_of(w1_words, 1))
         nc.sync.dma_start(list2[:], offs2)
-        nc.sync.dma_start(gate_rows[0 : G * TOKEN_TILES, :], gate[:, 0, :].rearrange("r (c t) -> r c t", t=P))
+        nc.sync.dma_start(list1[:], offs)
+        nc.sync.dma_start(x_raw[0][:], rows_of_x(0))
         for j in range(4):
             nc.sync.dma_start(s2_all[W2_PLANE + j : P : 32, :].bitcast(I32), w2_scales[0, j:16:4, :].bitcast(I32))
-        nc.sync.dma_start(w2_all[:], words_of(w2_words, 0))
+        nc.sync.dma_start(w1_all[0][:], words_of(w1_words, 0))
+        nc.sync.dma_start(gate_rows[0 : G * TOKEN_TILES, :], gate[:, 0, :].rearrange("r (c t) -> r c t", t=P))
+        nc.sync.dma_start(x_raw[1][:], rows_of_x(1))
 
         gate_ps = ps.tile([P, P], F32, name="bank6")
         nc.tensor.transpose(gate_ps[:], gate_rows[:], ident[:])
@@ -90,7 +85,7 @@ def tile_moe_wsel_b_silu_f_kernel(
         nc.scalar.copy(gate_cols[:], gate_ps[:, 0:8])
 
         x_bf = [tile([P, T, 4], BF16, f"x_bf{a}") for a in range(PASSES)]
-        x_codes = [tile([P, T], U32, f"x_codes{a}") for a in range(PASSES)]
+        x_codes = [tile([P, T], U32, "s2_all"), tile([P, T], U32, "x_codes1")]
         x_scales = [tile([P, T], U8, f"x_scales{a}") for a in range(PASSES)]
         w1 = [[tile([P, H], U32, f"w1_{a}_{r}") for r in range(G)] for a in range(PASSES)]
         acc = {(r, c): ps.tile([P, H], F32, name=f"bank{2 * r + c}") for r in range(G) for c in range(TOKEN_TILES)}
@@ -98,18 +93,22 @@ def tile_moe_wsel_b_silu_f_kernel(
         def gather_words(dst, window, lst, r):
             nc.vector.tensor_copy(dst[:], window[:].bitcast(U32).indirect(lst[:, 32 * r : 32 * (r + 1)]))
 
-        def first_product(r):
+        def quantize_x(a):
+            nc.vector.quantize_mx(
+                out=x_codes[a][:].bitcast(FP8X4), scales=x_scales[a][:], in_=x_bf[a][:].rearrange("p t j -> p (t j)")
+            )
+
+        def first_product(a, r):
             for c in range(TOKEN_TILES):
-                for a in range(PASSES):
-                    nc.tensor.matmul_mx(
-                        out=acc[r, c][:],
-                        lhsT=x_codes[a][:, P * c : P * (c + 1)].bitcast(FP8X4),
-                        lhsT_scale=x_scales[a][:, P * c : P * (c + 1)],
-                        rhs=w1[a][r][:].bitcast(FP8X4),
-                        rhs_scale=s1[r][4 * a : P, :],
-                        start=(a == 0),
-                        stop=(a == PASSES - 1),
-                    )
+                nc.tensor.matmul_mx(
+                    out=acc[r, c][:],
+                    lhsT=x_codes[a][:, P * c : P * (c + 1)].bitcast(FP8X4),
+                    lhsT_scale=x_scales[a][:, P * c : P * (c + 1)],
+                    rhs=w1[a][r][:].bitcast(FP8X4),
+                    rhs_scale=s1[r][4 * a : P, :],
+                    start=(a == 0),
+                    stop=(a == PASSES - 1),
+                )
 
         act = {(r, c): tile([P, 2, P, 2], F32, f"act{r}{c}") for r in range(G) for c in range(TOKEN_TILES)}
         h_bf = {(r, c): tile([P, H], BF16, f"h_bf{r}{c}") for r in range(G) for c in range(TOKEN_TILES)}
@@ -126,10 +125,7 @@ def tile_moe_wsel_b_silu_f_kernel(
         def weigh_and_turn(r, c):
             col = TOKEN_TILES * r + c
             values = act[r, c][:].rearrange("t u p e -> t (u p e)")
-            if (r, c) in GATED_ON_VECTOR:
-                nc.vector.tensor_scalar(h_bf[r, c][:], values, gate_cols[:, col : col + 1], None, MULT)
-            else:
-                nc.scalar.activation(h_bf[r, c][:], values, COPY, scale=gate_cols[:, col : col + 1])
+            nc.vector.tensor_scalar(h_bf[r, c][:], values, gate_cols[:, col : col + 1], None, MULT)
             if c == 0:
                 turned[r] = ps.tile([P, 2, T], F32, name=f"bank{6 + r % 2}")
             pairs = h_bf[r, c][:].bitcast(F32)
@@ -163,43 +159,36 @@ def tile_moe_wsel_b_silu_f_kernel(
                     stop=(r == G - 1),
                 )
 
+        def round_x(a):
+            nc.scalar.copy(x_bf[a][:], x_raw[a][:].rearrange("p j t -> p t j"))
+
+        s2 = tile([P, G * N], U8, "s2")
+        nc.vector.tensor_copy(s2[:], s2_all[:].indirect(list2[:]))
+        round_x(0)
+        w1_all.append(tile([P, COLS], I32, "x_raw0"))
+        nc.sync.dma_start(w1_all[1][:], words_of(w1_words, 1))
+        quantize_x(0)
+        w2_all = tile([P, COLS], I32, "x_bf0")
+        nc.sync.dma_start(w2_all[:], words_of(w2_words, 0))
         for r in range(G):
             gather_words(w1[0][r], w1_all[0], list1, r)
-        for a in range(PASSES):
-            nc.scalar.copy(x_bf[a][:], x_raw[a][:].rearrange("p j t -> p t j"))
-        s1_early = tile([P, 2 * H], U8, "x_raw0_then_s1")
-        nc.vector.tensor_copy(s1_early[:], s1_all[:].indirect(list1[:, 0:64]))
-        for a in range(PASSES):
-            nc.vector.quantize_mx(
-                out=x_codes[a][:].bitcast(FP8X4), scales=x_scales[a][:], in_=x_bf[a][:].rearrange("p t j -> p (t j)")
-            )
-        s1 = [s1_early[:, 0:H], s1_early[:, H : 2 * H]]
+        round_x(1)
+        quantize_x(1)
+        s1_tile = tile([P, G * H], U8, "row")
+        s1 = [s1_tile[:, H * r : H * (r + 1)] for r in range(G)]
+        for r in range(G):
+            nc.vector.tensor_copy(s1[r], s1_all[:].indirect(list1[:, 32 * r : 32 * (r + 1)]))
+            first_product(0, r)
         for r in range(G):
             gather_words(w1[1][r], w1_all[1], list1, r)
-            if r < G - 1:
-                first_product(r)
-        for c in range(TOKEN_TILES):
-            activate(0, c)
-        for c in range(TOKEN_TILES):
-            weigh_and_turn(0, c)
-        s1_late = tile([P, H], U8, "w1_1_0")
-        nc.vector.tensor_copy(s1_late[:], s1_all[:].indirect(list1[:, 64:96]))
-        s1.append(s1_late[:])
-        first_product(G - 1)
-        s2 = tile([P, G * N], U8, "act01")
-        nc.vector.tensor_copy(s2[:], s2_all[:].indirect(list2[:]))
-
-        for c in range(TOKEN_TILES):
-            activate(1, c)
-        for c in range(TOKEN_TILES):
-            weigh_and_turn(1, c)
-        activate(2, 0)
-        take_out(0)
-        activate(2, 1)
-        take_out(1)
-        weigh_and_turn(2, 0)
-        weigh_and_turn(2, 1)
-        take_out(2)
+            first_product(1, r)
+        for r in range(G):
+            for c in range(TOKEN_TILES):
+                activate(r, c)
+                weigh_and_turn(r, c)
+            if r > 0:
+                take_out(r - 1)
+        take_out(G - 1)
         for r in range(G):
             gather_w2(r, f"w2_{r}")
             quantize_h(r, "w2_0" if r == G - 1 else f"h_codes{r}")

@@ -53,6 +53,11 @@ def tile_moe_wsel_b_silu_f_kernel(
         def rows_of_x(a):
             return xT[512 * a : 512 * (a + 1), :].rearrange("(p j) t -> p j t", j=4)
 
+        warm_in = tile([P, 8], F32, "warm_in")
+        warm_out = tile([P, 8], F32, "warm_out")
+        nc.gpsimd.memset(warm_in[:], 0.0)
+        nc.scalar.activation(warm_out[:], warm_in[:], SILU)
+
         nc.vector.memset(s2_all[:].bitcast(I32), 0)
         nc.vector.memset(s1_all[:].bitcast(I32), 0)
         nc.vector.memset(ones[:], 1.0)

@@ -24,6 +24,7 @@ TOKEN_TILES = T // P
 OUT_TILES = N // P
 COLS = E * H
 W2_PLANE = 8
+ROWS_AT = 96
 
 
 def tile_moe_wsel_b_silu_f_kernel(
@@ -53,36 +54,26 @@ def tile_moe_wsel_b_silu_f_kernel(
         def rows_of_x(a):
             return xT[512 * a : 512 * (a + 1), :].rearrange("(p j) t -> p j t", j=4)
 
-        warm_in = tile([P, 8], F32, "warm_in")
-        warm_out = tile([P, 8], F32, "warm_out")
-        nc.gpsimd.memset(warm_in[:], 0.0)
-        nc.scalar.activation(warm_out[:], warm_in[:], SILU)
-
-        nc.vector.memset(s2_all[:].bitcast(I32), 0)
-        nc.vector.memset(s1_all[:].bitcast(I32), 0)
         nc.vector.memset(ones[:], 1.0)
-        nc.vector.memset(gate_rows[:], 0.0)
+        nc.vector.memset(s1_all[0:ROWS_AT, :].bitcast(I32), 0)
         nc.vector.tensor_tensor_scan(column[:], ones[:], ones[:], 0.0, MULT, ADD)
+        nc.vector.memset(s2_all[:].bitcast(I32), 0)
+        nc.vector.memset(gate_rows[:], 0.0)
         nc.vector.transpose(row[:], column[:])
         for q in range(4):
             rows = slice(32 * q, 32 * (q + 1))
             nc.vector.tensor_scalar(ident[rows, :], column[rows, :], row[rows, 32 * q : 32 * q + 1], None, IS_EQUAL)
 
-        x_raw = [tile([P, 4, T], F32, "x_raw0"), tile([P, 4, T], F32, "row")]
-        w1_all = [tile([P, COLS], I32, "ones")]
-        for q in range(4):
-            nc.gpsimd.dma_start(
-                s1_all[32 * q : 32 * q + 4 * PASSES, :].bitcast(I32),
-                w1_scales[:, 4 * q : 4 * q + 4, :].bitcast(I32),
-            )
-        nc.sync.dma_start(list2[:], offs2)
+        x_raw = [tile([P, 4, T], F32, f"x_raw{a}") for a in range(PASSES)]
+        w1_all = [tile([P, COLS], I32, "w1_all0")]
         nc.sync.dma_start(list1[:], offs)
-        nc.sync.dma_start(x_raw[0][:], rows_of_x(0))
-        for j in range(4):
-            nc.sync.dma_start(s2_all[W2_PLANE + j : P : 32, :].bitcast(I32), w2_scales[0, j:16:4, :].bitcast(I32))
+        nc.sync.dma_start(s1_all[ROWS_AT:P, :].bitcast(I32), w1_scales.rearrange("a b n -> b a n").bitcast(I32))
+        nc.sync.dma_start(list2[:], offs2)
         nc.sync.dma_start(w1_all[0][:], words_of(w1_words, 0))
-        nc.sync.dma_start(gate_rows[0 : G * TOKEN_TILES, :], gate[:, 0, :].rearrange("r (c t) -> r c t", t=P))
+        nc.sync.dma_start(x_raw[0][:], rows_of_x(0))
         nc.sync.dma_start(x_raw[1][:], rows_of_x(1))
+        nc.sync.dma_start(s2_all[0:P:8, :].bitcast(I32), w2_scales[0].bitcast(I32))
+        nc.sync.dma_start(gate_rows[0 : G * TOKEN_TILES, :], gate[:, 0, :].rearrange("r (c t) -> r c t", t=P))
 
         gate_ps = ps.tile([P, P], F32, name="bank6")
         nc.tensor.transpose(gate_ps[:], gate_rows[:], ident[:])
@@ -90,7 +81,7 @@ def tile_moe_wsel_b_silu_f_kernel(
         nc.scalar.copy(gate_cols[:], gate_ps[:, 0:8])
 
         x_bf = [tile([P, T, 4], BF16, f"x_bf{a}") for a in range(PASSES)]
-        x_codes = [tile([P, T], U32, "s2_all"), tile([P, T], U32, "x_codes1")]
+        x_codes = [tile([P, T], U32, "x_codes0"), tile([P, T], U32, "x_codes1")]
         x_scales = [tile([P, T], U8, f"x_scales{a}") for a in range(PASSES)]
         w1 = [[tile([P, H], U32, f"w1_{a}_{r}") for r in range(G)] for a in range(PASSES)]
         acc = {(r, c): ps.tile([P, H], F32, name=f"bank{2 * r + c}") for r in range(G) for c in range(TOKEN_TILES)}
@@ -110,7 +101,7 @@ def tile_moe_wsel_b_silu_f_kernel(
                     lhsT=x_codes[a][:, P * c : P * (c + 1)].bitcast(FP8X4),
                     lhsT_scale=x_scales[a][:, P * c : P * (c + 1)],
                     rhs=w1[a][r][:].bitcast(FP8X4),
-                    rhs_scale=s1[r][4 * a : P, :],
+                    rhs_scale=s1[:, a, H * r : H * (r + 1)],
                     start=(a == 0),
                     stop=(a == PASSES - 1),
                 )
@@ -167,37 +158,54 @@ def tile_moe_wsel_b_silu_f_kernel(
         def round_x(a):
             nc.scalar.copy(x_bf[a][:], x_raw[a][:].rearrange("p j t -> p t j"))
 
-        s2 = tile([P, G * N], U8, "s2")
-        nc.vector.tensor_copy(s2[:], s2_all[:].indirect(list2[:]))
-        round_x(0)
-        w1_all.append(tile([P, COLS], I32, "x_raw0"))
+        s1_rows = tile([P, G * H], U8, "s1_rows")
+        nc.vector.tensor_copy(s1_rows[:], s1_all[:].indirect(list1[:]))
+        s1 = tile([P, PASSES, G * H], U8, "s1")
+        for q in range(4):
+            nc.sync.dma_start(
+                s1[32 * q : 32 * q + 4, :, :].bitcast(I32),
+                s1_rows[ROWS_AT + 8 * q : ROWS_AT + 8 * (q + 1), :].bitcast(I32),
+            )
+        w1_all.append(tile([P, COLS], I32, "s1_all"))
         nc.sync.dma_start(w1_all[1][:], words_of(w1_words, 1))
-        quantize_x(0)
-        w2_all = tile([P, COLS], I32, "x_bf0")
+        round_x(0)
+        w2_all = tile([P, COLS], I32, "x_raw0")
         nc.sync.dma_start(w2_all[:], words_of(w2_words, 0))
         for r in range(G):
             gather_words(w1[0][r], w1_all[0], list1, r)
+        quantize_x(0)
+        for r in range(G):
+            first_product(0, r)
         round_x(1)
         quantize_x(1)
-        s1_tile = tile([P, G * H], U8, "row")
-        s1 = [s1_tile[:, H * r : H * (r + 1)] for r in range(G)]
-        for r in range(G):
-            nc.vector.tensor_copy(s1[r], s1_all[:].indirect(list1[:, 32 * r : 32 * (r + 1)]))
-            first_product(0, r)
+        s2_rows = tile([P, G * N], U8, "x_raw1")
+        nc.vector.tensor_copy(s2_rows[:], s2_all[:].indirect(list2[:]))
+        s2 = tile([P, G * N], U8, "s2")
+        for q in range(4):
+            nc.sync.dma_start(
+                s2[32 * q + W2_PLANE : 32 * q + W2_PLANE + 4, :].bitcast(I32),
+                s2_rows[32 * q : 32 * (q + 1) : 8, :].bitcast(I32),
+            )
         for r in range(G):
             gather_words(w1[1][r], w1_all[1], list1, r)
             first_product(1, r)
         for r in range(G):
+            if r == G - 1:
+                gather_w2(0, "act11")
+                take_out(0)
             for c in range(TOKEN_TILES):
                 activate(r, c)
                 weigh_and_turn(r, c)
-            if r > 0:
-                take_out(r - 1)
-        take_out(G - 1)
-        for r in range(G):
-            gather_w2(r, f"w2_{r}")
-            quantize_h(r, "w2_0" if r == G - 1 else f"h_codes{r}")
-            second_product(r)
+        take_out(1)
+        take_out(2)
+        quantize_h(0, "h_codes0")
+        second_product(0)
+        gather_w2(1, "act21")
+        quantize_h(1, "h_codes1")
+        second_product(1)
+        gather_w2(2, "hT1")
+        quantize_h(2, "h_codes2")
+        second_product(2)
         for m in range(OUT_TILES):
             res = tile([P, T], F32, f"res{m}")
             if m % 2 == 0:

@@ -14,8 +14,10 @@ U16 = mybir.dt.uint16
 U8 = mybir.dt.uint8
 FP8X4 = mybir.dt.float8_e4m3fn_x4
 SILU = mybir.ActivationFunctionType.Silu
+COPY = mybir.ActivationFunctionType.Copy
 MULT = mybir.AluOpType.mult
 ADD = mybir.AluOpType.add
+SUBTRACT = mybir.AluOpType.subtract
 IS_EQUAL = mybir.AluOpType.is_equal
 
 P = 128
@@ -46,7 +48,8 @@ def tile_moe_wsel_b_silu_f_kernel(
         ident = tile([P, P], F32, "ident")
         ones = tile([P, P], F32, "ones")
         column = tile([P, P], F32, "column")
-        row = tile([P, P], F32, "row")
+        row = tile([P, 32], F32, "row")
+        quadrant = tile([P, 1], F32, "quadrant")
 
         def words_of(dram, a):
             return dram[a].rearrange("p n d -> p (n d)").bitcast(I32)
@@ -59,10 +62,10 @@ def tile_moe_wsel_b_silu_f_kernel(
         nc.vector.tensor_tensor_scan(column[:], ones[:], ones[:], 0.0, MULT, ADD)
         nc.vector.memset(s2_all[:].bitcast(I32), 0)
         nc.vector.memset(gate_rows[:], 0.0)
-        nc.vector.transpose(row[:], column[:])
         for q in range(4):
-            rows = slice(32 * q, 32 * (q + 1))
-            nc.vector.tensor_scalar(ident[rows, :], column[rows, :], row[rows, 32 * q : 32 * q + 1], None, IS_EQUAL)
+            nc.gpsimd.memset(quadrant[32 * q : 32 * (q + 1), :], 32.0 * q)
+        nc.vector.transpose(row[:], column[:, 0:32])
+        nc.vector.tensor_scalar(ident[:], column[:], row[:, 0:1], quadrant[:], SUBTRACT, IS_EQUAL)
 
         x_raw = [tile([P, 4, T], F32, f"x_raw{a}") for a in range(PASSES)]
         w1_all = [tile([P, COLS], I32, "w1_all0")]
@@ -83,11 +86,15 @@ def tile_moe_wsel_b_silu_f_kernel(
         x_bf = [tile([P, T, 4], BF16, f"x_bf{a}") for a in range(PASSES)]
         x_codes = [tile([P, T], U32, "x_codes0"), tile([P, T], U32, "x_codes1")]
         x_scales = [tile([P, T], U8, f"x_scales{a}") for a in range(PASSES)]
-        w1 = [[tile([P, H], U32, f"w1_{a}_{r}") for r in range(G)] for a in range(PASSES)]
+        w1_first = tile([P, G * H], U32, "w1_first")
+        w1 = [
+            [w1_first[:, H * r : H * (r + 1)] for r in range(G)],
+            [tile([P, H], U32, f"w1_second{r}")[:] for r in range(G)],
+        ]
         acc = {(r, c): ps.tile([P, H], F32, name=f"bank{2 * r + c}") for r in range(G) for c in range(TOKEN_TILES)}
 
         def gather_words(dst, window, lst, r):
-            nc.vector.tensor_copy(dst[:], window[:].bitcast(U32).indirect(lst[:, 32 * r : 32 * (r + 1)]))
+            nc.vector.tensor_copy(dst, window[:].bitcast(U32).indirect(lst[:, 32 * r : 32 * (r + 1)]))
 
         def quantize_x(a):
             nc.vector.quantize_mx(
@@ -100,7 +107,7 @@ def tile_moe_wsel_b_silu_f_kernel(
                     out=acc[r, c][:],
                     lhsT=x_codes[a][:, P * c : P * (c + 1)].bitcast(FP8X4),
                     lhsT_scale=x_scales[a][:, P * c : P * (c + 1)],
-                    rhs=w1[a][r][:].bitcast(FP8X4),
+                    rhs=w1[a][r].bitcast(FP8X4),
                     rhs_scale=s1[:, a, H * r : H * (r + 1)],
                     start=(a == 0),
                     stop=(a == PASSES - 1),
@@ -121,7 +128,10 @@ def tile_moe_wsel_b_silu_f_kernel(
         def weigh_and_turn(r, c):
             col = TOKEN_TILES * r + c
             values = act[r, c][:].rearrange("t u p e -> t (u p e)")
-            nc.vector.tensor_scalar(h_bf[r, c][:], values, gate_cols[:, col : col + 1], None, MULT)
+            if r < G - 1:
+                nc.vector.tensor_scalar(h_bf[r, c][:], values, gate_cols[:, col : col + 1], None, MULT)
+            else:
+                nc.scalar.activation(h_bf[r, c][:], values, COPY, scale=gate_cols[:, col : col + 1])
             if c == 0:
                 turned[r] = ps.tile([P, 2, T], F32, name=f"bank{6 + r % 2}")
             pairs = h_bf[r, c][:].bitcast(F32)
@@ -139,7 +149,7 @@ def tile_moe_wsel_b_silu_f_kernel(
 
         def gather_w2(r, buffer):
             w2[r] = tile([P, N], U32, buffer)
-            gather_words(w2[r], w2_all, list2, r)
+            gather_words(w2[r][:], w2_all, list2, r)
 
         def second_product(r):
             for m in range(OUT_TILES):
@@ -161,7 +171,7 @@ def tile_moe_wsel_b_silu_f_kernel(
         s1_rows = tile([P, G * H], U8, "s1_rows")
         nc.vector.tensor_copy(s1_rows[:], s1_all[:].indirect(list1[:]))
         s1 = tile([P, PASSES, G * H], U8, "s1")
-        for q in range(4):
+        for q in (0, 2, 1, 3):
             nc.sync.dma_start(
                 s1[32 * q : 32 * q + 4, :, :].bitcast(I32),
                 s1_rows[ROWS_AT + 8 * q : ROWS_AT + 8 * (q + 1), :].bitcast(I32),
@@ -171,8 +181,7 @@ def tile_moe_wsel_b_silu_f_kernel(
         round_x(0)
         w2_all = tile([P, COLS], I32, "x_raw0")
         nc.sync.dma_start(w2_all[:], words_of(w2_words, 0))
-        for r in range(G):
-            gather_words(w1[0][r], w1_all[0], list1, r)
+        nc.vector.tensor_copy(w1_first[:], w1_all[0][:].bitcast(U32).indirect(list1[:]))
         quantize_x(0)
         for r in range(G):
             first_product(0, r)
@@ -181,7 +190,7 @@ def tile_moe_wsel_b_silu_f_kernel(
         s2_rows = tile([P, G * N], U8, "x_raw1")
         nc.vector.tensor_copy(s2_rows[:], s2_all[:].indirect(list2[:]))
         s2 = tile([P, G * N], U8, "s2")
-        for q in range(4):
+        for q in (0, 2, 1, 3):
             nc.sync.dma_start(
                 s2[32 * q + W2_PLANE : 32 * q + W2_PLANE + 4, :].bitcast(I32),
                 s2_rows[32 * q : 32 * (q + 1) : 8, :].bitcast(I32),
@@ -189,23 +198,21 @@ def tile_moe_wsel_b_silu_f_kernel(
         for r in range(G):
             gather_words(w1[1][r], w1_all[1], list1, r)
             first_product(1, r)
-        for r in range(G):
-            if r == G - 1:
-                gather_w2(0, "act11")
-                take_out(0)
+        for r in range(G - 1):
             for c in range(TOKEN_TILES):
                 activate(r, c)
                 weigh_and_turn(r, c)
-        take_out(1)
-        take_out(2)
-        quantize_h(0, "h_codes0")
-        second_product(0)
-        gather_w2(1, "act21")
-        quantize_h(1, "h_codes1")
-        second_product(1)
-        gather_w2(2, "hT1")
-        quantize_h(2, "h_codes2")
-        second_product(2)
+        activate(G - 1, 0)
+        take_out(0)
+        activate(G - 1, 1)
+        for c in range(TOKEN_TILES):
+            weigh_and_turn(G - 1, c)
+        for r in range(1, G):
+            take_out(r)
+        for r in range(G):
+            gather_w2(r, "act11" if r == 0 else f"hT{r - 1}")
+            quantize_h(r, f"h_codes{r}")
+            second_product(r)
         for m in range(OUT_TILES):
             res = tile([P, T], F32, f"res{m}")
             if m % 2 == 0:

@@ -25,8 +25,12 @@ PASSES = K // 512
 TOKEN_TILES = T // P
 OUT_TILES = N // P
 COLS = E * H
+LAST = G - 1
+W1_ROWS_AT = 96
+W2_ROW_STEP = 8
 W2_PLANE = 8
-ROWS_AT = 96
+QUADRANTS_BY_PORT = (0, 2, 1, 3)
+GATED_ON_SCALAR = (LAST, 0)
 
 
 def tile_moe_wsel_b_silu_f_kernel(
@@ -35,10 +39,11 @@ def tile_moe_wsel_b_silu_f_kernel(
     nc = tc.nc
     with ExitStack() as ctx:
         sb = ctx.enter_context(tc.tile_pool(name="sb", bufs=1))
+        shared = ctx.enter_context(tc.tile_pool(name="shared", bufs=1))
         ps = ctx.enter_context(tc.psum_pool(name="ps", bufs=1))
 
-        def tile(shape, dtype, name):
-            return sb.tile(shape, dtype, name=name, align_bytes=64)
+        def tile(shape, dtype, buffer):
+            return sb.tile(shape, dtype, name=buffer, align_bytes=64)
 
         list1 = tile([P, G * H // 16], U16, "list1")
         list2 = tile([P, G * N // 16], U16, "list2")
@@ -58,7 +63,7 @@ def tile_moe_wsel_b_silu_f_kernel(
             return xT[512 * a : 512 * (a + 1), :].rearrange("(p j) t -> p j t", j=4)
 
         nc.vector.memset(ones[:], 1.0)
-        nc.vector.memset(s1_all[0:ROWS_AT, :].bitcast(I32), 0)
+        nc.vector.memset(s1_all[0:W1_ROWS_AT, :].bitcast(I32), 0)
         nc.vector.tensor_tensor_scan(column[:], ones[:], ones[:], 0.0, MULT, ADD)
         nc.vector.memset(s2_all[:].bitcast(I32), 0)
         nc.vector.memset(gate_rows[:], 0.0)
@@ -67,15 +72,18 @@ def tile_moe_wsel_b_silu_f_kernel(
         nc.vector.transpose(row[:], column[:, 0:32])
         nc.vector.tensor_scalar(ident[:], column[:], row[:, 0:1], quadrant[:], SUBTRACT, IS_EQUAL)
 
-        x_raw = [tile([P, 4, T], F32, f"x_raw{a}") for a in range(PASSES)]
+        x_raw = [
+            shared.tile([P, 4, T], F32, name="x_raw0", offset=4 * COLS - 8 * T, align_bytes=64),
+            tile([P, 4, T], F32, "x_raw1"),
+        ]
         w1_all = [tile([P, COLS], I32, "w1_all0")]
         nc.sync.dma_start(list1[:], offs)
-        nc.sync.dma_start(s1_all[ROWS_AT:P, :].bitcast(I32), w1_scales.rearrange("a b n -> b a n").bitcast(I32))
+        nc.sync.dma_start(s1_all[W1_ROWS_AT:P, :].bitcast(I32), w1_scales.rearrange("a b n -> b a n").bitcast(I32))
         nc.sync.dma_start(list2[:], offs2)
         nc.sync.dma_start(w1_all[0][:], words_of(w1_words, 0))
         nc.sync.dma_start(x_raw[0][:], rows_of_x(0))
         nc.sync.dma_start(x_raw[1][:], rows_of_x(1))
-        nc.sync.dma_start(s2_all[0:P:8, :].bitcast(I32), w2_scales[0].bitcast(I32))
+        nc.sync.dma_start(s2_all[0:P:W2_ROW_STEP, :].bitcast(I32), w2_scales[0].bitcast(I32))
         nc.sync.dma_start(gate_rows[0 : G * TOKEN_TILES, :], gate[:, 0, :].rearrange("r (c t) -> r c t", t=P))
 
         gate_ps = ps.tile([P, P], F32, name="bank6")
@@ -84,7 +92,7 @@ def tile_moe_wsel_b_silu_f_kernel(
         nc.scalar.copy(gate_cols[:], gate_ps[:, 0:8])
 
         x_bf = [tile([P, T, 4], BF16, f"x_bf{a}") for a in range(PASSES)]
-        x_codes = [tile([P, T], U32, "x_codes0"), tile([P, T], U32, "x_codes1")]
+        x_codes = [tile([P, T], U32, f"x_codes{a}") for a in range(PASSES)]
         x_scales = [tile([P, T], U8, f"x_scales{a}") for a in range(PASSES)]
         w1_first = tile([P, G * H], U32, "w1_first")
         w1 = [
@@ -92,13 +100,24 @@ def tile_moe_wsel_b_silu_f_kernel(
             [tile([P, H], U32, f"w1_second{r}")[:] for r in range(G)],
         ]
         acc = {(r, c): ps.tile([P, H], F32, name=f"bank{2 * r + c}") for r in range(G) for c in range(TOKEN_TILES)}
+        act = {(r, c): tile([P, 2, P, 2], F32, f"act{r}{c}") for r in range(G) for c in range(TOKEN_TILES)}
+        h_bf = {(r, c): tile([P, H], BF16, f"h_bf{r}{c}") for r in range(G) for c in range(TOKEN_TILES)}
+        hT = [tile([P, T, 4], BF16, f"hT{r}") for r in range(G)]
+        h_codes = [tile([P, T], U32, f"h_codes{r}") for r in range(G)]
+        h_scales = [tile([P, T], U8, f"h_scales{r}") for r in range(G)]
+        turned = {}
+        w2 = {}
+        y = {}
 
-        def gather_words(dst, window, lst, r):
+        def gather_expert(dst, window, lst, r):
             nc.vector.tensor_copy(dst, window[:].bitcast(U32).indirect(lst[:, 32 * r : 32 * (r + 1)]))
 
-        def quantize_x(a):
+        def round_x(a):
+            nc.scalar.copy(x_bf[a][:], x_raw[a][:].rearrange("p j t -> p t j"))
+
+        def quantize(codes, scales, values):
             nc.vector.quantize_mx(
-                out=x_codes[a][:].bitcast(FP8X4), scales=x_scales[a][:], in_=x_bf[a][:].rearrange("p t j -> p (t j)")
+                out=codes[:].bitcast(FP8X4), scales=scales[:], in_=values[:].rearrange("p t j -> p (t j)")
             )
 
         def first_product(a, r):
@@ -113,25 +132,16 @@ def tile_moe_wsel_b_silu_f_kernel(
                     stop=(a == PASSES - 1),
                 )
 
-        act = {(r, c): tile([P, 2, P, 2], F32, f"act{r}{c}") for r in range(G) for c in range(TOKEN_TILES)}
-        h_bf = {(r, c): tile([P, H], BF16, f"h_bf{r}{c}") for r in range(G) for c in range(TOKEN_TILES)}
-        hT = [tile([P, T, 4], BF16, f"hT{r}") for r in range(G)]
-        h_codes = {}
-        h_scales = [tile([P, T], U8, f"h_scales{r}") for r in range(G)]
-        turned = {}
-        w2 = {}
-        y = {}
-
         def activate(r, c):
             nc.scalar.activation(act[r, c][:], acc[r, c][:].rearrange("t (p u e) -> t u p e", u=2, e=2), SILU)
 
         def weigh_and_turn(r, c):
-            col = TOKEN_TILES * r + c
+            gate_col = gate_cols[:, TOKEN_TILES * r + c : TOKEN_TILES * r + c + 1]
             values = act[r, c][:].rearrange("t u p e -> t (u p e)")
-            if r < G - 1:
-                nc.vector.tensor_scalar(h_bf[r, c][:], values, gate_cols[:, col : col + 1], None, MULT)
+            if (r, c) == GATED_ON_SCALAR:
+                nc.scalar.activation(h_bf[r, c][:], values, COPY, scale=gate_col)
             else:
-                nc.scalar.activation(h_bf[r, c][:], values, COPY, scale=gate_cols[:, col : col + 1])
+                nc.vector.tensor_scalar(h_bf[r, c][:], values, gate_col, None, MULT)
             if c == 0:
                 turned[r] = ps.tile([P, 2, T], F32, name=f"bank{6 + r % 2}")
             pairs = h_bf[r, c][:].bitcast(F32)
@@ -141,17 +151,10 @@ def tile_moe_wsel_b_silu_f_kernel(
         def take_out(r):
             nc.scalar.copy(hT[r][:].bitcast(F32), turned[r][:].rearrange("p u t -> p t u"))
 
-        def quantize_h(r, buffer):
-            h_codes[r] = tile([P, T], U32, buffer)
-            nc.vector.quantize_mx(
-                out=h_codes[r][:].bitcast(FP8X4), scales=h_scales[r][:], in_=hT[r][:].rearrange("p t j -> p (t j)")
-            )
-
-        def gather_w2(r, buffer):
+        def second_product(r, buffer):
             w2[r] = tile([P, N], U32, buffer)
-            gather_words(w2[r][:], w2_all, list2, r)
-
-        def second_product(r):
+            gather_expert(w2[r][:], w2_all, list2, r)
+            quantize(h_codes[r], h_scales[r], hT[r])
             for m in range(OUT_TILES):
                 if r == 0:
                     y[m] = ps.tile([P, T], F32, name=f"bank{m}")
@@ -162,57 +165,59 @@ def tile_moe_wsel_b_silu_f_kernel(
                     rhs=h_codes[r][:].bitcast(FP8X4),
                     rhs_scale=h_scales[r][:],
                     start=(r == 0),
-                    stop=(r == G - 1),
+                    stop=(r == LAST),
                 )
-
-        def round_x(a):
-            nc.scalar.copy(x_bf[a][:], x_raw[a][:].rearrange("p j t -> p t j"))
 
         s1_rows = tile([P, G * H], U8, "s1_rows")
         nc.vector.tensor_copy(s1_rows[:], s1_all[:].indirect(list1[:]))
         s1 = tile([P, PASSES, G * H], U8, "s1")
-        for q in (0, 2, 1, 3):
+        for q in QUADRANTS_BY_PORT:
             nc.sync.dma_start(
                 s1[32 * q : 32 * q + 4, :, :].bitcast(I32),
-                s1_rows[ROWS_AT + 8 * q : ROWS_AT + 8 * (q + 1), :].bitcast(I32),
+                s1_rows[W1_ROWS_AT + 8 * q : W1_ROWS_AT + 8 * (q + 1), :].bitcast(I32),
             )
+
         w1_all.append(tile([P, COLS], I32, "s1_all"))
         nc.sync.dma_start(w1_all[1][:], words_of(w1_words, 1))
         round_x(0)
-        w2_all = tile([P, COLS], I32, "x_raw0")
+        w2_all = shared.tile([P, COLS], I32, name="w2_all", offset=0, align_bytes=64)
         nc.sync.dma_start(w2_all[:], words_of(w2_words, 0))
+
         nc.vector.tensor_copy(w1_first[:], w1_all[0][:].bitcast(U32).indirect(list1[:]))
-        quantize_x(0)
+        quantize(x_codes[0], x_scales[0], x_bf[0])
         for r in range(G):
             first_product(0, r)
         round_x(1)
-        quantize_x(1)
-        s2_rows = tile([P, G * N], U8, "x_raw1")
+
+        s2_rows = shared.tile([P, G * N], U8, name="s2_rows", offset=4 * COLS, align_bytes=64)
         nc.vector.tensor_copy(s2_rows[:], s2_all[:].indirect(list2[:]))
+        quantize(x_codes[1], x_scales[1], x_bf[1])
         s2 = tile([P, G * N], U8, "s2")
-        for q in (0, 2, 1, 3):
+        for q in QUADRANTS_BY_PORT:
             nc.sync.dma_start(
                 s2[32 * q + W2_PLANE : 32 * q + W2_PLANE + 4, :].bitcast(I32),
-                s2_rows[32 * q : 32 * (q + 1) : 8, :].bitcast(I32),
+                s2_rows[32 * q : 32 * (q + 1) : W2_ROW_STEP, :].bitcast(I32),
             )
+
         for r in range(G):
-            gather_words(w1[1][r], w1_all[1], list1, r)
+            gather_expert(w1[1][r], w1_all[1], list1, r)
             first_product(1, r)
-        for r in range(G - 1):
+
+        for r in range(LAST):
             for c in range(TOKEN_TILES):
                 activate(r, c)
                 weigh_and_turn(r, c)
-        activate(G - 1, 0)
+        activate(LAST, 0)
         take_out(0)
-        activate(G - 1, 1)
+        activate(LAST, 1)
+        second_product(0, "act11")
         for c in range(TOKEN_TILES):
-            weigh_and_turn(G - 1, c)
+            weigh_and_turn(LAST, c)
         for r in range(1, G):
             take_out(r)
-        for r in range(G):
-            gather_w2(r, "act11" if r == 0 else f"hT{r - 1}")
-            quantize_h(r, f"h_codes{r}")
-            second_product(r)
+        second_product(1, "act21")
+        second_product(2, "hT1")
+
         for m in range(OUT_TILES):
             res = tile([P, T], F32, f"res{m}")
             if m % 2 == 0:

@@ -14,7 +14,6 @@ U16 = mybir.dt.uint16
 U8 = mybir.dt.uint8
 FP8X4 = mybir.dt.float8_e4m3fn_x4
 SILU = mybir.ActivationFunctionType.Silu
-COPY = mybir.ActivationFunctionType.Copy
 MULT = mybir.AluOpType.mult
 ADD = mybir.AluOpType.add
 SUBTRACT = mybir.AluOpType.subtract
@@ -30,7 +29,6 @@ W1_ROWS_AT = 96
 W2_ROW_STEP = 8
 W2_PLANE = 8
 QUADRANTS_BY_PORT = (0, 2, 1, 3)
-GATED_ON_SCALAR = (LAST, 0)
 
 
 def tile_moe_wsel_b_silu_f_kernel(
@@ -39,17 +37,19 @@ def tile_moe_wsel_b_silu_f_kernel(
     nc = tc.nc
     with ExitStack() as ctx:
         sb = ctx.enter_context(tc.tile_pool(name="sb", bufs=1))
-        shared = ctx.enter_context(tc.tile_pool(name="shared", bufs=1))
         ps = ctx.enter_context(tc.psum_pool(name="ps", bufs=1))
 
         def tile(shape, dtype, buffer):
             return sb.tile(shape, dtype, name=buffer, align_bytes=64)
 
+        def bank(shape, number):
+            return ps.tile(shape, F32, name=f"bank{number}")
+
         list1 = tile([P, G * H // 16], U16, "list1")
         list2 = tile([P, G * N // 16], U16, "list2")
         s1_all = tile([P, COLS], U8, "s1_all")
         s2_all = tile([P, COLS], U8, "s2_all")
-        gate_rows = tile([P, P], F32, "gate_rows")
+        gate_rows = tile([P, G, P], F32, "gate_rows")
         ident = tile([P, P], F32, "ident")
         ones = tile([P, P], F32, "ones")
         column = tile([P, P], F32, "column")
@@ -62,49 +62,40 @@ def tile_moe_wsel_b_silu_f_kernel(
         def rows_of_x(a):
             return xT[512 * a : 512 * (a + 1), :].rearrange("(p j) t -> p j t", j=4)
 
+        nc.vector.memset(s2_all[:].bitcast(I32), 0)
         nc.vector.memset(ones[:], 1.0)
         nc.vector.memset(s1_all[0:W1_ROWS_AT, :].bitcast(I32), 0)
         nc.vector.tensor_tensor_scan(column[:], ones[:], ones[:], 0.0, MULT, ADD)
-        nc.vector.memset(s2_all[:].bitcast(I32), 0)
-        nc.vector.memset(gate_rows[:], 0.0)
+        nc.gpsimd.memset(gate_rows[:], 0.0)
         for q in range(4):
             nc.gpsimd.memset(quadrant[32 * q : 32 * (q + 1), :], 32.0 * q)
         nc.vector.transpose(row[:], column[:, 0:32])
         nc.vector.tensor_scalar(ident[:], column[:], row[:, 0:1], quadrant[:], SUBTRACT, IS_EQUAL)
 
-        x_raw = [
-            shared.tile([P, 4, T], F32, name="x_raw0", offset=4 * COLS - 8 * T, align_bytes=64),
-            tile([P, 4, T], F32, "x_raw1"),
-        ]
-        w1_all = [tile([P, COLS], I32, "w1_all0")]
+        x_raw = [tile([P, 4, T], F32, f"x_raw{a}") for a in range(PASSES)]
+        w1_all = [tile([P, COLS], I32, f"w1_all{a}") for a in range(PASSES)]
+        w2_all = tile([P, COLS], I32, "w2_all")
         nc.sync.dma_start(list1[:], offs)
         nc.sync.dma_start(s1_all[W1_ROWS_AT:P, :].bitcast(I32), w1_scales.rearrange("a b n -> b a n").bitcast(I32))
+        nc.sync.dma_start(x_raw[0][:], rows_of_x(0))
         nc.sync.dma_start(list2[:], offs2)
         nc.sync.dma_start(w1_all[0][:], words_of(w1_words, 0))
-        nc.sync.dma_start(x_raw[0][:], rows_of_x(0))
         nc.sync.dma_start(x_raw[1][:], rows_of_x(1))
-        nc.sync.dma_start(s2_all[0:P:W2_ROW_STEP, :].bitcast(I32), w2_scales[0].bitcast(I32))
-        nc.sync.dma_start(gate_rows[0 : G * TOKEN_TILES, :], gate[:, 0, :].rearrange("r (c t) -> r c t", t=P))
-
-        gate_ps = ps.tile([P, P], F32, name="bank6")
-        nc.tensor.transpose(gate_ps[:], gate_rows[:], ident[:])
-        gate_cols = tile([P, 8], F32, "gate_cols")
-        nc.scalar.copy(gate_cols[:], gate_ps[:, 0:8])
+        nc.sync.dma_start(w1_all[1][:], words_of(w1_words, 1))
+        nc.sync.dma_start(w2_all[:], words_of(w2_words, 0))
+        nc.scalar.dma_start(s2_all[0:P:W2_ROW_STEP, :].bitcast(I32), w2_scales[0].bitcast(I32))
+        nc.scalar.dma_start(gate_rows[0:TOKEN_TILES, :, :], gate[:, 0, :].rearrange("r (c t) -> c r t", t=P))
 
         x_bf = [tile([P, T, 4], BF16, f"x_bf{a}") for a in range(PASSES)]
         x_codes = [tile([P, T], U32, f"x_codes{a}") for a in range(PASSES)]
         x_scales = [tile([P, T], U8, f"x_scales{a}") for a in range(PASSES)]
-        w1_first = tile([P, G * H], U32, "w1_first")
-        w1 = [
-            [w1_first[:, H * r : H * (r + 1)] for r in range(G)],
-            [tile([P, H], U32, f"w1_second{r}")[:] for r in range(G)],
-        ]
-        acc = {(r, c): ps.tile([P, H], F32, name=f"bank{2 * r + c}") for r in range(G) for c in range(TOKEN_TILES)}
+        acc = {(r, c): bank([P, H], 2 * r + c) for r in range(G) for c in range(TOKEN_TILES)}
         act = {(r, c): tile([P, 2, P, 2], F32, f"act{r}{c}") for r in range(G) for c in range(TOKEN_TILES)}
         h_bf = {(r, c): tile([P, H], BF16, f"h_bf{r}{c}") for r in range(G) for c in range(TOKEN_TILES)}
         hT = [tile([P, T, 4], BF16, f"hT{r}") for r in range(G)]
         h_codes = [tile([P, T], U32, f"h_codes{r}") for r in range(G)]
         h_scales = [tile([P, T], U8, f"h_scales{r}") for r in range(G)]
+        w1 = {}
         turned = {}
         w2 = {}
         y = {}
@@ -113,12 +104,16 @@ def tile_moe_wsel_b_silu_f_kernel(
             nc.vector.tensor_copy(dst, window[:].bitcast(U32).indirect(lst[:, 32 * r : 32 * (r + 1)]))
 
         def round_x(a):
-            nc.scalar.copy(x_bf[a][:], x_raw[a][:].rearrange("p j t -> p t j"))
+            nc.vector.tensor_copy(x_bf[a][:], x_raw[a][:].rearrange("p j t -> p t j"))
 
         def quantize(codes, scales, values):
             nc.vector.quantize_mx(
                 out=codes[:].bitcast(FP8X4), scales=scales[:], in_=values[:].rearrange("p t j -> p (t j)")
             )
+
+        def gather_w1(a, r, buffer):
+            w1[a, r] = tile([P, H], U32, buffer)
+            gather_expert(w1[a, r][:], w1_all[a], list1, r)
 
         def first_product(a, r):
             for c in range(TOKEN_TILES):
@@ -126,7 +121,7 @@ def tile_moe_wsel_b_silu_f_kernel(
                     out=acc[r, c][:],
                     lhsT=x_codes[a][:, P * c : P * (c + 1)].bitcast(FP8X4),
                     lhsT_scale=x_scales[a][:, P * c : P * (c + 1)],
-                    rhs=w1[a][r].bitcast(FP8X4),
+                    rhs=w1[a, r][:].bitcast(FP8X4),
                     rhs_scale=s1[:, a, H * r : H * (r + 1)],
                     start=(a == 0),
                     stop=(a == PASSES - 1),
@@ -136,28 +131,23 @@ def tile_moe_wsel_b_silu_f_kernel(
             nc.scalar.activation(act[r, c][:], acc[r, c][:].rearrange("t (p u e) -> t u p e", u=2, e=2), SILU)
 
         def weigh_and_turn(r, c):
-            gate_col = gate_cols[:, TOKEN_TILES * r + c : TOKEN_TILES * r + c + 1]
             values = act[r, c][:].rearrange("t u p e -> t (u p e)")
-            if (r, c) == GATED_ON_SCALAR:
-                nc.scalar.activation(h_bf[r, c][:], values, COPY, scale=gate_col)
-            else:
-                nc.vector.tensor_scalar(h_bf[r, c][:], values, gate_col, None, MULT)
-            if c == 0:
-                turned[r] = ps.tile([P, 2, T], F32, name=f"bank{6 + r % 2}")
+            nc.vector.tensor_scalar(h_bf[r, c][:], values, gate_cols[:, r, c : c + 1], None, MULT)
+            turned[r, c] = bank([P, 2, P], 2 * r + c)
             pairs = h_bf[r, c][:].bitcast(F32)
             for u in range(2):
-                nc.tensor.transpose(turned[r][:, u, P * c : P * (c + 1)], pairs[:, P * u : P * (u + 1)], ident[:])
+                nc.tensor.transpose(turned[r, c][:, u, :], pairs[:, P * u : P * (u + 1)], ident[:])
 
-        def take_out(r):
-            nc.scalar.copy(hT[r][:].bitcast(F32), turned[r][:].rearrange("p u t -> p t u"))
+        def take_out(r, c):
+            nc.scalar.copy(hT[r][:, P * c : P * (c + 1), :].bitcast(F32), turned[r, c][:].rearrange("p u t -> p t u"))
 
-        def second_product(r, buffer):
-            w2[r] = tile([P, N], U32, buffer)
+        def second_product(r):
+            w2[r] = tile([P, N], U32, f"w2_{r}")
             gather_expert(w2[r][:], w2_all, list2, r)
             quantize(h_codes[r], h_scales[r], hT[r])
             for m in range(OUT_TILES):
                 if r == 0:
-                    y[m] = ps.tile([P, T], F32, name=f"bank{m}")
+                    y[m] = bank([P, T], (6 + m) % 8)
                 nc.tensor.matmul_mx(
                     out=y[m][:],
                     lhsT=w2[r][:, P * m : P * (m + 1)].bitcast(FP8X4),
@@ -172,51 +162,54 @@ def tile_moe_wsel_b_silu_f_kernel(
         nc.vector.tensor_copy(s1_rows[:], s1_all[:].indirect(list1[:]))
         s1 = tile([P, PASSES, G * H], U8, "s1")
         for q in QUADRANTS_BY_PORT:
-            nc.sync.dma_start(
+            nc.scalar.dma_start(
                 s1[32 * q : 32 * q + 4, :, :].bitcast(I32),
                 s1_rows[W1_ROWS_AT + 8 * q : W1_ROWS_AT + 8 * (q + 1), :].bitcast(I32),
             )
-
-        w1_all.append(tile([P, COLS], I32, "s1_all"))
-        nc.sync.dma_start(w1_all[1][:], words_of(w1_words, 1))
         round_x(0)
-        w2_all = shared.tile([P, COLS], I32, name="w2_all", offset=0, align_bytes=64)
-        nc.sync.dma_start(w2_all[:], words_of(w2_words, 0))
 
-        nc.vector.tensor_copy(w1_first[:], w1_all[0][:].bitcast(U32).indirect(list1[:]))
-        quantize(x_codes[0], x_scales[0], x_bf[0])
+        gate_ps = bank([P, G, P], 6)
         for r in range(G):
-            first_product(0, r)
-        round_x(1)
+            nc.tensor.transpose(gate_ps[:, r, :], gate_rows[:, r, :], ident[:])
+        gate_cols = tile([P, G, TOKEN_TILES], F32, "gate_cols")
+        nc.vector.tensor_copy(gate_cols[:], gate_ps[:, :, 0:TOKEN_TILES])
+        quantize(x_codes[0], x_scales[0], x_bf[0])
 
-        s2_rows = shared.tile([P, G * N], U8, name="s2_rows", offset=4 * COLS, align_bytes=64)
+        s2_rows = tile([P, G * N], U8, "s2_rows")
         nc.vector.tensor_copy(s2_rows[:], s2_all[:].indirect(list2[:]))
-        quantize(x_codes[1], x_scales[1], x_bf[1])
         s2 = tile([P, G * N], U8, "s2")
         for q in QUADRANTS_BY_PORT:
-            nc.sync.dma_start(
+            nc.gpsimd.dma_start(
                 s2[32 * q + W2_PLANE : 32 * q + W2_PLANE + 4, :].bitcast(I32),
                 s2_rows[32 * q : 32 * (q + 1) : W2_ROW_STEP, :].bitcast(I32),
             )
 
+        for r in range(LAST):
+            gather_w1(0, r, f"w1_0{r}")
+            first_product(0, r)
+        round_x(1)
+        gather_w1(0, LAST, "x_raw1")
+        quantize(x_codes[1], x_scales[1], x_bf[1])
+        first_product(0, LAST)
+
         for r in range(G):
-            gather_expert(w1[1][r], w1_all[1], list1, r)
+            gather_w1(1, r, f"w1_1{r}")
             first_product(1, r)
 
         for r in range(LAST):
             for c in range(TOKEN_TILES):
                 activate(r, c)
                 weigh_and_turn(r, c)
-        activate(LAST, 0)
-        take_out(0)
-        activate(LAST, 1)
-        second_product(0, "act11")
         for c in range(TOKEN_TILES):
+            take_out(0, c)
+        for c in range(TOKEN_TILES):
+            activate(LAST, c)
             weigh_and_turn(LAST, c)
         for r in range(1, G):
-            take_out(r)
-        second_product(1, "act21")
-        second_product(2, "hT1")
+            for c in range(TOKEN_TILES):
+                take_out(r, c)
+        for r in range(G):
+            second_product(r)
 
         for m in range(OUT_TILES):
             res = tile([P, T], F32, f"res{m}")

@@ -26,7 +26,8 @@ OUT_TILES = N // P
 COLS = E * H
 LAST = G - 1
 W1_ROWS_AT = 96
-W2_ROW_STEP = 8
+W2_ROWS_AT = 112
+GATE_ROWS_AT = P - TOKEN_TILES
 W2_PLANE = 8
 QUADRANTS_BY_PORT = (0, 2, 1, 3)
 
@@ -37,6 +38,7 @@ def tile_moe_wsel_b_silu_f_kernel(
     nc = tc.nc
     with ExitStack() as ctx:
         sb = ctx.enter_context(tc.tile_pool(name="sb", bufs=1))
+        shared = ctx.enter_context(tc.tile_pool(name="shared", bufs=1))
         ps = ctx.enter_context(tc.psum_pool(name="ps", bufs=1))
 
         def tile(shape, dtype, buffer):
@@ -47,7 +49,7 @@ def tile_moe_wsel_b_silu_f_kernel(
 
         list1 = tile([P, G * H // 16], U16, "list1")
         list2 = tile([P, G * N // 16], U16, "list2")
-        s1_all = tile([P, COLS], U8, "s1_all")
+        s1_all = shared.tile([P, COLS], U8, name="s1_all", offset=16 * T - COLS // 2, align_bytes=64)
         s2_all = tile([P, COLS], U8, "s2_all")
         gate_rows = tile([P, G, P], F32, "gate_rows")
         ident = tile([P, P], F32, "ident")
@@ -62,29 +64,25 @@ def tile_moe_wsel_b_silu_f_kernel(
         def rows_of_x(a):
             return xT[512 * a : 512 * (a + 1), :].rearrange("(p j) t -> p j t", j=4)
 
-        nc.vector.memset(s2_all[:].bitcast(I32), 0)
         nc.vector.memset(ones[:], 1.0)
         nc.vector.memset(s1_all[0:W1_ROWS_AT, :].bitcast(I32), 0)
         nc.vector.tensor_tensor_scan(column[:], ones[:], ones[:], 0.0, MULT, ADD)
-        nc.gpsimd.memset(gate_rows[:], 0.0)
         for q in range(4):
             nc.gpsimd.memset(quadrant[32 * q : 32 * (q + 1), :], 32.0 * q)
+        nc.gpsimd.memset(s2_all[0:W2_ROWS_AT, :].bitcast(I32), 0)
+        nc.gpsimd.memset(gate_rows[0:GATE_ROWS_AT, :, :], 0.0)
         nc.vector.transpose(row[:], column[:, 0:32])
         nc.vector.tensor_scalar(ident[:], column[:], row[:, 0:1], quadrant[:], SUBTRACT, IS_EQUAL)
 
-        x_raw = [tile([P, 4, T], F32, f"x_raw{a}") for a in range(PASSES)]
-        w1_all = [tile([P, COLS], I32, f"w1_all{a}") for a in range(PASSES)]
-        w2_all = tile([P, COLS], I32, "w2_all")
+        x_raw = [tile([P, 4, T], F32, "x_raw0")]
+        w1_all = [tile([P, COLS], I32, "w1_all0")]
         nc.sync.dma_start(list1[:], offs)
         nc.sync.dma_start(s1_all[W1_ROWS_AT:P, :].bitcast(I32), w1_scales.rearrange("a b n -> b a n").bitcast(I32))
-        nc.sync.dma_start(x_raw[0][:], rows_of_x(0))
         nc.sync.dma_start(list2[:], offs2)
+        nc.sync.dma_start(s2_all[W2_ROWS_AT:P, :].bitcast(I32), w2_scales[0].bitcast(I32))
+        nc.sync.dma_start(gate_rows[GATE_ROWS_AT:P, :, :], gate[:, 0, :].rearrange("r (c t) -> c r t", t=P))
+        nc.sync.dma_start(x_raw[0][:], rows_of_x(0))
         nc.sync.dma_start(w1_all[0][:], words_of(w1_words, 0))
-        nc.sync.dma_start(x_raw[1][:], rows_of_x(1))
-        nc.sync.dma_start(w1_all[1][:], words_of(w1_words, 1))
-        nc.sync.dma_start(w2_all[:], words_of(w2_words, 0))
-        nc.scalar.dma_start(s2_all[0:P:W2_ROW_STEP, :].bitcast(I32), w2_scales[0].bitcast(I32))
-        nc.scalar.dma_start(gate_rows[0:TOKEN_TILES, :, :], gate[:, 0, :].rearrange("r (c t) -> c r t", t=P))
 
         x_bf = [tile([P, T, 4], BF16, f"x_bf{a}") for a in range(PASSES)]
         x_codes = [tile([P, T], U32, f"x_codes{a}") for a in range(PASSES)]
@@ -92,9 +90,9 @@ def tile_moe_wsel_b_silu_f_kernel(
         acc = {(r, c): bank([P, H], 2 * r + c) for r in range(G) for c in range(TOKEN_TILES)}
         act = {(r, c): tile([P, 2, P, 2], F32, f"act{r}{c}") for r in range(G) for c in range(TOKEN_TILES)}
         h_bf = {(r, c): tile([P, H], BF16, f"h_bf{r}{c}") for r in range(G) for c in range(TOKEN_TILES)}
-        hT = [tile([P, T, 4], BF16, f"hT{r}") for r in range(G)]
-        h_codes = [tile([P, T], U32, f"h_codes{r}") for r in range(G)]
-        h_scales = [tile([P, T], U8, f"h_scales{r}") for r in range(G)]
+        hT = {(r, c): tile([P, P, 4], BF16, f"hT{r}{c}") for r in range(G) for c in range(TOKEN_TILES)}
+        h_codes = {(r, c): tile([P, P], U32, f"h_codes{r}{c}") for r in range(G) for c in range(TOKEN_TILES)}
+        h_scales = {(r, c): tile([P, P], U8, f"h_scales{r}{c}") for r in range(G) for c in range(TOKEN_TILES)}
         w1 = {}
         turned = {}
         w2 = {}
@@ -111,8 +109,8 @@ def tile_moe_wsel_b_silu_f_kernel(
                 out=codes[:].bitcast(FP8X4), scales=scales[:], in_=values[:].rearrange("p t j -> p (t j)")
             )
 
-        def gather_w1(a, r, buffer):
-            w1[a, r] = tile([P, H], U32, buffer)
+        def gather_w1(a, r, dst):
+            w1[a, r] = dst
             gather_expert(w1[a, r][:], w1_all[a], list1, r)
 
         def first_product(a, r):
@@ -139,82 +137,93 @@ def tile_moe_wsel_b_silu_f_kernel(
                 nc.tensor.transpose(turned[r, c][:, u, :], pairs[:, P * u : P * (u + 1)], ident[:])
 
         def take_out(r, c):
-            nc.scalar.copy(hT[r][:, P * c : P * (c + 1), :].bitcast(F32), turned[r, c][:].rearrange("p u t -> p t u"))
+            nc.scalar.copy(hT[r, c][:].bitcast(F32), turned[r, c][:].rearrange("p u t -> p t u"))
 
-        def second_product(r):
+        def gather_w2(r):
             w2[r] = tile([P, N], U32, f"w2_{r}")
             gather_expert(w2[r][:], w2_all, list2, r)
-            quantize(h_codes[r], h_scales[r], hT[r])
+
+        def second_product(r, c):
+            quantize(h_codes[r, c], h_scales[r, c], hT[r, c])
+            per_bank = OUT_TILES // (c + 1)
             for m in range(OUT_TILES):
-                if r == 0:
-                    y[m] = bank([P, T], (6 + m) % 8)
+                b, slot = divmod(m, per_bank)
+                if r == 0 and slot == 0:
+                    y[c, b] = bank([P, per_bank, P], (6 + c + b) % 8)
                 nc.tensor.matmul_mx(
-                    out=y[m][:],
+                    out=y[c, b][:, slot, :],
                     lhsT=w2[r][:, P * m : P * (m + 1)].bitcast(FP8X4),
                     lhsT_scale=s2[W2_PLANE:P, N * r + P * m : N * r + P * (m + 1)],
-                    rhs=h_codes[r][:].bitcast(FP8X4),
-                    rhs_scale=h_scales[r][:],
-                    start=(r == 0),
-                    stop=(r == LAST),
+                    rhs=h_codes[r, c][:].bitcast(FP8X4),
+                    rhs_scale=h_scales[r, c][:],
+                    start=(r == 0 and slot == 0),
+                    stop=(r == LAST and slot == per_bank - 1),
                 )
+
+        def store(c, b, copy):
+            per_bank = OUT_TILES // (c + 1)
+            res = tile([P, per_bank, P], F32, f"res{c}{b}")
+            copy(res[:], y[c, b][:])
+            rows = out[P * per_bank * b : P * per_bank * (b + 1), P * c : P * (c + 1)]
+            nc.sync.dma_start(rows.rearrange("(m p) t -> p m t", p=P), res[:])
 
         s1_rows = tile([P, G * H], U8, "s1_rows")
         nc.vector.tensor_copy(s1_rows[:], s1_all[:].indirect(list1[:]))
         s1 = tile([P, PASSES, G * H], U8, "s1")
         for q in QUADRANTS_BY_PORT:
-            nc.scalar.dma_start(
+            nc.sync.dma_start(
                 s1[32 * q : 32 * q + 4, :, :].bitcast(I32),
                 s1_rows[W1_ROWS_AT + 8 * q : W1_ROWS_AT + 8 * (q + 1), :].bitcast(I32),
             )
+        x_raw.append(shared.tile([P, 4, T], F32, name="x_raw1", offset=0, align_bytes=64))
+        w1_all.append(shared.tile([P, COLS], I32, name="w1_all1", offset=16 * T, align_bytes=64))
+        nc.sync.dma_start(x_raw[1][:], rows_of_x(1))
+        nc.sync.dma_start(w1_all[1][:], words_of(w1_words, 1))
         round_x(0)
 
         gate_ps = bank([P, G, P], 6)
         for r in range(G):
             nc.tensor.transpose(gate_ps[:, r, :], gate_rows[:, r, :], ident[:])
         gate_cols = tile([P, G, TOKEN_TILES], F32, "gate_cols")
-        nc.vector.tensor_copy(gate_cols[:], gate_ps[:, :, 0:TOKEN_TILES])
+        nc.vector.tensor_copy(gate_cols[:], gate_ps[:, :, GATE_ROWS_AT:P])
         quantize(x_codes[0], x_scales[0], x_bf[0])
 
         s2_rows = tile([P, G * N], U8, "s2_rows")
         nc.vector.tensor_copy(s2_rows[:], s2_all[:].indirect(list2[:]))
-        s2 = tile([P, G * N], U8, "s2")
-        for q in QUADRANTS_BY_PORT:
-            nc.gpsimd.dma_start(
-                s2[32 * q + W2_PLANE : 32 * q + W2_PLANE + 4, :].bitcast(I32),
-                s2_rows[32 * q : 32 * (q + 1) : W2_ROW_STEP, :].bitcast(I32),
-            )
+        w2_all = tile([P, COLS], I32, "s1_rows")
+        nc.sync.dma_start(w2_all[:], words_of(w2_words, 0))
 
         for r in range(LAST):
-            gather_w1(0, r, f"w1_0{r}")
+            gather_w1(0, r, tile([P, H], U32, f"w1_0{r}"))
             first_product(0, r)
         round_x(1)
-        gather_w1(0, LAST, "x_raw1")
+        gather_w1(0, LAST, shared.tile([P, H], U32, name="w1_0last", offset=0, align_bytes=64))
         quantize(x_codes[1], x_scales[1], x_bf[1])
         first_product(0, LAST)
+        s2 = tile([P, G * N], U8, "w1_all0")
+        for q in QUADRANTS_BY_PORT:
+            nc.sync.dma_start(
+                s2[32 * q + W2_PLANE : 32 * q + W2_PLANE + 4, :].bitcast(I32),
+                s2_rows[W2_ROWS_AT + 4 * q : W2_ROWS_AT + 4 * (q + 1), :].bitcast(I32),
+            )
+
 
         for r in range(G):
-            gather_w1(1, r, f"w1_1{r}")
+            gather_w1(1, r, tile([P, H], U32, f"w1_1{r}"))
             first_product(1, r)
 
-        for r in range(LAST):
-            for c in range(TOKEN_TILES):
+        for c in range(TOKEN_TILES):
+            for r in range(G):
                 activate(r, c)
                 weigh_and_turn(r, c)
         for c in range(TOKEN_TILES):
-            take_out(0, c)
-        for c in range(TOKEN_TILES):
-            activate(LAST, c)
-            weigh_and_turn(LAST, c)
-        for r in range(1, G):
-            for c in range(TOKEN_TILES):
+            for r in range(G):
                 take_out(r, c)
-        for r in range(G):
-            second_product(r)
-
-        for m in range(OUT_TILES):
-            res = tile([P, T], F32, f"res{m}")
-            if m % 2 == 0:
-                nc.scalar.copy(res[:], y[m][:])
-            else:
-                nc.vector.tensor_copy(res[:], y[m][:])
-            nc.sync.dma_start(out[P * m : P * (m + 1), :], res[:])
+        for c in range(TOKEN_TILES):
+            for r in range(G):
+                if c == 0:
+                    gather_w2(r)
+                second_product(r, c)
+        store(0, 0, nc.scalar.copy)
+        store(1, 0, nc.scalar.copy)
+        store(1, 1, nc.vector.tensor_copy)

@@ -29,7 +29,6 @@ W1_ROWS_AT = 96
 W2_ROWS_AT = 112
 GATE_ROWS_AT = P - TOKEN_TILES
 W2_PLANE = 8
-QUADRANTS_BY_PORT = (0, 2, 1, 3)
 
 
 def tile_moe_wsel_b_silu_f_kernel(
@@ -74,20 +73,20 @@ def tile_moe_wsel_b_silu_f_kernel(
         nc.vector.transpose(row[:], column[:, 0:32])
         nc.vector.tensor_scalar(ident[:], column[:], row[:, 0:1], quadrant[:], SUBTRACT, IS_EQUAL)
 
-        x_raw = [tile([P, 4, T], F32, "x_raw0")]
+        x_raw = {1: tile([P, 4, T], F32, "x_raw1")}
         w1_all = [tile([P, COLS], I32, "w1_all0")]
         nc.sync.dma_start(list1[:], offs)
         nc.sync.dma_start(s1_all[W1_ROWS_AT:P, :].bitcast(I32), w1_scales.rearrange("a b n -> b a n").bitcast(I32))
         nc.sync.dma_start(list2[:], offs2)
         nc.sync.dma_start(s2_all[W2_ROWS_AT:P, :].bitcast(I32), w2_scales[0].bitcast(I32))
         nc.sync.dma_start(gate_rows[GATE_ROWS_AT:P, :, :], gate[:, 0, :].rearrange("r (c t) -> c r t", t=P))
-        nc.sync.dma_start(x_raw[0][:], rows_of_x(0))
+        nc.sync.dma_start(x_raw[1][:], rows_of_x(1))
         nc.sync.dma_start(w1_all[0][:], words_of(w1_words, 0))
 
         x_bf = [tile([P, T, 4], BF16, f"x_bf{a}") for a in range(PASSES)]
         x_codes = [tile([P, T], U32, f"x_codes{a}") for a in range(PASSES)]
         x_scales = [tile([P, T], U8, f"x_scales{a}") for a in range(PASSES)]
-        acc = {(r, c): bank([P, H], 2 * r + c) for r in range(G) for c in range(TOKEN_TILES)}
+        acc = {}
         act = {(r, c): tile([P, 2, P, 2], F32, f"act{r}{c}") for r in range(G) for c in range(TOKEN_TILES)}
         h_bf = {(r, c): tile([P, H], BF16, f"h_bf{r}{c}") for r in range(G) for c in range(TOKEN_TILES)}
         hT = {(r, c): tile([P, P, 4], BF16, f"hT{r}{c}") for r in range(G) for c in range(TOKEN_TILES)}
@@ -113,17 +112,18 @@ def tile_moe_wsel_b_silu_f_kernel(
             w1[a, r] = dst
             gather_expert(w1[a, r][:], w1_all[a], list1, r)
 
-        def first_product(a, r):
-            for c in range(TOKEN_TILES):
-                nc.tensor.matmul_mx(
-                    out=acc[r, c][:],
-                    lhsT=x_codes[a][:, P * c : P * (c + 1)].bitcast(FP8X4),
-                    lhsT_scale=x_scales[a][:, P * c : P * (c + 1)],
-                    rhs=w1[a, r][:].bitcast(FP8X4),
-                    rhs_scale=s1[:, a, H * r : H * (r + 1)],
-                    start=(a == 0),
-                    stop=(a == PASSES - 1),
-                )
+        def first_product(a, r, c):
+            if a == 0:
+                acc[r, c] = bank([P, H], r)
+            nc.tensor.matmul_mx(
+                out=acc[r, c][:],
+                lhsT=x_codes[a][:, P * c : P * (c + 1)].bitcast(FP8X4),
+                lhsT_scale=x_scales[a][:, P * c : P * (c + 1)],
+                rhs=w1[a, r][:].bitcast(FP8X4),
+                rhs_scale=s1[4 * a : P, H * r : H * (r + 1)],
+                start=(a == 0),
+                stop=(a == PASSES - 1),
+            )
 
         def activate(r, c):
             nc.scalar.activation(act[r, c][:], acc[r, c][:].rearrange("t (p u e) -> t u p e", u=2, e=2), SILU)
@@ -131,7 +131,7 @@ def tile_moe_wsel_b_silu_f_kernel(
         def weigh_and_turn(r, c):
             values = act[r, c][:].rearrange("t u p e -> t (u p e)")
             nc.vector.tensor_scalar(h_bf[r, c][:], values, gate_cols[:, r, c : c + 1], None, MULT)
-            turned[r, c] = bank([P, 2, P], 2 * r + c)
+            turned[r, c] = bank([P, 2, P], r + G * (1 - c))
             pairs = h_bf[r, c][:].bitcast(F32)
             for u in range(2):
                 nc.tensor.transpose(turned[r, c][:, u, :], pairs[:, P * u : P * (u + 1)], ident[:])
@@ -149,7 +149,7 @@ def tile_moe_wsel_b_silu_f_kernel(
             for m in range(OUT_TILES):
                 b, slot = divmod(m, per_bank)
                 if r == 0 and slot == 0:
-                    y[c, b] = bank([P, per_bank, P], (6 + c + b) % 8)
+                    y[c, b] = bank([P, per_bank, P], (6, 7, G)[c + b])
                 nc.tensor.matmul_mx(
                     out=y[c, b][:, slot, :],
                     lhsT=w2[r][:, P * m : P * (m + 1)].bitcast(FP8X4),
@@ -169,53 +169,60 @@ def tile_moe_wsel_b_silu_f_kernel(
 
         s1_rows = tile([P, G * H], U8, "s1_rows")
         nc.vector.tensor_copy(s1_rows[:], s1_all[:].indirect(list1[:]))
-        s1 = tile([P, PASSES, G * H], U8, "s1")
-        for q in QUADRANTS_BY_PORT:
-            nc.sync.dma_start(
-                s1[32 * q : 32 * q + 4, :, :].bitcast(I32),
-                s1_rows[W1_ROWS_AT + 8 * q : W1_ROWS_AT + 8 * (q + 1), :].bitcast(I32),
-            )
-        x_raw.append(shared.tile([P, 4, T], F32, name="x_raw1", offset=0, align_bytes=64))
+        s1 = tile([P, G * H], U8, "s1")
+
+        def move_w1_rows(j):
+            for a in range(PASSES):
+                nc.sync.dma_start(
+                    s1[4 * a + j : P : 32, :].bitcast(I32),
+                    s1_rows[W1_ROWS_AT + 2 * j + a : P : 8, :].bitcast(I32),
+                )
+
+        x_raw[0] = shared.tile([P, 4, T], F32, name="x_raw0", offset=0, align_bytes=64)
         w1_all.append(shared.tile([P, COLS], I32, name="w1_all1", offset=16 * T, align_bytes=64))
-        nc.sync.dma_start(x_raw[1][:], rows_of_x(1))
+        for j in range(2):
+            move_w1_rows(j)
+        nc.sync.dma_start(x_raw[0][:], rows_of_x(0))
+        for j in range(2, 4):
+            move_w1_rows(j)
         nc.sync.dma_start(w1_all[1][:], words_of(w1_words, 1))
-        round_x(0)
+        round_x(1)
 
         gate_ps = bank([P, G, P], 6)
         for r in range(G):
             nc.tensor.transpose(gate_ps[:, r, :], gate_rows[:, r, :], ident[:])
         gate_cols = tile([P, G, TOKEN_TILES], F32, "gate_cols")
         nc.vector.tensor_copy(gate_cols[:], gate_ps[:, :, GATE_ROWS_AT:P])
-        quantize(x_codes[0], x_scales[0], x_bf[0])
+        quantize(x_codes[1], x_scales[1], x_bf[1])
 
         s2_rows = tile([P, G * N], U8, "s2_rows")
         nc.vector.tensor_copy(s2_rows[:], s2_all[:].indirect(list2[:]))
         w2_all = tile([P, COLS], I32, "s1_rows")
         nc.sync.dma_start(w2_all[:], words_of(w2_words, 0))
 
-        for r in range(LAST):
+        for r in range(G):
             gather_w1(0, r, tile([P, H], U32, f"w1_0{r}"))
-            first_product(0, r)
-        round_x(1)
-        gather_w1(0, LAST, shared.tile([P, H], U32, name="w1_0last", offset=0, align_bytes=64))
-        quantize(x_codes[1], x_scales[1], x_bf[1])
-        first_product(0, LAST)
+        round_x(0)
+        quantize(x_codes[0], x_scales[0], x_bf[0])
+        for r in range(G):
+            first_product(0, r, 0)
         s2 = tile([P, G * N], U8, "w1_all0")
-        for q in QUADRANTS_BY_PORT:
+        for j in range(4):
             nc.sync.dma_start(
-                s2[32 * q + W2_PLANE : 32 * q + W2_PLANE + 4, :].bitcast(I32),
-                s2_rows[W2_ROWS_AT + 4 * q : W2_ROWS_AT + 4 * (q + 1), :].bitcast(I32),
+                s2[W2_PLANE + j : P : 32, :].bitcast(I32), s2_rows[W2_ROWS_AT + j : P : 4, :].bitcast(I32)
             )
-
 
         for r in range(G):
             gather_w1(1, r, tile([P, H], U32, f"w1_1{r}"))
-            first_product(1, r)
-
-        for c in range(TOKEN_TILES):
-            for r in range(G):
-                activate(r, c)
-                weigh_and_turn(r, c)
+            first_product(1, r, 0)
+        for r in range(G):
+            activate(r, 0)
+            for a in range(PASSES):
+                first_product(a, r, 1)
+            weigh_and_turn(r, 0)
+        for r in range(G):
+            activate(r, 1)
+            weigh_and_turn(r, 1)
         for c in range(TOKEN_TILES):
             for r in range(G):
                 take_out(r, c)

@@ -120,7 +120,7 @@ def tile_moe_wsel_b_silu_f_kernel(
                 lhsT=x_codes[a][:, P * c : P * (c + 1)].bitcast(FP8X4),
                 lhsT_scale=x_scales[a][:, P * c : P * (c + 1)],
                 rhs=w1[a, r][:].bitcast(FP8X4),
-                rhs_scale=s1[4 * a : P, H * r : H * (r + 1)],
+                rhs_scale=s1[a][4 * a : P, H * r : H * (r + 1)],
                 start=(a == 0),
                 stop=(a == PASSES - 1),
             )
@@ -128,10 +128,12 @@ def tile_moe_wsel_b_silu_f_kernel(
         def activate(r, c):
             nc.scalar.activation(act[r, c][:], acc[r, c][:].rearrange("t (p u e) -> t u p e", u=2, e=2), SILU)
 
-        def weigh_and_turn(r, c):
+        def weigh(r, c):
             values = act[r, c][:].rearrange("t u p e -> t (u p e)")
             nc.vector.tensor_scalar(h_bf[r, c][:], values, gate_cols[:, r, c : c + 1], None, MULT)
-            turned[r, c] = bank([P, 2, P], r + G * (1 - c))
+
+        def turn(r, c):
+            turned[r, c] = bank([P, 2, P], r + G * c)
             pairs = h_bf[r, c][:].bitcast(F32)
             for u in range(2):
                 nc.tensor.transpose(turned[r, c][:, u, :], pairs[:, P * u : P * (u + 1)], ident[:])
@@ -169,23 +171,21 @@ def tile_moe_wsel_b_silu_f_kernel(
 
         s1_rows = tile([P, G * H], U8, "s1_rows")
         nc.vector.tensor_copy(s1_rows[:], s1_all[:].indirect(list1[:]))
-        s1 = tile([P, G * H], U8, "s1")
+        s1 = [tile([P, G * H], U8, f"s1_{a}") for a in range(PASSES)]
 
-        def move_w1_rows(j):
-            for a in range(PASSES):
+        def move_w1_rows(a):
+            for j in range(4):
                 nc.sync.dma_start(
-                    s1[4 * a + j : P : 32, :].bitcast(I32),
+                    s1[a][4 * a + j : P : 32, :].bitcast(I32),
                     s1_rows[W1_ROWS_AT + 2 * j + a : P : 8, :].bitcast(I32),
                 )
 
         x_raw[0] = shared.tile([P, 4, T], F32, name="x_raw0", offset=0, align_bytes=64)
         w1_all.append(shared.tile([P, COLS], I32, name="w1_all1", offset=16 * T, align_bytes=64))
-        for j in range(2):
-            move_w1_rows(j)
+        move_w1_rows(0)
         nc.sync.dma_start(x_raw[0][:], rows_of_x(0))
-        for j in range(2, 4):
-            move_w1_rows(j)
         nc.sync.dma_start(w1_all[1][:], words_of(w1_words, 1))
+        move_w1_rows(1)
         round_x(1)
 
         gate_ps = bank([P, G, P], 6)
@@ -197,7 +197,7 @@ def tile_moe_wsel_b_silu_f_kernel(
 
         s2_rows = tile([P, G * N], U8, "s2_rows")
         nc.vector.tensor_copy(s2_rows[:], s2_all[:].indirect(list2[:]))
-        w2_all = tile([P, COLS], I32, "s1_rows")
+        w2_all = tile([P, COLS], I32, "s2_all")
         nc.sync.dma_start(w2_all[:], words_of(w2_words, 0))
 
         for r in range(G):
@@ -219,10 +219,12 @@ def tile_moe_wsel_b_silu_f_kernel(
             activate(r, 0)
             for a in range(PASSES):
                 first_product(a, r, 1)
-            weigh_and_turn(r, 0)
+            weigh(r, 0)
         for r in range(G):
             activate(r, 1)
-            weigh_and_turn(r, 1)
+            turn(r, 0)
+            weigh(r, 1)
+            turn(r, 1)
         for c in range(TOKEN_TILES):
             for r in range(G):
                 take_out(r, c)

@@ -125,6 +125,19 @@ def tile_moe_wsel_b_silu_f_kernel(
                 stop=(a == PASSES - 1),
             )
 
+        def keep_clock(r):
+            spare = bank([P, H], r)
+            for a in range(PASSES):
+                nc.tensor.matmul_mx(
+                    out=spare[:],
+                    lhsT=x_codes[a][:, 0:P].bitcast(FP8X4),
+                    lhsT_scale=x_scales[a][:, 0:P],
+                    rhs=w1[a, r][:].bitcast(FP8X4),
+                    rhs_scale=s1[a][4 * a : P, H * r : H * (r + 1)],
+                    start=(a == 0),
+                    stop=(a == PASSES - 1),
+                )
+
         def activate(r, c):
             nc.scalar.activation(act[r, c][:], acc[r, c][:].rearrange("t (p u e) -> t u p e", u=2, e=2), SILU)
 
@@ -222,6 +235,8 @@ def tile_moe_wsel_b_silu_f_kernel(
             weigh(r, 0)
         for r in range(G):
             activate(r, 1)
+            if r == 1:
+                keep_clock(r)
             turn(r, 0)
             weigh(r, 1)
             turn(r, 1)

@@ -146,7 +146,7 @@ def tile_moe_wsel_b_silu_f_kernel(
             nc.vector.tensor_scalar(h_bf[r, c][:], values, gate_cols[:, r, c : c + 1], None, MULT)
 
         def turn(r, c):
-            turned[r, c] = bank([P, 2, P], r + G * c)
+            turned[r, c] = bank([P, 2, P], 7 if (r, c) == (LAST, 0) else r + G * c)
             pairs = h_bf[r, c][:].bitcast(F32)
             for u in range(2):
                 nc.tensor.transpose(turned[r, c][:, u, :], pairs[:, P * u : P * (u + 1)], ident[:])
@@ -164,7 +164,7 @@ def tile_moe_wsel_b_silu_f_kernel(
             for m in range(OUT_TILES):
                 b, slot = divmod(m, per_bank)
                 if r == 0 and slot == 0:
-                    y[c, b] = bank([P, per_bank, P], (6, 7, G)[c + b])
+                    y[c, b] = bank([P, per_bank, P], (6, LAST, G)[c + b])
                 nc.tensor.matmul_mx(
                     out=y[c, b][:, slot, :],
                     lhsT=w2[r][:, P * m : P * (m + 1)].bitcast(FP8X4),
@@ -235,7 +235,7 @@ def tile_moe_wsel_b_silu_f_kernel(
             weigh(r, 0)
         for r in range(G):
             activate(r, 1)
-            if r == 1:
+            if r == LAST:
                 keep_clock(r)
             turn(r, 0)
             weigh(r, 1)

@@ -15,9 +15,6 @@ U8 = mybir.dt.uint8
 FP8X4 = mybir.dt.float8_e4m3fn_x4
 SILU = mybir.ActivationFunctionType.Silu
 MULT = mybir.AluOpType.mult
-ADD = mybir.AluOpType.add
-SUBTRACT = mybir.AluOpType.subtract
-IS_EQUAL = mybir.AluOpType.is_equal
 
 P = 128
 PASSES = K // 512
@@ -26,9 +23,10 @@ OUT_TILES = N // P
 COLS = E * H
 LAST = G - 1
 W1_ROWS_AT = 96
-W2_ROWS_AT = 112
-GATE_ROWS_AT = P - TOKEN_TILES
+W2_ROWS_AT = 48
 W2_PLANE = 8
+MOVES_AHEAD = 6
+ACC_BANK = {(0, 0): 0, (1, 0): 1, (2, 0): 2, (0, 1): 3, (1, 1): 1, (2, 1): 3}
 
 
 def tile_moe_wsel_b_silu_f_kernel(
@@ -38,6 +36,7 @@ def tile_moe_wsel_b_silu_f_kernel(
     with ExitStack() as ctx:
         sb = ctx.enter_context(tc.tile_pool(name="sb", bufs=1))
         shared = ctx.enter_context(tc.tile_pool(name="shared", bufs=1))
+        late = ctx.enter_context(tc.tile_pool(name="late", bufs=1))
         ps = ctx.enter_context(tc.psum_pool(name="ps", bufs=1))
 
         def tile(shape, dtype, buffer):
@@ -46,125 +45,87 @@ def tile_moe_wsel_b_silu_f_kernel(
         def bank(shape, number):
             return ps.tile(shape, F32, name=f"bank{number}")
 
-        list1 = tile([P, G * H // 16], U16, "list1")
-        list2 = tile([P, G * N // 16], U16, "list2")
-        s1_all = shared.tile([P, COLS], U8, name="s1_all", offset=16 * T - COLS // 2, align_bytes=64)
-        s2_all = tile([P, COLS], U8, "s2_all")
-        gate_rows = tile([P, G, P], F32, "gate_rows")
-        ident = tile([P, P], F32, "ident")
-        ones = tile([P, P], F32, "ones")
-        column = tile([P, P], F32, "column")
-        row = tile([P, 32], F32, "row")
-        quadrant = tile([P, 1], F32, "quadrant")
-
         def words_of(dram, a):
             return dram[a].rearrange("p n d -> p (n d)").bitcast(I32)
 
         def rows_of_x(a):
             return xT[512 * a : 512 * (a + 1), :].rearrange("(p j) t -> p j t", j=4)
 
-        nc.vector.memset(ones[:], 1.0)
-        nc.vector.memset(s1_all[0:W1_ROWS_AT, :].bitcast(I32), 0)
-        nc.vector.tensor_tensor_scan(column[:], ones[:], ones[:], 0.0, MULT, ADD)
-        for q in range(4):
-            nc.gpsimd.memset(quadrant[32 * q : 32 * (q + 1), :], 32.0 * q)
-        nc.gpsimd.memset(s2_all[0:W2_ROWS_AT, :].bitcast(I32), 0)
-        nc.gpsimd.memset(gate_rows[0:GATE_ROWS_AT, :, :], 0.0)
-        nc.vector.transpose(row[:], column[:, 0:32])
-        nc.vector.tensor_scalar(ident[:], column[:], row[:, 0:1], quadrant[:], SUBTRACT, IS_EQUAL)
-
-        x_raw = {1: tile([P, 4, T], F32, "x_raw1")}
+        list1 = tile([P, G * H // 16], U16, "list1")
+        list2 = tile([P, G * N // 16], U16, "list2")
+        s1_all = tile([P, COLS], U8, "s1_all")
+        s2_all = late.tile([P, COLS], U8, name="s2_all", offset=0, align_bytes=64)
+        x_raw = [tile([P, 4, T], F32, f"x_raw{a}") for a in range(PASSES)]
         w1_all = [tile([P, COLS], I32, "w1_all0")]
+
+        nc.vector.memset(s1_all[0:W1_ROWS_AT, :].bitcast(I32), 0)
+        nc.gpsimd.memset(s2_all[0:W2_ROWS_AT, :].bitcast(I32), 0)
+        nc.gpsimd.memset(s2_all[W2_ROWS_AT + 16 : P, :].bitcast(I32), 0)
+
         nc.sync.dma_start(list1[:], offs)
         nc.sync.dma_start(s1_all[W1_ROWS_AT:P, :].bitcast(I32), w1_scales.rearrange("a b n -> b a n").bitcast(I32))
         nc.sync.dma_start(list2[:], offs2)
-        nc.sync.dma_start(s2_all[W2_ROWS_AT:P, :].bitcast(I32), w2_scales[0].bitcast(I32))
-        nc.sync.dma_start(gate_rows[GATE_ROWS_AT:P, :, :], gate[:, 0, :].rearrange("r (c t) -> c r t", t=P))
-        nc.sync.dma_start(x_raw[1][:], rows_of_x(1))
+        nc.sync.dma_start(s2_all[W2_ROWS_AT : W2_ROWS_AT + 16, :].bitcast(I32), w2_scales[0].bitcast(I32))
+        for a in range(PASSES):
+            nc.sync.dma_start(x_raw[a][:], rows_of_x(a))
         nc.sync.dma_start(w1_all[0][:], words_of(w1_words, 0))
 
         x_bf = [tile([P, T, 4], BF16, f"x_bf{a}") for a in range(PASSES)]
         x_codes = [tile([P, T], U32, f"x_codes{a}") for a in range(PASSES)]
         x_scales = [tile([P, T], U8, f"x_scales{a}") for a in range(PASSES)]
+        units = [(r, c) for c in range(TOKEN_TILES) for r in range(G)]
+        act = {u: tile([P, P, 4], F32, f"act{u[0]}{u[1]}") for u in units}
+        h_bf = {u: tile([P, P, 4], BF16, f"h_bf{u[0]}{u[1]}") for u in units[:4]}
+        for n, u in enumerate(units[4:]):
+            h_bf[u] = late.tile([P, P, 4], BF16, name=f"h_bf{u[0]}{u[1]}", offset=2 * H * n, align_bytes=64)
+        h_codes = {u: tile([P, P], U32, f"h_codes{u[0]}{u[1]}") for u in units}
+        h_scales = {u: tile([P, P], U8, f"h_scales{u[0]}{u[1]}") for u in units}
         acc = {}
-        act = {(r, c): tile([P, 2, P, 2], F32, f"act{r}{c}") for r in range(G) for c in range(TOKEN_TILES)}
-        h_bf = {(r, c): tile([P, H], BF16, f"h_bf{r}{c}") for r in range(G) for c in range(TOKEN_TILES)}
-        hT = {(r, c): tile([P, P, 4], BF16, f"hT{r}{c}") for r in range(G) for c in range(TOKEN_TILES)}
-        h_codes = {(r, c): tile([P, P], U32, f"h_codes{r}{c}") for r in range(G) for c in range(TOKEN_TILES)}
-        h_scales = {(r, c): tile([P, P], U8, f"h_scales{r}{c}") for r in range(G) for c in range(TOKEN_TILES)}
         w1 = {}
-        turned = {}
         w2 = {}
         y = {}
-
-        def gather_expert(dst, window, lst, r):
-            nc.vector.tensor_copy(dst, window[:].bitcast(U32).indirect(lst[:, 32 * r : 32 * (r + 1)]))
-
-        def round_x(a):
-            nc.vector.tensor_copy(x_bf[a][:], x_raw[a][:].rearrange("p j t -> p t j"))
 
         def quantize(codes, scales, values):
             nc.vector.quantize_mx(
                 out=codes[:].bitcast(FP8X4), scales=scales[:], in_=values[:].rearrange("p t j -> p (t j)")
             )
 
-        def gather_w1(a, r, dst):
-            w1[a, r] = dst
-            gather_expert(w1[a, r][:], w1_all[a], list1, r)
-
-        def first_product(a, r, c):
-            if a == 0:
-                acc[r, c] = bank([P, H], r)
-            nc.tensor.matmul_mx(
-                out=acc[r, c][:],
-                lhsT=x_codes[a][:, P * c : P * (c + 1)].bitcast(FP8X4),
-                lhsT_scale=x_scales[a][:, P * c : P * (c + 1)],
-                rhs=w1[a, r][:].bitcast(FP8X4),
-                rhs_scale=s1[a][4 * a : P, H * r : H * (r + 1)],
-                start=(a == 0),
-                stop=(a == PASSES - 1),
-            )
-
-        def keep_clock(r):
-            spare = bank([P, H], r)
-            for a in range(PASSES):
-                nc.tensor.matmul_mx(
-                    out=spare[:],
-                    lhsT=x_codes[a][:, 0:P].bitcast(FP8X4),
-                    lhsT_scale=x_scales[a][:, 0:P],
-                    rhs=w1[a, r][:].bitcast(FP8X4),
-                    rhs_scale=s1[a][4 * a : P, H * r : H * (r + 1)],
-                    start=(a == 0),
-                    stop=(a == PASSES - 1),
-                )
-
-        def activate(r, c):
-            nc.scalar.activation(act[r, c][:], acc[r, c][:].rearrange("t (p u e) -> t u p e", u=2, e=2), SILU)
-
-        def weigh(r, c):
-            values = act[r, c][:].rearrange("t u p e -> t (u p e)")
-            nc.vector.tensor_scalar(h_bf[r, c][:], values, gate_cols[:, r, c : c + 1], None, MULT)
-
-        def turn(r, c):
-            turned[r, c] = bank([P, 2, P], 7 if (r, c) == (LAST, 0) else r + G * c)
-            pairs = h_bf[r, c][:].bitcast(F32)
-            for u in range(2):
-                nc.tensor.transpose(turned[r, c][:, u, :], pairs[:, P * u : P * (u + 1)], ident[:])
-
-        def take_out(r, c):
-            nc.scalar.copy(hT[r, c][:].bitcast(F32), turned[r, c][:].rearrange("p u t -> p t u"))
+        def gather_w1(a, r):
+            w1[a, r] = tile([P, 4, P], U32, f"w1_{a}{r}")
+            window = w1_all[a][:].bitcast(U32).indirect(list1[:, 32 * r : 32 * (r + 1)])
+            nc.vector.tensor_copy(w1[a, r][:].rearrange("p j m -> p m j"), window)
 
         def gather_w2(r):
             w2[r] = tile([P, N], U32, f"w2_{r}")
-            gather_expert(w2[r][:], w2_all, list2, r)
+            nc.vector.tensor_copy(w2[r][:], w2_all[:].bitcast(U32).indirect(list2[:, 32 * r : 32 * (r + 1)]))
+
+        def first_product(a, r, c):
+            if a == 0:
+                acc[r, c] = bank([P, 4, P], ACC_BANK[r, c])
+            for j in range(4):
+                nc.tensor.matmul_mx(
+                    out=acc[r, c][:, j, :],
+                    lhsT=w1[a, r][:, j, :].bitcast(FP8X4),
+                    lhsT_scale=s1[a][4 * a : P, H * r + P * j : H * r + P * (j + 1)],
+                    rhs=x_codes[a][:, P * c : P * (c + 1)].bitcast(FP8X4),
+                    rhs_scale=x_scales[a][:, P * c : P * (c + 1)],
+                    start=(a == 0 and j == 0),
+                    stop=(a == PASSES - 1 and j == 3),
+                )
+
+        def activate(r, c):
+            nc.scalar.activation(act[r, c][:], acc[r, c][:].rearrange("p j t -> p t j"), SILU)
+
+        def weigh(r, c):
+            factor = gates[:, r, P * c : P * (c + 1)].unsqueeze(2).to_broadcast([P, P, 4])
+            nc.vector.tensor_tensor(h_bf[r, c][:], act[r, c][:], factor, MULT)
 
         def second_product(r, c):
-            quantize(h_codes[r, c], h_scales[r, c], hT[r, c])
             per_bank = OUT_TILES // (c + 1)
             for m in range(OUT_TILES):
                 b, slot = divmod(m, per_bank)
                 if r == 0 and slot == 0:
-                    y[c, b] = bank([P, per_bank, P], (6, LAST, G)[c + b])
+                    y[c, b] = bank([P, per_bank, P], G + 1 + c + b)
                 nc.tensor.matmul_mx(
                     out=y[c, b][:, slot, :],
                     lhsT=w2[r][:, P * m : P * (m + 1)].bitcast(FP8X4),
@@ -182,72 +143,87 @@ def tile_moe_wsel_b_silu_f_kernel(
             rows = out[P * per_bank * b : P * per_bank * (b + 1), P * c : P * (c + 1)]
             nc.sync.dma_start(rows.rearrange("(m p) t -> p m t", p=P), res[:])
 
-        s1_rows = tile([P, G * H], U8, "s1_rows")
-        nc.vector.tensor_copy(s1_rows[:], s1_all[:].indirect(list1[:]))
+        gates = shared.tile([P, G, T], F32, name="gates", offset=0, align_bytes=64)
+        s1_rows = shared.tile([P, G, P, 4], U8, name="s1_rows", offset=4 * G * T - G * H // 2, align_bytes=64)
+        w1_all.append(shared.tile([P, COLS], I32, name="w1_all1", offset=4 * G * T, align_bytes=64))
+        s1_turned = tile([P, G, 4, P], U8, "s1_turned")
+
+        def gather_w1_scales(r):
+            picked = s1_all[:].indirect(list1[:, 32 * r : 32 * (r + 1)])
+            nc.vector.tensor_copy(s1_rows[:, r].rearrange("p m j -> p (m j)"), picked)
+
+        def turn_w1_scales(r):
+            nc.vector.tensor_copy(s1_turned[:, r], s1_rows[:, r].rearrange("p m j -> p j m"))
+
+        gather_w1_scales(0)
+        for r in range(1, G):
+            gather_w1_scales(r)
+            turn_w1_scales(r - 1)
+        turn_w1_scales(LAST)
         s1 = [tile([P, G * H], U8, f"s1_{a}") for a in range(PASSES)]
 
-        def move_w1_rows(a):
-            for j in range(4):
-                nc.sync.dma_start(
-                    s1[a][4 * a + j : P : 32, :].bitcast(I32),
-                    s1_rows[W1_ROWS_AT + 2 * j + a : P : 8, :].bitcast(I32),
-                )
-
-        x_raw[0] = shared.tile([P, 4, T], F32, name="x_raw0", offset=0, align_bytes=64)
-        w1_all.append(shared.tile([P, COLS], I32, name="w1_all1", offset=16 * T, align_bytes=64))
-        move_w1_rows(0)
-        nc.sync.dma_start(x_raw[0][:], rows_of_x(0))
-        nc.sync.dma_start(w1_all[1][:], words_of(w1_words, 1))
-        move_w1_rows(1)
-        round_x(1)
-
-        gate_ps = bank([P, G, P], 6)
-        for r in range(G):
-            nc.tensor.transpose(gate_ps[:, r, :], gate_rows[:, r, :], ident[:])
-        gate_cols = tile([P, G, TOKEN_TILES], F32, "gate_cols")
-        nc.vector.tensor_copy(gate_cols[:], gate_ps[:, :, GATE_ROWS_AT:P])
-        quantize(x_codes[1], x_scales[1], x_bf[1])
-
-        s2_rows = tile([P, G * N], U8, "s2_rows")
-        nc.vector.tensor_copy(s2_rows[:], s2_all[:].indirect(list2[:]))
-        w2_all = tile([P, COLS], I32, "s2_all")
-        nc.sync.dma_start(w2_all[:], words_of(w2_words, 0))
-
-        for r in range(G):
-            gather_w1(0, r, tile([P, H], U32, f"w1_0{r}"))
-        round_x(0)
-        quantize(x_codes[0], x_scales[0], x_bf[0])
-        for r in range(G):
-            first_product(0, r, 0)
-        s2 = tile([P, G * N], U8, "w1_all0")
-        for j in range(4):
+        def move_w1_rows(a, j):
             nc.sync.dma_start(
-                s2[W2_PLANE + j : P : 32, :].bitcast(I32), s2_rows[W2_ROWS_AT + j : P : 4, :].bitcast(I32)
+                s1[a][4 * a + j : P : 32, :].bitcast(I32),
+                s1_turned[W1_ROWS_AT + 2 * j + a : P : 8].rearrange("p r j m -> p (r j m)").bitcast(I32),
             )
 
+        moves = [(0, 0), (0, 1), (1, 0), (0, 2), (1, 1), (0, 3), (1, 2), (1, 3)]
+        for a, j in moves[:MOVES_AHEAD]:
+            move_w1_rows(a, j)
+        nc.sync.dma_start(w1_all[1][:], words_of(w1_words, 1))
+        for a, j in moves[MOVES_AHEAD:]:
+            move_w1_rows(a, j)
+        nc.sync.dma_start(gates[:], gate.rearrange("r p t -> p r t"))
+
+        s2_rows = tile([P, G * N], U8, "s1_all")
+        nc.vector.tensor_copy(s2_rows[:], s2_all[:].indirect(list2[:]))
+        w2_all = late.tile([P, COLS], I32, name="w2_all", offset=0, align_bytes=64)
+        nc.sync.dma_start(w2_all[:], words_of(w2_words, 0))
+        s2 = tile([P, G * N], U8, "s2")
+        for j in range(4):
+            nc.sync.dma_start(
+                s2[W2_PLANE + j : P : 32, :].bitcast(I32),
+                s2_rows[W2_ROWS_AT + j : W2_ROWS_AT + 16 : 4, :].bitcast(I32),
+            )
+
+        for a in range(PASSES):
+            nc.scalar.copy(x_bf[a][:], x_raw[a][:].rearrange("p j t -> p t j"))
+            quantize(x_codes[a], x_scales[a], x_bf[a])
         for r in range(G):
-            gather_w1(1, r, tile([P, H], U32, f"w1_1{r}"))
+            gather_w1(0, r)
+            first_product(0, r, 0)
+            if r == 0:
+                first_product(0, 0, 1)
+        for r in range(G):
+            gather_w1(1, r)
             first_product(1, r, 0)
-        for r in range(G):
-            activate(r, 0)
+        first_product(1, 0, 1)
+        for r, c in units[:4]:
+            activate(r, c)
+        for r, c in units[4:]:
             for a in range(PASSES):
-                first_product(a, r, 1)
+                first_product(a, r, c)
+            activate(r, c)
+
+        def pack(r, c):
+            quantize(h_codes[r, c], h_scales[r, c], h_bf[r, c])
+
+        weigh(0, 0)
+        for r in range(1, G):
             weigh(r, 0)
+            pack(r - 1, 0)
+        weigh(0, 1)
+        pack(LAST, 0)
         for r in range(G):
-            activate(r, 1)
-            if r == LAST:
-                keep_clock(r)
-            turn(r, 0)
+            gather_w2(r)
+            second_product(r, 0)
+        for r in range(1, G):
             weigh(r, 1)
-            turn(r, 1)
-        for c in range(TOKEN_TILES):
-            for r in range(G):
-                take_out(r, c)
-        for c in range(TOKEN_TILES):
-            for r in range(G):
-                if c == 0:
-                    gather_w2(r)
-                second_product(r, c)
+            pack(r - 1, 1)
+            second_product(r - 1, 1)
+        pack(LAST, 1)
+        second_product(LAST, 1)
         store(0, 0, nc.scalar.copy)
         store(1, 0, nc.scalar.copy)
         store(1, 1, nc.vector.tensor_copy)

@@ -14,7 +14,11 @@ U16 = mybir.dt.uint16
 U8 = mybir.dt.uint8
 FP8X4 = mybir.dt.float8_e4m3fn_x4
 SILU = mybir.ActivationFunctionType.Silu
+COPY = mybir.ActivationFunctionType.Copy
 MULT = mybir.AluOpType.mult
+ADD = mybir.AluOpType.add
+SUBTRACT = mybir.AluOpType.subtract
+IS_EQUAL = mybir.AluOpType.is_equal
 
 P = 128
 PASSES = K // 512
@@ -27,6 +31,9 @@ W2_ROWS_AT = 48
 W2_PLANE = 8
 MOVES_AHEAD = 6
 ACC_BANK = {(0, 0): 0, (1, 0): 1, (2, 0): 2, (0, 1): 3, (1, 1): 1, (2, 1): 3}
+TURNED = [(0, 1), (1, 1)]
+TURN_BANK = {(0, 1): 0, (1, 1): 2}
+GATE_ROWS_AT = P - len(TURNED)
 
 
 def tile_moe_wsel_b_silu_f_kernel(
@@ -58,14 +65,29 @@ def tile_moe_wsel_b_silu_f_kernel(
         x_raw = [tile([P, 4, T], F32, f"x_raw{a}") for a in range(PASSES)]
         w1_all = [tile([P, COLS], I32, "w1_all0")]
 
+        gate_rows = tile([P, P], F32, "gate_rows")
+        ident = tile([P, P], F32, "ident")
+        ones = tile([P, P], F32, "ones")
+        column = tile([P, P], F32, "column")
+        row = tile([P, 32], F32, "row")
+        quadrant = tile([P, 1], F32, "quadrant")
+
+        nc.vector.memset(ones[:], 1.0)
         nc.vector.memset(s1_all[0:W1_ROWS_AT, :].bitcast(I32), 0)
+        nc.vector.tensor_tensor_scan(column[:], ones[:], ones[:], 0.0, MULT, ADD)
+        for q in range(4):
+            nc.gpsimd.memset(quadrant[32 * q : 32 * (q + 1), :], 32.0 * q)
+        nc.gpsimd.memset(gate_rows[0:GATE_ROWS_AT, :], 0.0)
         nc.gpsimd.memset(s2_all[0:W2_ROWS_AT, :].bitcast(I32), 0)
         nc.gpsimd.memset(s2_all[W2_ROWS_AT + 16 : P, :].bitcast(I32), 0)
+        nc.vector.transpose(row[:], column[:, 0:32])
+        nc.vector.tensor_scalar(ident[:], column[:], row[:, 0:1], quadrant[:], SUBTRACT, IS_EQUAL)
 
         nc.sync.dma_start(list1[:], offs)
         nc.sync.dma_start(s1_all[W1_ROWS_AT:P, :].bitcast(I32), w1_scales.rearrange("a b n -> b a n").bitcast(I32))
         nc.sync.dma_start(list2[:], offs2)
         nc.sync.dma_start(s2_all[W2_ROWS_AT : W2_ROWS_AT + 16, :].bitcast(I32), w2_scales[0].bitcast(I32))
+        nc.sync.dma_start(gate_rows[GATE_ROWS_AT:P, :], gate[0 : len(TURNED), 0, P:T])
         for a in range(PASSES):
             nc.sync.dma_start(x_raw[a][:], rows_of_x(a))
         nc.sync.dma_start(w1_all[0][:], words_of(w1_words, 0))
@@ -74,11 +96,14 @@ def tile_moe_wsel_b_silu_f_kernel(
         x_codes = [tile([P, T], U32, f"x_codes{a}") for a in range(PASSES)]
         x_scales = [tile([P, T], U8, f"x_scales{a}") for a in range(PASSES)]
         units = [(r, c) for c in range(TOKEN_TILES) for r in range(G)]
-        act = {u: tile([P, P, 4], F32, f"act{u[0]}{u[1]}") for u in units}
-        h_bf = {u: tile([P, P, 4], BF16, f"h_bf{u[0]}{u[1]}") for u in units[:4]}
-        for n, u in enumerate(units[4:]):
-            h_bf[u] = late.tile([P, P, 4], BF16, name=f"h_bf{u[0]}{u[1]}", offset=2 * H * n, align_bytes=64)
-        h_codes = {u: tile([P, P], U32, f"h_codes{u[0]}{u[1]}") for u in units}
+        act = {u: tile([P, P, 4], F32, f"act{u[0]}{u[1]}") for u in units[:-1]}
+        h_bf = {u: tile([P, P, 4], BF16, f"h_bf{u[0]}{u[1]}") for u in units[:-1]}
+        h_bf[LAST, 1] = late.tile([P, P, 4], BF16, name="h_bf_last", offset=0, align_bytes=64)
+        h_codes = {u: tile([P, P], U32, f"h_codes{u[0]}{u[1]}") for u in units if u not in TURNED}
+        for n, u in enumerate(TURNED):
+            h_codes[u] = late.tile([P, P], U32, name=f"h_codes{u[0]}{u[1]}", offset=2 * H + 4 * P * n, align_bytes=64)
+        by_token = {}
+        turned = {}
         h_scales = {u: tile([P, P], U8, f"h_scales{u[0]}{u[1]}") for u in units}
         acc = {}
         w1 = {}
@@ -102,6 +127,17 @@ def tile_moe_wsel_b_silu_f_kernel(
         def first_product(a, r, c):
             if a == 0:
                 acc[r, c] = bank([P, 4, P], ACC_BANK[r, c])
+            if (r, c) in TURNED:
+                nc.tensor.matmul_mx(
+                    out=acc[r, c][:].rearrange("t j m -> t (j m)"),
+                    lhsT=x_codes[a][:, P * c : P * (c + 1)].bitcast(FP8X4),
+                    lhsT_scale=x_scales[a][:, P * c : P * (c + 1)],
+                    rhs=w1[a, r][:].rearrange("p j m -> p (j m)").bitcast(FP8X4),
+                    rhs_scale=s1[a][4 * a : P, H * r : H * (r + 1)],
+                    start=(a == 0),
+                    stop=(a == PASSES - 1),
+                )
+                return
             for j in range(4):
                 nc.tensor.matmul_mx(
                     out=acc[r, c][:, j, :],
@@ -114,7 +150,25 @@ def tile_moe_wsel_b_silu_f_kernel(
                 )
 
         def activate(r, c):
-            nc.scalar.activation(act[r, c][:], acc[r, c][:].rearrange("p j t -> p t j"), SILU)
+            if (r, c) in TURNED:
+                values = act[r, c][:].rearrange("t a b -> t (a b)").rearrange("t (u m e) -> t u m e", u=2, e=2)
+                nc.scalar.activation(values, acc[r, c][:].rearrange("t (u e) m -> t u m e", u=2), SILU)
+            else:
+                nc.scalar.activation(act[r, c][:], acc[r, c][:].rearrange("p j t -> p t j"), SILU)
+
+        def weigh_by_token(r, c):
+            by_token[r, c] = tile([P, H], BF16, f"by_token{r}")
+            values = act[r, c][:].rearrange("t a b -> t (a b)")
+            nc.scalar.activation(by_token[r, c][:], values, COPY, scale=gate_cols[:, r : r + 1])
+
+        def turn(r, c):
+            turned[r, c] = bank([P, 2, P], TURN_BANK[r, c])
+            pairs = by_token[r, c][:].bitcast(F32)
+            for u in range(2):
+                nc.tensor.transpose(turned[r, c][:, u, :], pairs[:, P * u : P * (u + 1)], ident[:])
+
+        def take_out(r, c):
+            nc.scalar.copy(h_bf[r, c][:].bitcast(F32), turned[r, c][:].rearrange("p u t -> p t u"))
 
         def weigh(r, c):
             factor = gates[:, r, P * c : P * (c + 1)].unsqueeze(2).to_broadcast([P, P, 4])
@@ -125,7 +179,7 @@ def tile_moe_wsel_b_silu_f_kernel(
             for m in range(OUT_TILES):
                 b, slot = divmod(m, per_bank)
                 if r == 0 and slot == 0:
-                    y[c, b] = bank([P, per_bank, P], G + 1 + c + b)
+                    y[c, b] = bank([P, per_bank, P], 5 + c + b)
                 nc.tensor.matmul_mx(
                     out=y[c, b][:, slot, :],
                     lhsT=w2[r][:, P * m : P * (m + 1)].bitcast(FP8X4),
@@ -187,6 +241,10 @@ def tile_moe_wsel_b_silu_f_kernel(
                 s2_rows[W2_ROWS_AT + j : W2_ROWS_AT + 16 : 4, :].bitcast(I32),
             )
 
+        gate_ps = bank([P, P], 4)
+        nc.tensor.transpose(gate_ps[:], gate_rows[:], ident[:])
+        gate_cols = tile([P, len(TURNED)], F32, "gate_cols")
+        nc.scalar.copy(gate_cols[:], gate_ps[:, GATE_ROWS_AT:P])
         for a in range(PASSES):
             nc.scalar.copy(x_bf[a][:], x_raw[a][:].rearrange("p j t -> p t j"))
             quantize(x_codes[a], x_scales[a], x_bf[a])
@@ -199,31 +257,39 @@ def tile_moe_wsel_b_silu_f_kernel(
             gather_w1(1, r)
             first_product(1, r, 0)
         first_product(1, 0, 1)
-        for r, c in units[:4]:
-            activate(r, c)
-        for r, c in units[4:]:
-            for a in range(PASSES):
-                first_product(a, r, c)
-            activate(r, c)
 
         def pack(r, c):
             quantize(h_codes[r, c], h_scales[r, c], h_bf[r, c])
 
+        for r in range(G):
+            activate(r, 0)
+        for a in range(PASSES):
+            first_product(a, 1, 1)
+        for u in TURNED:
+            activate(*u)
+        for a in range(PASSES):
+            first_product(a, LAST, 1)
         weigh(0, 0)
         for r in range(1, G):
             weigh(r, 0)
             pack(r - 1, 0)
-        weigh(0, 1)
         pack(LAST, 0)
+        for u in TURNED:
+            weigh_by_token(*u)
+            turn(*u)
         for r in range(G):
             gather_w2(r)
             second_product(r, 0)
+        take_out(0, 1)
+        act[LAST, 1] = tile([P, P, 4], F32, "by_token0")
+        activate(LAST, 1)
+        take_out(1, 1)
+        pack(0, 1)
+        second_product(0, 1)
+        weigh(LAST, 1)
         for r in range(1, G):
-            weigh(r, 1)
-            pack(r - 1, 1)
-            second_product(r - 1, 1)
-        pack(LAST, 1)
-        second_product(LAST, 1)
+            pack(r, 1)
+            second_product(r, 1)
         store(0, 0, nc.scalar.copy)
         store(1, 0, nc.scalar.copy)
         store(1, 1, nc.vector.tensor_copy)

@@ -26,14 +26,15 @@ TOKEN_TILES = T // P
 OUT_TILES = N // P
 COLS = E * H
 LAST = G - 1
-W1_ROWS_AT = 96
-W2_ROWS_AT = 48
+ROW_STEP = 4
+W2_ROWS_AT = 32
 W2_PLANE = 8
 MOVES_AHEAD = 6
 ACC_BANK = {(0, 0): 0, (1, 0): 1, (2, 0): 2, (0, 1): 3, (1, 1): 1, (2, 1): 3}
 TURNED = [(0, 1), (1, 1)]
 TURN_BANK = {(0, 1): 0, (1, 1): 2}
-GATE_ROWS_AT = P - len(TURNED)
+GATE_ROWS_AT = P - TOKEN_TILES
+UPRIGHT = [(0, 0), (1, 0), (2, 0), (2, 1)]
 
 
 def tile_moe_wsel_b_silu_f_kernel(
@@ -65,31 +66,32 @@ def tile_moe_wsel_b_silu_f_kernel(
         x_raw = [tile([P, 4, T], F32, f"x_raw{a}") for a in range(PASSES)]
         w1_all = [tile([P, COLS], I32, "w1_all0")]
 
-        gate_rows = tile([P, P], F32, "gate_rows")
+        gate_rows = tile([P, G, P], F32, "gate_rows")
         ident = tile([P, P], F32, "ident")
         ones = tile([P, P], F32, "ones")
         column = tile([P, P], F32, "column")
         row = tile([P, 32], F32, "row")
         quadrant = tile([P, 1], F32, "quadrant")
 
+        nc.vector.memset(s1_all[:].bitcast(I32), 0)
         nc.vector.memset(ones[:], 1.0)
-        nc.vector.memset(s1_all[0:W1_ROWS_AT, :].bitcast(I32), 0)
         nc.vector.tensor_tensor_scan(column[:], ones[:], ones[:], 0.0, MULT, ADD)
         for q in range(4):
             nc.gpsimd.memset(quadrant[32 * q : 32 * (q + 1), :], 32.0 * q)
-        nc.gpsimd.memset(gate_rows[0:GATE_ROWS_AT, :], 0.0)
-        nc.gpsimd.memset(s2_all[0:W2_ROWS_AT, :].bitcast(I32), 0)
-        nc.gpsimd.memset(s2_all[W2_ROWS_AT + 16 : P, :].bitcast(I32), 0)
+        nc.gpsimd.memset(gate_rows[0:GATE_ROWS_AT, :, :], 0.0)
+        nc.gpsimd.memset(s2_all[:].bitcast(I32), 0)
         nc.vector.transpose(row[:], column[:, 0:32])
         nc.vector.tensor_scalar(ident[:], column[:], row[:, 0:1], quadrant[:], SUBTRACT, IS_EQUAL)
 
         nc.sync.dma_start(list1[:], offs)
-        nc.sync.dma_start(s1_all[W1_ROWS_AT:P, :].bitcast(I32), w1_scales.rearrange("a b n -> b a n").bitcast(I32))
+        nc.sync.dma_start(x_raw[0][:, 0:2, :], rows_of_x(0)[:, 0:2, :])
+        nc.sync.dma_start(s1_all[0:P:ROW_STEP, :].bitcast(I32), w1_scales.rearrange("a b n -> b a n").bitcast(I32))
         nc.sync.dma_start(list2[:], offs2)
-        nc.sync.dma_start(s2_all[W2_ROWS_AT : W2_ROWS_AT + 16, :].bitcast(I32), w2_scales[0].bitcast(I32))
-        nc.sync.dma_start(gate_rows[GATE_ROWS_AT:P, :], gate[0 : len(TURNED), 0, P:T])
-        for a in range(PASSES):
-            nc.sync.dma_start(x_raw[a][:], rows_of_x(a))
+        w2_rows = slice(W2_ROWS_AT, W2_ROWS_AT + 16 * ROW_STEP, ROW_STEP)
+        nc.sync.dma_start(gate_rows[GATE_ROWS_AT:P, :, :], gate[:, 0, :].rearrange("r (c t) -> c r t", t=P))
+        nc.sync.dma_start(x_raw[0][:, 2:4, :], rows_of_x(0)[:, 2:4, :])
+        nc.sync.dma_start(x_raw[1][:], rows_of_x(1))
+        nc.sync.dma_start(s2_all[w2_rows, :].bitcast(I32), w2_scales[0].bitcast(I32))
         nc.sync.dma_start(w1_all[0][:], words_of(w1_words, 0))
 
         x_bf = [tile([P, T, 4], BF16, f"x_bf{a}") for a in range(PASSES)]
@@ -159,7 +161,7 @@ def tile_moe_wsel_b_silu_f_kernel(
         def weigh_by_token(r, c):
             by_token[r, c] = tile([P, H], BF16, f"by_token{r}")
             values = act[r, c][:].rearrange("t a b -> t (a b)")
-            nc.scalar.activation(by_token[r, c][:], values, COPY, scale=gate_cols[:, r : r + 1])
+            nc.scalar.activation(by_token[r, c][:], values, COPY, scale=gate_cols[:, r, c : c + 1])
 
         def turn(r, c):
             turned[r, c] = bank([P, 2, P], TURN_BANK[r, c])
@@ -171,7 +173,7 @@ def tile_moe_wsel_b_silu_f_kernel(
             nc.scalar.copy(h_bf[r, c][:].bitcast(F32), turned[r, c][:].rearrange("p u t -> p t u"))
 
         def weigh(r, c):
-            factor = gates[:, r, P * c : P * (c + 1)].unsqueeze(2).to_broadcast([P, P, 4])
+            factor = gates[:, UPRIGHT.index((r, c)), :].unsqueeze(2).to_broadcast([P, P, 4])
             nc.vector.tensor_tensor(h_bf[r, c][:], act[r, c][:], factor, MULT)
 
         def second_product(r, c):
@@ -197,9 +199,8 @@ def tile_moe_wsel_b_silu_f_kernel(
             rows = out[P * per_bank * b : P * per_bank * (b + 1), P * c : P * (c + 1)]
             nc.sync.dma_start(rows.rearrange("(m p) t -> p m t", p=P), res[:])
 
-        gates = shared.tile([P, G, T], F32, name="gates", offset=0, align_bytes=64)
-        s1_rows = shared.tile([P, G, P, 4], U8, name="s1_rows", offset=4 * G * T - G * H // 2, align_bytes=64)
-        w1_all.append(shared.tile([P, COLS], I32, name="w1_all1", offset=4 * G * T, align_bytes=64))
+        s1_rows = shared.tile([P, G, P, 4], U8, name="s1_rows", offset=0, align_bytes=64)
+        w1_all.append(shared.tile([P, COLS], I32, name="w1_all1", offset=0, align_bytes=64))
         s1_turned = tile([P, G, 4, P], U8, "s1_turned")
 
         def gather_w1_scales(r):
@@ -219,7 +220,7 @@ def tile_moe_wsel_b_silu_f_kernel(
         def move_w1_rows(a, j):
             nc.sync.dma_start(
                 s1[a][4 * a + j : P : 32, :].bitcast(I32),
-                s1_turned[W1_ROWS_AT + 2 * j + a : P : 8].rearrange("p r j m -> p (r j m)").bitcast(I32),
+                s1_turned[ROW_STEP * (2 * j + a) : P : 8 * ROW_STEP].rearrange("p r j m -> p (r j m)").bitcast(I32),
             )
 
         moves = [(0, 0), (0, 1), (1, 0), (0, 2), (1, 1), (0, 3), (1, 2), (1, 3)]
@@ -228,7 +229,6 @@ def tile_moe_wsel_b_silu_f_kernel(
         nc.sync.dma_start(w1_all[1][:], words_of(w1_words, 1))
         for a, j in moves[MOVES_AHEAD:]:
             move_w1_rows(a, j)
-        nc.sync.dma_start(gates[:], gate.rearrange("r p t -> p r t"))
 
         s2_rows = tile([P, G * N], U8, "s1_all")
         nc.vector.tensor_copy(s2_rows[:], s2_all[:].indirect(list2[:]))
@@ -238,13 +238,19 @@ def tile_moe_wsel_b_silu_f_kernel(
         for j in range(4):
             nc.sync.dma_start(
                 s2[W2_PLANE + j : P : 32, :].bitcast(I32),
-                s2_rows[W2_ROWS_AT + j : W2_ROWS_AT + 16 : 4, :].bitcast(I32),
+                s2_rows[W2_ROWS_AT + ROW_STEP * j : W2_ROWS_AT + 16 * ROW_STEP : 4 * ROW_STEP, :].bitcast(I32),
             )
 
-        gate_ps = bank([P, P], 4)
-        nc.tensor.transpose(gate_ps[:], gate_rows[:], ident[:])
-        gate_cols = tile([P, len(TURNED)], F32, "gate_cols")
-        nc.scalar.copy(gate_cols[:], gate_ps[:, GATE_ROWS_AT:P])
+        gate_ps = bank([P, G, P], 4)
+        for r in range(G):
+            nc.tensor.transpose(gate_ps[:, r, :], gate_rows[:, r, :], ident[:])
+        gate_cols = tile([P, G, TOKEN_TILES], F32, "gate_cols")
+        nc.scalar.copy(gate_cols[:], gate_ps[:, :, GATE_ROWS_AT:P])
+        spread = bank([P, len(UPRIGHT), P], 5)
+        for n, (r, c) in enumerate(UPRIGHT):
+            nc.tensor.transpose(spread[:, n, :], gate_cols[:, r, c : c + 1].to_broadcast([P, P]), ident[:])
+        gates = tile([P, len(UPRIGHT), P], F32, "gates")
+        nc.scalar.copy(gates[:], spread[:])
         for a in range(PASSES):
             nc.scalar.copy(x_bf[a][:], x_raw[a][:].rearrange("p j t -> p t j"))
             quantize(x_codes[a], x_scales[a], x_bf[a])

@@ -29,7 +29,7 @@ LAST = G - 1
 ROW_STEP = 4
 W2_ROWS_AT = 32
 W2_PLANE = 8
-MOVES_AHEAD = 6
+MOVES_AHEAD = 5
 ACC_BANK = {(0, 0): 0, (1, 0): 1, (2, 0): 2, (0, 1): 3, (1, 1): 1, (2, 1): 3}
 TURNED = [(0, 1), (1, 1)]
 TURN_BANK = {(0, 1): 0, (1, 1): 2}
@@ -43,7 +43,6 @@ def tile_moe_wsel_b_silu_f_kernel(
     nc = tc.nc
     with ExitStack() as ctx:
         sb = ctx.enter_context(tc.tile_pool(name="sb", bufs=1))
-        shared = ctx.enter_context(tc.tile_pool(name="shared", bufs=1))
         late = ctx.enter_context(tc.tile_pool(name="late", bufs=1))
         ps = ctx.enter_context(tc.psum_pool(name="ps", bufs=1))
 
@@ -199,8 +198,9 @@ def tile_moe_wsel_b_silu_f_kernel(
             rows = out[P * per_bank * b : P * per_bank * (b + 1), P * c : P * (c + 1)]
             nc.sync.dma_start(rows.rearrange("(m p) t -> p m t", p=P), res[:])
 
-        s1_rows = shared.tile([P, G, P, 4], U8, name="s1_rows", offset=0, align_bytes=64)
-        w1_all.append(shared.tile([P, COLS], I32, name="w1_all1", offset=0, align_bytes=64))
+        s1_rows = tile([P, G, P, 4], U8, "s1_rows")
+        w1_all.append(tile([P, COLS], I32, "w1_all1"))
+        nc.sync.dma_start(w1_all[1][:, 0 : COLS // 2], words_of(w1_words, 1)[:, 0 : COLS // 2])
         s1_turned = tile([P, G, 4, P], U8, "s1_turned")
 
         def gather_w1_scales(r):
@@ -223,10 +223,10 @@ def tile_moe_wsel_b_silu_f_kernel(
                 s1_turned[ROW_STEP * (2 * j + a) : P : 8 * ROW_STEP].rearrange("p r j m -> p (r j m)").bitcast(I32),
             )
 
-        moves = [(0, 0), (0, 1), (1, 0), (0, 2), (1, 1), (0, 3), (1, 2), (1, 3)]
+        moves = [(0, 0), (0, 1), (1, 0), (0, 2), (0, 3), (1, 1), (1, 2), (1, 3)]
         for a, j in moves[:MOVES_AHEAD]:
             move_w1_rows(a, j)
-        nc.sync.dma_start(w1_all[1][:], words_of(w1_words, 1))
+        nc.sync.dma_start(w1_all[1][:, COLS // 2 : COLS], words_of(w1_words, 1)[:, COLS // 2 : COLS])
         for a, j in moves[MOVES_AHEAD:]:
             move_w1_rows(a, j)
 

@@ -29,11 +29,13 @@ LAST = G - 1
 ROW_STEP = 4
 W2_ROWS_AT = 32
 W2_PLANE = 8
-MOVES_AHEAD = 5
+COVER = COLS // 4
 ACC_BANK = {(0, 0): 0, (1, 0): 1, (2, 0): 2, (0, 1): 3, (1, 1): 1, (2, 1): 3}
 TURNED = [(0, 1), (1, 1)]
 TURN_BANK = {(0, 1): 0, (1, 1): 2}
 GATE_ROWS_AT = P - TOKEN_TILES
+PER_BANK = (OUT_TILES, 1)
+OUT_BANKS = ((5,), (4, 6, 7, 1))
 UPRIGHT = [(0, 0), (1, 0), (2, 0), (2, 1)]
 
 
@@ -84,10 +86,10 @@ def tile_moe_wsel_b_silu_f_kernel(
 
         nc.sync.dma_start(list1[:], offs)
         nc.sync.dma_start(x_raw[0][:, 0:2, :], rows_of_x(0)[:, 0:2, :])
-        nc.sync.dma_start(s1_all[0:P:ROW_STEP, :].bitcast(I32), w1_scales.rearrange("a b n -> b a n").bitcast(I32))
         nc.sync.dma_start(list2[:], offs2)
         w2_rows = slice(W2_ROWS_AT, W2_ROWS_AT + 16 * ROW_STEP, ROW_STEP)
         nc.sync.dma_start(gate_rows[GATE_ROWS_AT:P, :, :], gate[:, 0, :].rearrange("r (c t) -> c r t", t=P))
+        nc.sync.dma_start(s1_all[0:P:ROW_STEP, :].bitcast(I32), w1_scales.rearrange("a b n -> b a n").bitcast(I32))
         nc.sync.dma_start(x_raw[0][:, 2:4, :], rows_of_x(0)[:, 2:4, :])
         nc.sync.dma_start(x_raw[1][:], rows_of_x(1))
         nc.sync.dma_start(s2_all[w2_rows, :].bitcast(I32), w2_scales[0].bitcast(I32))
@@ -176,11 +178,11 @@ def tile_moe_wsel_b_silu_f_kernel(
             nc.vector.tensor_tensor(h_bf[r, c][:], act[r, c][:], factor, MULT)
 
         def second_product(r, c):
-            per_bank = OUT_TILES // (c + 1)
+            per_bank = PER_BANK[c]
             for m in range(OUT_TILES):
                 b, slot = divmod(m, per_bank)
                 if r == 0 and slot == 0:
-                    y[c, b] = bank([P, per_bank, P], 5 + c + b)
+                    y[c, b] = bank([P, per_bank, P], OUT_BANKS[c][b])
                 nc.tensor.matmul_mx(
                     out=y[c, b][:, slot, :],
                     lhsT=w2[r][:, P * m : P * (m + 1)].bitcast(FP8X4),
@@ -191,16 +193,16 @@ def tile_moe_wsel_b_silu_f_kernel(
                     stop=(r == LAST and slot == per_bank - 1),
                 )
 
-        def store(c, b, copy):
-            per_bank = OUT_TILES // (c + 1)
+        def store(c, b, copy, queue):
+            per_bank = PER_BANK[c]
             res = tile([P, per_bank, P], F32, f"res{c}{b}")
             copy(res[:], y[c, b][:])
             rows = out[P * per_bank * b : P * per_bank * (b + 1), P * c : P * (c + 1)]
-            nc.sync.dma_start(rows.rearrange("(m p) t -> p m t", p=P), res[:])
+            queue.dma_start(rows.rearrange("(m p) t -> p m t", p=P), res[:])
 
         s1_rows = tile([P, G, P, 4], U8, "s1_rows")
         w1_all.append(tile([P, COLS], I32, "w1_all1"))
-        nc.sync.dma_start(w1_all[1][:, 0 : COLS // 2], words_of(w1_words, 1)[:, 0 : COLS // 2])
+        nc.sync.dma_start(w1_all[1][:, 0 : COVER], words_of(w1_words, 1)[:, 0 : COVER])
         s1_turned = tile([P, G, 4, P], U8, "s1_turned")
 
         def gather_w1_scales(r):
@@ -223,12 +225,11 @@ def tile_moe_wsel_b_silu_f_kernel(
                 s1_turned[ROW_STEP * (2 * j + a) : P : 8 * ROW_STEP].rearrange("p r j m -> p (r j m)").bitcast(I32),
             )
 
-        moves = [(0, 0), (0, 1), (1, 0), (0, 2), (0, 3), (1, 1), (1, 2), (1, 3)]
-        for a, j in moves[:MOVES_AHEAD]:
-            move_w1_rows(a, j)
-        nc.sync.dma_start(w1_all[1][:, COLS // 2 : COLS], words_of(w1_words, 1)[:, COLS // 2 : COLS])
-        for a, j in moves[MOVES_AHEAD:]:
-            move_w1_rows(a, j)
+        for j in range(4):
+            move_w1_rows(0, j)
+        nc.sync.dma_start(w1_all[1][:, COVER : COLS], words_of(w1_words, 1)[:, COVER : COLS])
+        for j in range(4):
+            move_w1_rows(1, j)
 
         s2_rows = tile([P, G * N], U8, "s1_all")
         nc.vector.tensor_copy(s2_rows[:], s2_all[:].indirect(list2[:]))
@@ -296,6 +297,8 @@ def tile_moe_wsel_b_silu_f_kernel(
         for r in range(1, G):
             pack(r, 1)
             second_product(r, 1)
-        store(0, 0, nc.scalar.copy)
-        store(1, 0, nc.scalar.copy)
-        store(1, 1, nc.vector.tensor_copy)
+        store(0, 0, nc.scalar.copy, nc.sync)
+        store(1, 0, nc.vector.tensor_copy, nc.sync)
+        store(1, 1, nc.scalar.copy, nc.sync)
+        store(1, 2, nc.vector.tensor_copy, nc.sync)
+        store(1, 3, nc.scalar.copy, nc.scalar)

@@ -34,8 +34,8 @@ ACC_BANK = {(0, 0): 0, (1, 0): 1, (2, 0): 2, (0, 1): 3, (1, 1): 1, (2, 1): 3}
 TURNED = [(0, 1), (1, 1)]
 TURN_BANK = {(0, 1): 0, (1, 1): 2}
 GATE_ROWS_AT = P - TOKEN_TILES
-PER_BANK = (OUT_TILES, 1)
-OUT_BANKS = ((5,), (4, 6, 7, 1))
+PER_BANK = (OUT_TILES, OUT_TILES // 2)
+OUT_BANKS = ((5,), (6, 7))
 UPRIGHT = [(0, 0), (1, 0), (2, 0), (2, 1)]
 
 
@@ -193,12 +193,12 @@ def tile_moe_wsel_b_silu_f_kernel(
                     stop=(r == LAST and slot == per_bank - 1),
                 )
 
-        def store(c, b, copy, queue):
+        def store(c, b, copy):
             per_bank = PER_BANK[c]
             res = tile([P, per_bank, P], F32, f"res{c}{b}")
             copy(res[:], y[c, b][:])
             rows = out[P * per_bank * b : P * per_bank * (b + 1), P * c : P * (c + 1)]
-            queue.dma_start(rows.rearrange("(m p) t -> p m t", p=P), res[:])
+            nc.sync.dma_start(rows.rearrange("(m p) t -> p m t", p=P), res[:])
 
         s1_rows = tile([P, G, P, 4], U8, "s1_rows")
         w1_all.append(tile([P, COLS], I32, "w1_all1"))
@@ -297,8 +297,6 @@ def tile_moe_wsel_b_silu_f_kernel(
         for r in range(1, G):
             pack(r, 1)
             second_product(r, 1)
-        store(0, 0, nc.scalar.copy, nc.sync)
-        store(1, 0, nc.vector.tensor_copy, nc.sync)
-        store(1, 1, nc.scalar.copy, nc.sync)
-        store(1, 2, nc.vector.tensor_copy, nc.sync)
-        store(1, 3, nc.scalar.copy, nc.scalar)
+        store(0, 0, nc.scalar.copy)
+        store(1, 0, nc.scalar.copy)
+        store(1, 1, nc.vector.tensor_copy)

@@ -29,7 +29,6 @@ LAST = G - 1
 ROW_STEP = 4
 W2_ROWS_AT = 32
 W2_PLANE = 8
-COVER = COLS // 4
 ACC_BANK = {(0, 0): 0, (1, 0): 1, (2, 0): 2, (0, 1): 3, (1, 1): 1, (2, 1): 3}
 TURNED = [(0, 1), (1, 1)]
 TURN_BANK = {(0, 1): 0, (1, 1): 2}
@@ -57,14 +56,11 @@ def tile_moe_wsel_b_silu_f_kernel(
         def words_of(dram, a):
             return dram[a].rearrange("p n d -> p (n d)").bitcast(I32)
 
-        def rows_of_x(a):
-            return xT[512 * a : 512 * (a + 1), :].rearrange("(p j) t -> p j t", j=4)
-
         list1 = tile([P, G * H // 16], U16, "list1")
         list2 = tile([P, G * N // 16], U16, "list2")
         s1_all = tile([P, COLS], U8, "s1_all")
         s2_all = late.tile([P, COLS], U8, name="s2_all", offset=0, align_bytes=64)
-        x_raw = [tile([P, 4, T], F32, f"x_raw{a}") for a in range(PASSES)]
+        x_raw = tile([P, PASSES, 4, T], F32, "x_raw")
         w1_all = [tile([P, COLS], I32, "w1_all0")]
 
         gate_rows = tile([P, G, P], F32, "gate_rows")
@@ -85,13 +81,11 @@ def tile_moe_wsel_b_silu_f_kernel(
         nc.vector.tensor_scalar(ident[:], column[:], row[:, 0:1], quadrant[:], SUBTRACT, IS_EQUAL)
 
         nc.sync.dma_start(list1[:], offs)
-        nc.sync.dma_start(x_raw[0][:, 0:2, :], rows_of_x(0)[:, 0:2, :])
         nc.sync.dma_start(list2[:], offs2)
-        w2_rows = slice(W2_ROWS_AT, W2_ROWS_AT + 16 * ROW_STEP, ROW_STEP)
         nc.sync.dma_start(gate_rows[GATE_ROWS_AT:P, :, :], gate[:, 0, :].rearrange("r (c t) -> c r t", t=P))
         nc.sync.dma_start(s1_all[0:P:ROW_STEP, :].bitcast(I32), w1_scales.rearrange("a b n -> b a n").bitcast(I32))
-        nc.sync.dma_start(x_raw[0][:, 2:4, :], rows_of_x(0)[:, 2:4, :])
-        nc.sync.dma_start(x_raw[1][:], rows_of_x(1))
+        nc.sync.dma_start(x_raw[:], xT.rearrange("(a p j) t -> p a j t", a=PASSES, j=4))
+        w2_rows = slice(W2_ROWS_AT, W2_ROWS_AT + 16 * ROW_STEP, ROW_STEP)
         nc.sync.dma_start(s2_all[w2_rows, :].bitcast(I32), w2_scales[0].bitcast(I32))
         nc.sync.dma_start(w1_all[0][:], words_of(w1_words, 0))
 
@@ -202,7 +196,6 @@ def tile_moe_wsel_b_silu_f_kernel(
 
         s1_rows = tile([P, G, P, 4], U8, "s1_rows")
         w1_all.append(tile([P, COLS], I32, "w1_all1"))
-        nc.sync.dma_start(w1_all[1][:, 0 : COVER], words_of(w1_words, 1)[:, 0 : COVER])
         s1_turned = tile([P, G, 4, P], U8, "s1_turned")
 
         def gather_w1_scales(r):
@@ -227,7 +220,7 @@ def tile_moe_wsel_b_silu_f_kernel(
 
         for j in range(4):
             move_w1_rows(0, j)
-        nc.sync.dma_start(w1_all[1][:, COVER : COLS], words_of(w1_words, 1)[:, COVER : COLS])
+        nc.sync.dma_start(w1_all[1][:], words_of(w1_words, 1))
         for j in range(4):
             move_w1_rows(1, j)
 
@@ -253,7 +246,7 @@ def tile_moe_wsel_b_silu_f_kernel(
         gates = tile([P, len(UPRIGHT), P], F32, "gates")
         nc.scalar.copy(gates[:], spread[:])
         for a in range(PASSES):
-            nc.scalar.copy(x_bf[a][:], x_raw[a][:].rearrange("p j t -> p t j"))
+            nc.scalar.copy(x_bf[a][:], x_raw[:, a].rearrange("p j t -> p t j"))
             quantize(x_codes[a], x_scales[a], x_bf[a])
         for r in range(G):
             gather_w1(0, r)

@@ -29,13 +29,15 @@ LAST = G - 1
 ROW_STEP = 4
 W2_ROWS_AT = 32
 W2_PLANE = 8
-ACC_BANK = {(0, 0): 0, (1, 0): 1, (2, 0): 2, (0, 1): 3, (1, 1): 1, (2, 1): 3}
-TURNED = [(0, 1), (1, 1)]
-TURN_BANK = {(0, 1): 0, (1, 1): 2}
+ACC_BANK = {(0, 0): 0, (0, 1): 1, (1, 0): 2, (2, 0): 3, (2, 1): 4, (1, 1): 3}
+TURNED = [(2, 0), (2, 1)]
+TURN_BANK = {(2, 0): 0, (2, 1): 1}
+CLOSING = (1, 1)
+LAST_OF_TILE = ((2, 0), CLOSING)
 GATE_ROWS_AT = P - TOKEN_TILES
 PER_BANK = (OUT_TILES, OUT_TILES // 2)
 OUT_BANKS = ((5,), (6, 7))
-UPRIGHT = [(0, 0), (1, 0), (2, 0), (2, 1)]
+UPRIGHT = [(0, 0), (0, 1), (1, 0), CLOSING]
 
 
 def tile_moe_wsel_b_silu_f_kernel(
@@ -93,9 +95,9 @@ def tile_moe_wsel_b_silu_f_kernel(
         x_codes = [tile([P, T], U32, f"x_codes{a}") for a in range(PASSES)]
         x_scales = [tile([P, T], U8, f"x_scales{a}") for a in range(PASSES)]
         units = [(r, c) for c in range(TOKEN_TILES) for r in range(G)]
-        act = {u: tile([P, P, 4], F32, f"act{u[0]}{u[1]}") for u in units[:-1]}
-        h_bf = {u: tile([P, P, 4], BF16, f"h_bf{u[0]}{u[1]}") for u in units[:-1]}
-        h_bf[LAST, 1] = late.tile([P, P, 4], BF16, name="h_bf_last", offset=0, align_bytes=64)
+        act = {u: tile([P, P, 4], F32, f"act{u[0]}{u[1]}") for u in units if u != CLOSING}
+        h_bf = {u: tile([P, P, 4], BF16, f"h_bf{u[0]}{u[1]}") for u in units if u != CLOSING}
+        h_bf[CLOSING] = late.tile([P, P, 4], BF16, name="h_bf_last", offset=0, align_bytes=64)
         h_codes = {u: tile([P, P], U32, f"h_codes{u[0]}{u[1]}") for u in units if u not in TURNED}
         for n, u in enumerate(TURNED):
             h_codes[u] = late.tile([P, P], U32, name=f"h_codes{u[0]}{u[1]}", offset=2 * H + 4 * P * n, align_bytes=64)
@@ -154,7 +156,7 @@ def tile_moe_wsel_b_silu_f_kernel(
                 nc.scalar.activation(act[r, c][:], acc[r, c][:].rearrange("p j t -> p t j"), SILU)
 
         def weigh_by_token(r, c):
-            by_token[r, c] = tile([P, H], BF16, f"by_token{r}")
+            by_token[r, c] = tile([P, H], BF16, f"by_token{c}")
             values = act[r, c][:].rearrange("t a b -> t (a b)")
             nc.scalar.activation(by_token[r, c][:], values, COPY, scale=gate_cols[:, r, c : c + 1])
 
@@ -184,7 +186,7 @@ def tile_moe_wsel_b_silu_f_kernel(
                     rhs=h_codes[r, c][:].bitcast(FP8X4),
                     rhs_scale=h_scales[r, c][:],
                     start=(r == 0 and slot == 0),
-                    stop=(r == LAST and slot == per_bank - 1),
+                    stop=((r, c) == LAST_OF_TILE[c] and slot == per_bank - 1),
                 )
 
         def store(c, b, copy):
@@ -248,48 +250,44 @@ def tile_moe_wsel_b_silu_f_kernel(
         for a in range(PASSES):
             nc.scalar.copy(x_bf[a][:], x_raw[:, a].rearrange("p j t -> p t j"))
             quantize(x_codes[a], x_scales[a], x_bf[a])
-        for r in range(G):
-            gather_w1(0, r)
-            first_product(0, r, 0)
-            if r == 0:
-                first_product(0, 0, 1)
-        for r in range(G):
-            gather_w1(1, r)
-            first_product(1, r, 0)
-        first_product(1, 0, 1)
+        for a in range(PASSES):
+            for r in range(G):
+                gather_w1(a, r)
+                for c in range(TOKEN_TILES):
+                    if (r, c) != CLOSING:
+                        first_product(a, r, c)
 
         def pack(r, c):
             quantize(h_codes[r, c], h_scales[r, c], h_bf[r, c])
 
-        for r in range(G):
-            activate(r, 0)
-        for a in range(PASSES):
-            first_product(a, 1, 1)
-        for u in TURNED:
+        early = UPRIGHT[:-1]
+        for u in early + TURNED:
             activate(*u)
         for a in range(PASSES):
-            first_product(a, LAST, 1)
-        weigh(0, 0)
-        for r in range(1, G):
-            weigh(r, 0)
-            pack(r - 1, 0)
-        pack(LAST, 0)
+            first_product(a, *CLOSING)
+        weigh(*early[0])
+        for before, now in zip(early, early[1:]):
+            weigh(*now)
+            pack(*before)
+        pack(*early[-1])
         for u in TURNED:
             weigh_by_token(*u)
             turn(*u)
         for r in range(G):
             gather_w2(r)
-            second_product(r, 0)
-        take_out(0, 1)
-        act[LAST, 1] = tile([P, P, 4], F32, "by_token0")
-        activate(LAST, 1)
-        take_out(1, 1)
-        pack(0, 1)
-        second_product(0, 1)
-        weigh(LAST, 1)
-        for r in range(1, G):
-            pack(r, 1)
-            second_product(r, 1)
+            for u in early:
+                if u[0] == r:
+                    second_product(*u)
+        take_out(*TURNED[0])
+        act[CLOSING] = tile([P, P, 4], F32, f"by_token{TURNED[0][1]}")
+        activate(*CLOSING)
+        take_out(*TURNED[1])
+        pack(*TURNED[0])
+        second_product(*TURNED[0])
+        weigh(*CLOSING)
+        for u in (TURNED[1], CLOSING):
+            pack(*u)
+            second_product(*u)
         store(0, 0, nc.scalar.copy)
         store(1, 0, nc.scalar.copy)
         store(1, 1, nc.vector.tensor_copy)

@@ -198,36 +198,38 @@ def tile_moe_wsel_b_silu_f_kernel(
 
         s1_rows = tile([P, G, P, 4], U8, "s1_rows")
         w1_all.append(tile([P, COLS], I32, "w1_all1"))
-        s1_turned = tile([P, G, 4, P], U8, "s1_turned")
+        s1 = [tile([P, G * H], U8, f"s1_{a}") for a in range(PASSES)]
 
         def gather_w1_scales(r):
             picked = s1_all[:].indirect(list1[:, 32 * r : 32 * (r + 1)])
             nc.vector.tensor_copy(s1_rows[:, r].rearrange("p m j -> p (m j)"), picked)
 
-        def turn_w1_scales(r):
-            nc.vector.tensor_copy(s1_turned[:, r], s1_rows[:, r].rearrange("p m j -> p j m"))
+        def turn_w1_scales(a, r):
+            columns = s1[a][:, H * r : H * (r + 1)].rearrange("p (j m) -> p j m", j=4)
+            nc.vector.tensor_copy(columns, s1_rows[:, r].rearrange("p m j -> p j m"))
 
         gather_w1_scales(0)
         for r in range(1, G):
             gather_w1_scales(r)
-            turn_w1_scales(r - 1)
-        turn_w1_scales(LAST)
-        s1 = [tile([P, G * H], U8, f"s1_{a}") for a in range(PASSES)]
+            turn_w1_scales(0, r - 1)
+        turn_w1_scales(0, LAST)
+        s2_rows = tile([P, G * N], U8, "s1_all")
+        nc.vector.tensor_copy(s2_rows[:], s2_all[:].indirect(list2[:]))
+        for r in range(G):
+            turn_w1_scales(1, r)
 
         def move_w1_rows(a, j):
             nc.sync.dma_start(
                 s1[a][4 * a + j : P : 32, :].bitcast(I32),
-                s1_turned[ROW_STEP * (2 * j + a) : P : 8 * ROW_STEP].rearrange("p r j m -> p (r j m)").bitcast(I32),
+                s1[a][ROW_STEP * (2 * j + a) : P : 8 * ROW_STEP, :].bitcast(I32),
             )
 
-        for j in range(4):
+        for j in range(1, 4):
             move_w1_rows(0, j)
         nc.sync.dma_start(w1_all[1][:], words_of(w1_words, 1))
-        for j in range(4):
+        for j in range(1, 4):
             move_w1_rows(1, j)
 
-        s2_rows = tile([P, G * N], U8, "s1_all")
-        nc.vector.tensor_copy(s2_rows[:], s2_all[:].indirect(list2[:]))
         w2_all = late.tile([P, COLS], I32, name="w2_all", offset=0, align_bytes=64)
         nc.sync.dma_start(w2_all[:], words_of(w2_words, 0))
         s2 = tile([P, G * N], U8, "s2")

@@ -37,7 +37,8 @@ LAST_OF_TILE = ((2, 0), CLOSING)
 GATE_ROWS_AT = P - TOKEN_TILES
 PER_BANK = (OUT_TILES, OUT_TILES // 2)
 OUT_BANKS = ((5,), (6, 7))
-UPRIGHT = [(0, 0), (0, 1), (1, 0), CLOSING]
+POOL_GATED = (1, 0)
+UPRIGHT = [(0, 0), (0, 1), CLOSING, POOL_GATED]
 
 
 def tile_moe_wsel_b_silu_f_kernel(
@@ -96,10 +97,10 @@ def tile_moe_wsel_b_silu_f_kernel(
         x_scales = [tile([P, T], U8, f"x_scales{a}") for a in range(PASSES)]
         units = [(r, c) for c in range(TOKEN_TILES) for r in range(G)]
         act = {u: tile([P, P, 4], F32, f"act{u[0]}{u[1]}") for u in units if u != CLOSING}
-        h_bf = {u: tile([P, P, 4], BF16, f"h_bf{u[0]}{u[1]}") for u in units if u != CLOSING}
+        h_bf = {u: tile([P, P, 4], BF16, f"h_bf{u[0]}{u[1]}") for u in units if u not in (CLOSING, POOL_GATED)}
         h_bf[CLOSING] = late.tile([P, P, 4], BF16, name="h_bf_last", offset=0, align_bytes=64)
-        h_codes = {u: tile([P, P], U32, f"h_codes{u[0]}{u[1]}") for u in units if u not in TURNED}
-        for n, u in enumerate(TURNED):
+        h_codes = {u: tile([P, P], U32, f"h_codes{u[0]}{u[1]}") for u in units if u not in TURNED + [POOL_GATED]}
+        for n, u in enumerate(TURNED + [POOL_GATED]):
             h_codes[u] = late.tile([P, P], U32, name=f"h_codes{u[0]}{u[1]}", offset=2 * H + 4 * P * n, align_bytes=64)
         by_token = {}
         turned = {}
@@ -114,14 +115,16 @@ def tile_moe_wsel_b_silu_f_kernel(
                 out=codes[:].bitcast(FP8X4), scales=scales[:], in_=values[:].rearrange("p t j -> p (t j)")
             )
 
+        def gather(into, window, offsets):
+            nc.vector.tensor_copy(into, window.indirect(offsets))
+
         def gather_w1(a, r):
             w1[a, r] = tile([P, 4, P], U32, f"w1_{a}{r}")
-            window = w1_all[a][:].bitcast(U32).indirect(list1[:, 32 * r : 32 * (r + 1)])
-            nc.vector.tensor_copy(w1[a, r][:].rearrange("p j m -> p m j"), window)
+            gather(w1[a, r][:].rearrange("p j m -> p m j"), w1_all[a][:].bitcast(U32), list1[:, 32 * r : 32 * (r + 1)])
 
         def gather_w2(r):
             w2[r] = tile([P, N], U32, f"w2_{r}")
-            nc.vector.tensor_copy(w2[r][:], w2_all[:].bitcast(U32).indirect(list2[:, 32 * r : 32 * (r + 1)]))
+            gather(w2[r][:], w2_all[:].bitcast(U32), list2[:, 32 * r : 32 * (r + 1)])
 
         def first_product(a, r, c):
             if a == 0:
@@ -201,8 +204,7 @@ def tile_moe_wsel_b_silu_f_kernel(
         s1 = [tile([P, G * H], U8, f"s1_{a}") for a in range(PASSES)]
 
         def gather_w1_scales(r):
-            picked = s1_all[:].indirect(list1[:, 32 * r : 32 * (r + 1)])
-            nc.vector.tensor_copy(s1_rows[:, r].rearrange("p m j -> p (m j)"), picked)
+            gather(s1_rows[:, r].rearrange("p m j -> p (m j)"), s1_all[:], list1[:, 32 * r : 32 * (r + 1)])
 
         def turn_w1_scales(a, r):
             columns = s1[a][:, H * r : H * (r + 1)].rearrange("p (j m) -> p j m", j=4)
@@ -214,7 +216,7 @@ def tile_moe_wsel_b_silu_f_kernel(
             turn_w1_scales(0, r - 1)
         turn_w1_scales(0, LAST)
         s2_rows = tile([P, G * N], U8, "s1_all")
-        nc.vector.tensor_copy(s2_rows[:], s2_all[:].indirect(list2[:]))
+        gather(s2_rows[:], s2_all[:], list2[:])
         for r in range(G):
             turn_w1_scales(1, r)
 
@@ -247,8 +249,10 @@ def tile_moe_wsel_b_silu_f_kernel(
         spread = bank([P, len(UPRIGHT), P], 5)
         for n, (r, c) in enumerate(UPRIGHT):
             nc.tensor.transpose(spread[:, n, :], gate_cols[:, r, c : c + 1].to_broadcast([P, P]), ident[:])
-        gates = tile([P, len(UPRIGHT), P], F32, "gates")
-        nc.scalar.copy(gates[:], spread[:])
+        gates = tile([P, len(UPRIGHT) - 1, P], F32, "gates")
+        nc.scalar.copy(gates[:], spread[:, 0 : len(UPRIGHT) - 1, :])
+        gates_wide = tile([P, P, 4], F32, "gates_wide")
+        nc.scalar.copy(gates_wide[:], spread[:, len(UPRIGHT) - 1, :].unsqueeze(2).to_broadcast([P, P, 4]))
         for a in range(PASSES):
             nc.scalar.copy(x_bf[a][:], x_raw[:, a].rearrange("p j t -> p t j"))
             quantize(x_codes[a], x_scales[a], x_bf[a])
@@ -262,24 +266,29 @@ def tile_moe_wsel_b_silu_f_kernel(
         def pack(r, c):
             quantize(h_codes[r, c], h_scales[r, c], h_bf[r, c])
 
-        early = UPRIGHT[:-1]
-        for u in early + TURNED:
+        def flat(values):
+            return values[:].rearrange("p t j -> p (t j)")
+
+        early = UPRIGHT[:TOKEN_TILES]
+        for u in early + [POOL_GATED] + TURNED:
             activate(*u)
         for a in range(PASSES):
             first_product(a, *CLOSING)
-        weigh(*early[0])
-        for before, now in zip(early, early[1:]):
-            weigh(*now)
-            pack(*before)
-        pack(*early[-1])
+        for u in early:
+            weigh(*u)
+        for u in early:
+            pack(*u)
+        h_bf[POOL_GATED] = tile([P, P, 4], BF16, "h_bf01")
+        nc.gpsimd.tensor_tensor(flat(h_bf[POOL_GATED]), flat(act[POOL_GATED]), flat(gates_wide), MULT)
         for u in TURNED:
             weigh_by_token(*u)
             turn(*u)
         for r in range(G):
             gather_w2(r)
-            for u in early:
-                if u[0] == r:
-                    second_product(*u)
+        for u in early:
+            second_product(*u)
+        pack(*POOL_GATED)
+        second_product(*POOL_GATED)
         take_out(*TURNED[0])
         act[CLOSING] = tile([P, P, 4], F32, f"by_token{TURNED[0][1]}")
         activate(*CLOSING)

@@ -26,6 +26,7 @@ TOKEN_TILES = T // P
 OUT_TILES = N // P
 COLS = E * H
 LAST = G - 1
+HEAD_COLS = COLS // 8
 ROW_STEP = 4
 W2_ROWS_AT = 32
 W2_PLANE = 8
@@ -83,6 +84,7 @@ def tile_moe_wsel_b_silu_f_kernel(
         nc.vector.transpose(row[:], column[:, 0:32])
         nc.vector.tensor_scalar(ident[:], column[:], row[:, 0:1], quadrant[:], SUBTRACT, IS_EQUAL)
 
+        nc.sync.dma_start(w1_all[0][:, 0:HEAD_COLS], words_of(w1_words, 0)[:, 0:HEAD_COLS])
         nc.sync.dma_start(list1[:], offs)
         nc.sync.dma_start(list2[:], offs2)
         nc.sync.dma_start(gate_rows[GATE_ROWS_AT:P, :, :], gate[:, 0, :].rearrange("r (c t) -> c r t", t=P))
@@ -90,7 +92,7 @@ def tile_moe_wsel_b_silu_f_kernel(
         nc.sync.dma_start(x_raw[:], xT.rearrange("(a p j) t -> p a j t", a=PASSES, j=4))
         w2_rows = slice(W2_ROWS_AT, W2_ROWS_AT + 16 * ROW_STEP, ROW_STEP)
         nc.sync.dma_start(s2_all[w2_rows, :].bitcast(I32), w2_scales[0].bitcast(I32))
-        nc.sync.dma_start(w1_all[0][:], words_of(w1_words, 0))
+        nc.sync.dma_start(w1_all[0][:, HEAD_COLS:COLS], words_of(w1_words, 0)[:, HEAD_COLS:COLS])
 
         x_bf = [tile([P, T, 4], BF16, f"x_bf{a}") for a in range(PASSES)]
         x_codes = [tile([P, T], U32, f"x_codes{a}") for a in range(PASSES)]

from contextlib import ExitStack

import concourse.mybir as mybir

K, T, E, G, H, N = 1024, 256, 6, 3, 512, 512
FLOPS = 2 * G * T * (K * H + H * N)
BYTES = 4 * K * T + (K * E * H + H * E * N) * 33 // 32 + 4 * G * T + 2 * 128 * (G * H + G * N) // 16 + 4 * N * T

F32 = mybir.dt.float32
BF16 = mybir.dt.bfloat16
I32 = mybir.dt.int32
U32 = mybir.dt.uint32
U16 = mybir.dt.uint16
U8 = mybir.dt.uint8
FP8X4 = mybir.dt.float8_e4m3fn_x4
SILU = mybir.ActivationFunctionType.Silu
COPY = mybir.ActivationFunctionType.Copy
MULT = mybir.AluOpType.mult
ADD = mybir.AluOpType.add
SUBTRACT = mybir.AluOpType.subtract
IS_EQUAL = mybir.AluOpType.is_equal

P = 128
PASSES = K // 512
TOKEN_TILES = T // P
OUT_TILES = N // P
COLS = E * H
LAST = G - 1
HEAD_COLS = COLS // 8
ROW_STEP = 4
W2_ROWS_AT = 32
W2_PLANE = 8
ACC_BANK = {(0, 0): 0, (0, 1): 1, (1, 0): 2, (2, 0): 3, (2, 1): 4, (1, 1): 3}
TURNED = [(2, 0), (2, 1)]
TURN_BANK = {(2, 0): 0, (2, 1): 1}
CLOSING = (1, 1)
LAST_OF_TILE = ((2, 0), CLOSING)
GATE_ROWS_AT = P - TOKEN_TILES
PER_BANK = (OUT_TILES, OUT_TILES // 2)
OUT_BANKS = ((5,), (6, 7))
POOL_GATED = (1, 0)
UPRIGHT = [(0, 0), (0, 1), CLOSING, POOL_GATED]


def tile_moe_wsel_b_silu_f_kernel(
    tc, xT, w1_words, w1_scales, w2_words, w2_scales, gate, offs, offs2, out
):
    nc = tc.nc
    with ExitStack() as ctx:
        sb = ctx.enter_context(tc.tile_pool(name="sb", bufs=1))
        late = ctx.enter_context(tc.tile_pool(name="late", bufs=1))
        ps = ctx.enter_context(tc.psum_pool(name="ps", bufs=1))

        def tile(shape, dtype, buffer):
            return sb.tile(shape, dtype, name=buffer, align_bytes=64)

        def bank(shape, number):
            return ps.tile(shape, F32, name=f"bank{number}")

        def words_of(dram, a):
            return dram[a].rearrange("p n d -> p (n d)").bitcast(I32)

        list1 = tile([P, G * H // 16], U16, "list1")
        list2 = tile([P, G * N // 16], U16, "list2")
        s1_all = tile([P, COLS], U8, "s1_all")
        s2_all = late.tile([P, COLS], U8, name="s2_all", offset=0, align_bytes=64)
        x_raw = tile([P, PASSES, 4, T], F32, "x_raw")
        w1_all = [tile([P, COLS], I32, "w1_all0")]

        gate_rows = tile([P, G, P], F32, "gate_rows")
        ident = tile([P, P], F32, "ident")
        ones = tile([P, P], F32, "ones")
        column = tile([P, P], F32, "column")
        row = tile([P, 32], F32, "row")
        quadrant = tile([P, 1], F32, "quadrant")

        nc.vector.memset(s1_all[:].bitcast(I32), 0)
        nc.vector.memset(ones[:], 1.0)
        nc.vector.tensor_tensor_scan(column[:], ones[:], ones[:], 0.0, MULT, ADD)
        for q in range(4):
            nc.gpsimd.memset(quadrant[32 * q : 32 * (q + 1), :], 32.0 * q)
        nc.gpsimd.memset(gate_rows[0:GATE_ROWS_AT, :, :], 0.0)
        nc.gpsimd.memset(s2_all[:].bitcast(I32), 0)
        nc.vector.transpose(row[:], column[:, 0:32])
        nc.vector.tensor_scalar(ident[:], column[:], row[:, 0:1], quadrant[:], SUBTRACT, IS_EQUAL)

        nc.sync.dma_start(w1_all[0][:, 0:HEAD_COLS], words_of(w1_words, 0)[:, 0:HEAD_COLS])
        nc.sync.dma_start(list1[:], offs)
        nc.sync.dma_start(list2[:], offs2)
        nc.sync.dma_start(gate_rows[GATE_ROWS_AT:P, :, :], gate[:, 0, :].rearrange("r (c t) -> c r t", t=P))
        nc.sync.dma_start(s1_all[0:P:ROW_STEP, :].bitcast(I32), w1_scales.rearrange("a b n -> b a n").bitcast(I32))
        nc.sync.dma_start(x_raw[:], xT.rearrange("(a p j) t -> p a j t", a=PASSES, j=4))
        w2_rows = slice(W2_ROWS_AT, W2_ROWS_AT + 16 * ROW_STEP, ROW_STEP)
        nc.sync.dma_start(s2_all[w2_rows, :].bitcast(I32), w2_scales[0].bitcast(I32))
        nc.sync.dma_start(w1_all[0][:, HEAD_COLS:COLS], words_of(w1_words, 0)[:, HEAD_COLS:COLS])

        x_bf = [tile([P, T, 4], BF16, f"x_bf{a}") for a in range(PASSES)]
        x_codes = [tile([P, T], U32, f"x_codes{a}") for a in range(PASSES)]
        x_scales = [tile([P, T], U8, f"x_scales{a}") for a in range(PASSES)]
        units = [(r, c) for c in range(TOKEN_TILES) for r in range(G)]
        act = {u: tile([P, P, 4], F32, f"act{u[0]}{u[1]}") for u in units if u != CLOSING}
        h_bf = {u: tile([P, P, 4], BF16, f"h_bf{u[0]}{u[1]}") for u in units if u not in (CLOSING, POOL_GATED)}
        h_bf[CLOSING] = late.tile([P, P, 4], BF16, name="h_bf_last", offset=0, align_bytes=64)
        h_codes = {u: tile([P, P], U32, f"h_codes{u[0]}{u[1]}") for u in units if u not in TURNED + [POOL_GATED]}
        for n, u in enumerate(TURNED + [POOL_GATED]):
            h_codes[u] = late.tile([P, P], U32, name=f"h_codes{u[0]}{u[1]}", offset=2 * H + 4 * P * n, align_bytes=64)
        by_token = {}
        turned = {}
        h_scales = {u: tile([P, P], U8, f"h_scales{u[0]}{u[1]}") for u in units}
        acc = {}
        w1 = {}
        w2 = {}
        y = {}

        def quantize(codes, scales, values):
            nc.vector.quantize_mx(
                out=codes[:].bitcast(FP8X4), scales=scales[:], in_=values[:].rearrange("p t j -> p (t j)")
            )

        def gather(into, window, offsets):
            nc.vector.tensor_copy(into, window.indirect(offsets))

        def gather_w1(a, r):
            w1[a, r] = tile([P, 4, P], U32, f"w1_{a}{r}")
            gather(w1[a, r][:].rearrange("p j m -> p m j"), w1_all[a][:].bitcast(U32), list1[:, 32 * r : 32 * (r + 1)])

        def gather_w2(r):
            w2[r] = tile([P, N], U32, f"w2_{r}")
            gather(w2[r][:], w2_all[:].bitcast(U32), list2[:, 32 * r : 32 * (r + 1)])

        def first_product(a, r, c):
            if a == 0:
                acc[r, c] = bank([P, 4, P], ACC_BANK[r, c])
            if (r, c) in TURNED:
                nc.tensor.matmul_mx(
                    out=acc[r, c][:].rearrange("t j m -> t (j m)"),
                    lhsT=x_codes[a][:, P * c : P * (c + 1)].bitcast(FP8X4),
                    lhsT_scale=x_scales[a][:, P * c : P * (c + 1)],
                    rhs=w1[a, r][:].rearrange("p j m -> p (j m)").bitcast(FP8X4),
                    rhs_scale=s1[a][4 * a : P, H * r : H * (r + 1)],
                    start=(a == 0),
                    stop=(a == PASSES - 1),
                )
                return
            for j in range(4):
                nc.tensor.matmul_mx(
                    out=acc[r, c][:, j, :],
                    lhsT=w1[a, r][:, j, :].bitcast(FP8X4),
                    lhsT_scale=s1[a][4 * a : P, H * r + P * j : H * r + P * (j + 1)],
                    rhs=x_codes[a][:, P * c : P * (c + 1)].bitcast(FP8X4),
                    rhs_scale=x_scales[a][:, P * c : P * (c + 1)],
                    start=(a == 0 and j == 0),
                    stop=(a == PASSES - 1 and j == 3),
                )

        def activate(r, c):
            if (r, c) in TURNED:
                values = act[r, c][:].rearrange("t a b -> t (a b)").rearrange("t (u m e) -> t u m e", u=2, e=2)
                nc.scalar.activation(values, acc[r, c][:].rearrange("t (u e) m -> t u m e", u=2), SILU)
            else:
                nc.scalar.activation(act[r, c][:], acc[r, c][:].rearrange("p j t -> p t j"), SILU)

        def weigh_by_token(r, c):
            by_token[r, c] = tile([P, H], BF16, f"by_token{c}")
            values = act[r, c][:].rearrange("t a b -> t (a b)")
            nc.scalar.activation(by_token[r, c][:], values, COPY, scale=gate_cols[:, r, c : c + 1])

        def turn(r, c):
            turned[r, c] = bank([P, 2, P], TURN_BANK[r, c])
            pairs = by_token[r, c][:].bitcast(F32)
            for u in range(2):
                nc.tensor.transpose(turned[r, c][:, u, :], pairs[:, P * u : P * (u + 1)], ident[:])

        def take_out(r, c):
            nc.scalar.copy(h_bf[r, c][:].bitcast(F32), turned[r, c][:].rearrange("p u t -> p t u"))

        def weigh(r, c):
            factor = gates[:, UPRIGHT.index((r, c)), :].unsqueeze(2).to_broadcast([P, P, 4])
            nc.vector.tensor_tensor(h_bf[r, c][:], act[r, c][:], factor, MULT)

        def second_product(r, c):
            per_bank = PER_BANK[c]
            for m in range(OUT_TILES):
                b, slot = divmod(m, per_bank)
                if r == 0 and slot == 0:
                    y[c, b] = bank([P, per_bank, P], OUT_BANKS[c][b])
                nc.tensor.matmul_mx(
                    out=y[c, b][:, slot, :],
                    lhsT=w2[r][:, P * m : P * (m + 1)].bitcast(FP8X4),
                    lhsT_scale=s2[W2_PLANE:P, N * r + P * m : N * r + P * (m + 1)],
                    rhs=h_codes[r, c][:].bitcast(FP8X4),
                    rhs_scale=h_scales[r, c][:],
                    start=(r == 0 and slot == 0),
                    stop=((r, c) == LAST_OF_TILE[c] and slot == per_bank - 1),
                )

        def store(c, b, copy):
            per_bank = PER_BANK[c]
            res = tile([P, per_bank, P], F32, f"res{c}{b}")
            copy(res[:], y[c, b][:])
            rows = out[P * per_bank * b : P * per_bank * (b + 1), P * c : P * (c + 1)]
            nc.sync.dma_start(rows.rearrange("(m p) t -> p m t", p=P), res[:])

        s1_rows = tile([P, G, P, 4], U8, "s1_rows")
        w1_all.append(tile([P, COLS], I32, "w1_all1"))
        s1 = [tile([P, G * H], U8, f"s1_{a}") for a in range(PASSES)]

        def gather_w1_scales(r):
            gather(s1_rows[:, r].rearrange("p m j -> p (m j)"), s1_all[:], list1[:, 32 * r : 32 * (r + 1)])

        def turn_w1_scales(a, r):
            columns = s1[a][:, H * r : H * (r + 1)].rearrange("p (j m) -> p j m", j=4)
            nc.vector.tensor_copy(columns, s1_rows[:, r].rearrange("p m j -> p j m"))

        gather_w1_scales(0)
        for r in range(1, G):
            gather_w1_scales(r)
            turn_w1_scales(0, r - 1)
        turn_w1_scales(0, LAST)
        s2_rows = tile([P, G * N], U8, "s1_all")
        gather(s2_rows[:], s2_all[:], list2[:])
        for r in range(G):
            turn_w1_scales(1, r)

        def move_w1_rows(a, j):
            nc.sync.dma_start(
                s1[a][4 * a + j : P : 32, :].bitcast(I32),
                s1[a][ROW_STEP * (2 * j + a) : P : 8 * ROW_STEP, :].bitcast(I32),
            )

        for j in range(1, 4):
            move_w1_rows(0, j)
        nc.sync.dma_start(w1_all[1][:], words_of(w1_words, 1))
        for j in range(1, 4):
            move_w1_rows(1, j)

        w2_all = late.tile([P, COLS], I32, name="w2_all", offset=0, align_bytes=64)
        nc.sync.dma_start(w2_all[:], words_of(w2_words, 0))
        s2 = tile([P, G * N], U8, "s2")
        for j in range(4):
            nc.sync.dma_start(
                s2[W2_PLANE + j : P : 32, :].bitcast(I32),
                s2_rows[W2_ROWS_AT + ROW_STEP * j : W2_ROWS_AT + 16 * ROW_STEP : 4 * ROW_STEP, :].bitcast(I32),
            )

        gate_ps = bank([P, G, P], 4)
        for r in range(G):
            nc.tensor.transpose(gate_ps[:, r, :], gate_rows[:, r, :], ident[:])
        gate_cols = tile([P, G, TOKEN_TILES], F32, "gate_cols")
        nc.scalar.copy(gate_cols[:], gate_ps[:, :, GATE_ROWS_AT:P])
        spread = bank([P, len(UPRIGHT), P], 5)
        for n, (r, c) in enumerate(UPRIGHT):
            nc.tensor.transpose(spread[:, n, :], gate_cols[:, r, c : c + 1].to_broadcast([P, P]), ident[:])
        gates = tile([P, len(UPRIGHT) - 1, P], F32, "gates")
        nc.scalar.copy(gates[:], spread[:, 0 : len(UPRIGHT) - 1, :])
        gates_wide = tile([P, P, 4], F32, "gates_wide")
        nc.scalar.copy(gates_wide[:], spread[:, len(UPRIGHT) - 1, :].unsqueeze(2).to_broadcast([P, P, 4]))
        for a in range(PASSES):
            nc.scalar.copy(x_bf[a][:], x_raw[:, a].rearrange("p j t -> p t j"))
            quantize(x_codes[a], x_scales[a], x_bf[a])
        for a in range(PASSES):
            for r in range(G):
                gather_w1(a, r)
                for c in range(TOKEN_TILES):
                    if (r, c) != CLOSING:
                        first_product(a, r, c)

        def pack(r, c):
            quantize(h_codes[r, c], h_scales[r, c], h_bf[r, c])

        def flat(values):
            return values[:].rearrange("p t j -> p (t j)")

        early = UPRIGHT[:TOKEN_TILES]
        for u in early + [POOL_GATED] + TURNED:
            activate(*u)
        for a in range(PASSES):
            first_product(a, *CLOSING)
        for u in early:
            weigh(*u)
        for u in early:
            pack(*u)
        h_bf[POOL_GATED] = tile([P, P, 4], BF16, "h_bf01")
        nc.gpsimd.tensor_tensor(flat(h_bf[POOL_GATED]), flat(act[POOL_GATED]), flat(gates_wide), MULT)
        for u in TURNED:
            weigh_by_token(*u)
            turn(*u)
        for r in range(G):
            gather_w2(r)
        for u in early:
            second_product(*u)
        pack(*POOL_GATED)
        second_product(*POOL_GATED)
        take_out(*TURNED[0])
        act[CLOSING] = tile([P, P, 4], F32, f"by_token{TURNED[0][1]}")
        activate(*CLOSING)
        take_out(*TURNED[1])
        pack(*TURNED[0])
        second_product(*TURNED[0])
        weigh(*CLOSING)
        for u in (TURNED[1], CLOSING):
            pack(*u)
            second_product(*u)
        store(0, 0, nc.scalar.copy)
        store(1, 0, nc.scalar.copy)
        store(1, 1, nc.vector.tensor_copy)
